import numpy as np
import ml_dtypes


def mxq(x, axis, fmt="e4m3"):
    dtype, down = {"e4m3": (ml_dtypes.float8_e4m3fn, 7), "e5m2": (ml_dtypes.float8_e5m2, 14)}[fmt]
    v = np.moveaxis(np.asarray(x, np.float32).astype(ml_dtypes.bfloat16).astype(np.float64), axis, -1)
    blocks = v.reshape(v.shape[:-1] + (-1, 32))
    amax = np.abs(blocks).max(-1, keepdims=True)
    byte = np.maximum(np.where(amax > 0, np.frexp(amax)[1] - 1 + 127, 0) - down, 1)
    scale = np.exp2(byte - 127.0)
    codes = (blocks / scale).astype(np.float32).astype(dtype).astype(np.float64)
    return np.moveaxis((codes * scale).reshape(v.shape), -1, axis)


WIDE = False


def mx_kscale(k):
    if not WIDE:
        return np.ones(k)
    levels = np.array([18, -18])
    if k % 512:
        return np.exp2(np.random.permutation(np.resize(levels, k // 32))).repeat(32)
    a = np.empty((k // 512, 16))
    for p in range(k // 512):
        a[p, :8] = np.random.permutation(np.resize(levels, 8))
        for g in range(8):
            far = levels[np.abs(levels - a[p, g]) >= 10]
            a[p, g + 8] = far[np.random.randint(len(far))]
    return np.exp2(a.ravel()).repeat(32)


def f64(x):
    return np.asarray(x).astype(np.float64)


def striped(idx):
    return np.tile(np.asarray(idx).reshape(-1, 16).T, (8, 1)).astype(np.uint16)


def unstriped(offs):
    return offs[:16].T.reshape(-1).astype(np.int64)

def planes(y):
    n, m = y.shape
    v = y.astype(np.float32).astype(ml_dtypes.bfloat16).astype(np.float64).reshape(n // 32, 32, m)
    top = np.abs(v).max(1)
    byte = np.clip(np.where(top > 0, np.frexp(top)[1] - 1 + 127 - 7, 1), 1, 254)
    codes = (v * np.exp2(127.0 - byte)[:, None, :]).reshape(n, m).astype(np.float32).astype(ml_dtypes.float8_e4m3fn).view(np.uint8)
    words = codes.reshape(n // 512, 128, 4, m).transpose(0, 1, 3, 2)
    return np.ascontiguousarray(words), np.ascontiguousarray(byte.astype(np.uint8).reshape(n // 512, 16, m))


def setup_inputs():
    n = np.random.standard_normal
    uni = np.random.uniform
    idx = np.random.permutation(2048)[:512]
    f_d = mx_kscale(512)
    f_r = mx_kscale(512)
    return {
        "kT": (n((512, 2048)) * f_d[:, None]).astype(np.float32),
        "cd": (uni(0.75, 1.3, (512, 1))).astype(np.float32),
        "ce": np.tile(uni(0.75, 1.3, 512), (128, 1)).astype(np.float32),
        "do": (n((512, 512)) * f_r[:, None]).astype(np.float32),
        "qT": (n((512, 512)) / np.sqrt(512) / f_d[:, None] / f_r[None, :]).astype(np.float32),
        "ts": np.tile(uni(0.75, 1.3, 2048), (128, 1)).astype(np.float32),
        "offs": striped(idx),
    }


def reference(kT, cd, ce, do, qT, ts, offs):
    idx = unstriped(offs)
    kT_i = f64(kT)[:, idx]
    S = mxq(f64(qT), 1, "e4m3") @ mxq(f64(do), 0, "e5m2")
    s = f64(cd) * f64(ce)[:1] * S
    ts_i = f64(ts)[:1][:, idx]
    dv0 = mxq(s, 0, "e5m2").T @ mxq(kT_i, 0, "e4m3")
    dv = ts_i * dv0
    out_0 = np.zeros((512, 2048))
    out_0[:, idx] = dv
    return (out_0,) + planes(out_0)

@@ -1,0 +1,206 @@
+from contextlib import ExitStack
+
+import concourse.mybir as mybir
+from concourse.masks import make_identity
+
+F32 = mybir.dt.float32
+BF16 = mybir.dt.bfloat16
+I32 = mybir.dt.int32
+U32 = mybir.dt.uint32
+U16 = mybir.dt.uint16
+U8 = mybir.dt.uint8
+E4M3 = mybir.dt.float8_e4m3fn_x4
+E5M2 = mybir.dt.float8_e5m2_x4
+MULT = mybir.AluOpType.mult
+
+P = 128
+LANES = 4
+D = 512
+T = 2048
+SLOTS = 512
+CHUNK = 256
+VECTOR_CHUNKS = 4
+STORE_CHUNKS = 2
+WINDOWS = 3
+DO_SCALAR_COLS = 192
+TIE = 16
+
+FLOPS = 2 * 2 * 512 * 512 * 512
+BYTES = 4 * (512 * 2048 + 512 + 512 + 2 * 512 * 512 + 2048) + 2 * 128 * 32 + 4 * 512 * 2048 + 512 * 2048 + 16 * 2048
+
+
+def tile_attend_glin_v_pl_kernel(tc, kT, cd, ce, do, qT, ts, offs, out_0, out_1, out_2):
+    nc = tc.nc
+    with ExitStack() as ctx:
+        sb = ctx.enter_context(tc.tile_pool(name="sb", bufs=1))
+        ps = ctx.enter_context(tc.psum_pool(name="ps", bufs=1))
+
+        q_rows = qT.rearrange("(m j) r -> m j r", j=LANES)
+        q_raw = [sb.tile([P, 2, D], F32, name="q_raw%d" % h) for h in range(2)]
+        for h in range(2):
+            nc.sync.dma_start(out=q_raw[h][:], in_=q_rows[:, 2 * h : 2 * h + 2, :])
+        offsets = sb.tile([P, SLOTS // 16], U16, name="offsets")
+        nc.sync.dma_start(offsets[:], offs)
+        do_raw = sb.tile([P, LANES, D], F32, name="do_raw")
+        nc.sync.dma_start(out=do_raw[:], in_=do.rearrange("(p t) e -> p t e", t=LANES))
+        cd_col = sb.tile([P, LANES], F32, name="cd_col")
+        nc.scalar.dma_start(out=cd_col[:], in_=cd.rearrange("(p j) o -> p (j o)", j=LANES))
+        ce_col = sb.tile([P, LANES], F32, name="ce_col")
+        nc.scalar.dma_start(out=ce_col[:], in_=ce[0:1, :].rearrange("o (m g) -> m (o g)", g=LANES))
+        k_rows = kT.rearrange("(p t) c -> p t c", t=LANES)
+        k_raw = [sb.tile([P, T], F32, name="k_raw%d" % t) for t in range(LANES)]
+        for t in range(LANES):
+            nc.sync.dma_start(out=k_raw[t][:], in_=k_rows[:, t, :])
+        ts_raw = sb.tile([P, T], F32, name="ts_raw")
+        nc.sync.dma_start(out=ts_raw[:], in_=ts)
+
+        ident = sb.tile([P, P], F32, name="ident")
+        make_identity(nc, ident[:])
+        zeroed = [sb.tile([P, T], F32, name="window%d" % w) for w in range(WINDOWS)]
+        for w in range(WINDOWS):
+            nc.vector.memset(zeroed[w][:], 0.0)
+        window = [zeroed[g % WINDOWS] for g in range(LANES)]
+
+        q_pairs = sb.tile([P, LANES, 2, P, 2], BF16, name="q_pairs")
+        q_il = sb.tile([P, D, LANES], BF16, name="q_il", align_bytes=64)
+        q_codes = sb.tile([P, D], U32, name="q_codes", align_bytes=64)
+        q_scales = sb.tile([P, D], U8, name="q_scales", align_bytes=64)
+        for h in range(2):
+            round_q = nc.scalar.copy if h == 0 else nc.vector.tensor_copy
+            round_q(
+                out=q_pairs[:, 2 * h : 2 * h + 2, :, :, :],
+                in_=q_raw[h][:].rearrange("m j (p u b) -> m j u p b", u=2, b=2),
+            )
+            words = q_pairs[:].rearrange("m j u p b -> m (j u p b)").bitcast(F32)
+            bank = ps.tile([P, 2, 2, P], F32, name="q_bank%d" % h, tag="bank%d" % h)
+            for jj in range(2):
+                for u in range(2):
+                    w0 = ((2 * h + jj) * 2 + u) * P
+                    nc.tensor.transpose(bank[:, jj, u, :], words[:, w0 : w0 + P], ident[:])
+            il_words = q_il[:].rearrange("p c t -> p (c t)").bitcast(F32)
+            nc.scalar.copy(
+                out=il_words[:, 512 * h : 512 * (h + 1)].rearrange("p (j m u) -> p j m u", j=2, u=2),
+                in_=bank[:].rearrange("p j u m -> p j m u"),
+            )
+        nc.vector.quantize_mx(out=q_codes[:].bitcast(E4M3), scales=q_scales[:], in_=q_il[:].rearrange("p c t -> p (c t)"))
+
+        ce_bank = ps.tile([P, LANES, P], F32, name="ce_bank", tag="bank2")
+        for g in range(LANES):
+            nc.tensor.transpose(ce_bank[:, g, :], ce_col[:, g : g + 1].to_broadcast([P, P]), ident[:])
+        ce_all = sb.tile([P, LANES, P], F32, name="ce_all")
+        nc.scalar.copy(out=ce_all[:], in_=ce_bank[:])
+
+        do_il = sb.tile([P, D, LANES], BF16, name="do_il", align_bytes=64)
+        do_codes = sb.tile([P, D], U32, name="do_codes", align_bytes=64)
+        do_scales = sb.tile([P, D], U8, name="do_scales", align_bytes=64)
+        for weave, c in ((nc.scalar.copy, slice(0, DO_SCALAR_COLS)), (nc.vector.tensor_copy, slice(DO_SCALAR_COLS, D))):
+            weave(
+                out=do_il[:, c, :].rearrange("p (c i) t -> p c t i", i=4),
+                in_=do_raw[:, :, c].rearrange("p t (c i) -> p c t i", i=4),
+            )
+        nc.vector.quantize_mx(out=do_codes[:].bitcast(E5M2), scales=do_scales[:], in_=do_il[:].rearrange("p c t -> p (c t)"))
+
+        s_rows = sb.tile([P, LANES, D], BF16, name="s_rows")
+        for j in range(LANES):
+            s_bank = ps.tile([P, D], F32, name="s_bank%d" % j, tag="bank%d" % (4 + j))
+            nc.tensor.matmul_mx(
+                out=s_bank[:],
+                lhsT=q_codes[:, P * j : P * (j + 1)].bitcast(E4M3),
+                lhsT_scale=q_scales[:, P * j : P * (j + 1)],
+                rhs=do_codes[:].bitcast(E5M2),
+                rhs_scale=do_scales[:],
+                start=True,
+                stop=True,
+            )
+            nc.vector.scalar_tensor_tensor(
+                out=s_rows[:, j, :].rearrange("p (g m) -> p g m", g=LANES),
+                in0=s_bank[:].rearrange("p (m g) -> p g m", g=LANES),
+                scalar=cd_col[:, j : j + 1],
+                in1=ce_all[:],
+                op0=MULT,
+                op1=MULT,
+            )
+        s_il = sb.tile([P, D, LANES], BF16, name="s_il", align_bytes=64)
+        s_codes = sb.tile([P, D], U32, name="s_codes", align_bytes=64)
+        s_scales = sb.tile([P, D], U8, name="s_scales", align_bytes=64)
+        nc.scalar.copy(
+            out=s_il[:].rearrange("p (c i) t -> p c t i", i=4),
+            in_=s_rows[:].rearrange("p t (c i) -> p c t i", i=4),
+        )
+        nc.vector.quantize_mx(out=s_codes[:].bitcast(E5M2), scales=s_scales[:], in_=s_il[:].rearrange("p c t -> p (c t)"))
+
+        k_il = sb.tile([P, SLOTS, LANES], BF16, name="k_il", align_bytes=64)
+        k_codes = sb.tile([P, SLOTS], U32, name="k_codes", align_bytes=64)
+        k_scales = sb.tile([P, SLOTS], U8, name="k_scales", align_bytes=64)
+        k_early = sb.tile([P, 2, SLOTS], BF16, name="k_early")
+        for t in range(2):
+            nc.vector.tensor_copy(out=k_early[:, t, :], in_=k_raw[t][:].indirect(offsets[:]))
+        nc.scalar.copy(out=k_il[:, :, 0:2], in_=k_early[:].rearrange("p t c -> p c t"))
+        for t in range(2, LANES):
+            nc.vector.tensor_copy(out=k_il[:, :, t], in_=k_raw[t][:].indirect(offsets[:]))
+        nc.vector.quantize_mx(out=k_codes[:].bitcast(E4M3), scales=k_scales[:], in_=k_il[:].rearrange("p c t -> p (c t)"))
+        ts_listed = sb.tile([P, SLOTS], F32, name="ts_listed")
+        nc.vector.tensor_copy(out=ts_listed[:], in_=ts_raw[:].indirect(offsets[:]))
+
+        out_rows = out_0.rearrange("(p g) c -> p g c", g=LANES)
+        y_pairs = sb.tile([P, 2, T, 2], BF16, name="y_pairs")
+        n_chunks = T // CHUNK
+        for g in range(LANES):
+            dv_bank = ps.tile([P, SLOTS], F32, name="dv_bank%d" % g, tag="bank%d" % g)
+            nc.tensor.matmul_mx(
+                out=dv_bank[:],
+                lhsT=s_codes[:, P * g : P * (g + 1)].bitcast(E5M2),
+                lhsT_scale=s_scales[:, P * g : P * (g + 1)],
+                rhs=k_codes[:].bitcast(E4M3),
+                rhs_scale=k_scales[:],
+                start=True,
+                stop=True,
+            )
+            dv0 = sb.tile([P, SLOTS], F32, name="dv0_%d" % g)
+            nc.scalar.copy(out=dv0[:], in_=dv_bank[:])
+            nc.vector.tensor_tensor(window[g][:].indirect(offsets[:]), dv0[:], ts_listed[:], MULT)
+            nc.sync.dma_start(out=out_rows[:, g, :], in_=window[g][:])
+            if g < 2:
+                nc.scalar.copy(out=y_pairs[:, 0, :, g], in_=window[g][:])
+            if g == 2:
+                split = VECTOR_CHUNKS * CHUNK
+                nc.scalar.copy(out=y_pairs[:, 1, TIE:split, 0], in_=window[g][:, TIE:split])
+                nc.scalar.copy(out=y_pairs[:, 1, 0:TIE, :], in_=window[g][:, 0:TIE].unsqueeze(2).to_broadcast([P, TIE, 2]))
+                nc.scalar.copy(out=y_pairs[:, 1, split:T, 0], in_=window[g][:, split:T])
+
+        y_words = y_pairs[:].rearrange("p u c b -> p (u c b)").bitcast(F32).rearrange("p (u c) -> p c u", u=2)
+        y_il = sb.tile([P, T * LANES], BF16, name="y_il", align_bytes=64)
+        y_codes = sb.tile([P, T], U32, name="y_codes", align_bytes=64)
+        y_scales = sb.tile([P, T], U8, name="y_scales", align_bytes=64)
+        il_words = y_il[:].bitcast(F32).rearrange("p (c u) -> p c u", u=2)
+        words_out = out_1.rearrange("a p c l -> p (a c l)").bitcast(I32)
+
+        def cols(n):
+            return slice(n * CHUNK, (n + 1) * CHUNK)
+
+        def quantise(n):
+            nc.vector.quantize_mx(
+                out=y_codes[:, cols(n)].bitcast(E4M3),
+                scales=y_scales[:, cols(n)],
+                in_=y_il[:, n * CHUNK * LANES : (n + 1) * CHUNK * LANES],
+            )
+
+        for n in range(VECTOR_CHUNKS, n_chunks):
+            nc.scalar.copy(out=y_pairs[:, 1, cols(n), 1], in_=window[3][:, cols(n)])
+            nc.scalar.copy(out=il_words[:, cols(n), :], in_=y_words[:, cols(n), :])
+        wide = slice(0, VECTOR_CHUNKS * CHUNK)
+        nc.vector.tensor_copy(out=y_pairs[:, 1, wide, 1], in_=window[3][:, wide])
+        for n in range(VECTOR_CHUNKS):
+            nc.vector.tensor_copy(out=il_words[:, cols(n), :], in_=y_words[:, cols(n), :])
+        for n in range(n_chunks):
+            quantise(n)
+            if n % STORE_CHUNKS == STORE_CHUNKS - 1:
+                c = slice((n + 1 - STORE_CHUNKS) * CHUNK, (n + 1) * CHUNK)
+                nc.sync.dma_start(out=words_out[:, c], in_=y_codes[:, c].bitcast(I32))
+        scales_out = out_2.rearrange("a f c -> (a f) c").bitcast(I32)
+        for quad in range(4):
+            queue = nc.sync if quad % 2 == 0 else nc.scalar
+            queue.dma_start(
+                out=scales_out[4 * quad : 4 * quad + 4, :],
+                in_=y_scales[32 * quad : 32 * quad + 4, :].bitcast(I32),
+            )

@@ -18,11 +18,10 @@ LANES = 4
 D = 512
 T = 2048
 SLOTS = 512
-CHUNK = 256
-VECTOR_CHUNKS = 4
-STORE_CHUNKS = 2
+SPLIT = 896
+PIECES = (0, 512, 1024, 1280, 1536, 1792, 2048)
+STORES = (0, 512, 1024, 1792, 2048)
 WINDOWS = 3
-DO_SCALAR_COLS = 192
 TIE = 16
 
 FLOPS = 2 * 2 * 512 * 512 * 512
@@ -39,10 +38,12 @@ def tile_attend_glin_v_pl_kernel(tc, kT, cd, ce, do, qT, ts, offs, out_0, out_1,
         q_raw = [sb.tile([P, 2, D], F32, name="q_raw%d" % h) for h in range(2)]
         for h in range(2):
             nc.sync.dma_start(out=q_raw[h][:], in_=q_rows[:, 2 * h : 2 * h + 2, :])
+        do_rows = do.rearrange("(p t) e -> p t e", t=LANES)
+        do_raw = [sb.tile([P, LANES, D // 2], F32, name="do_raw%d" % h) for h in range(2)]
+        for h in range(2):
+            nc.sync.dma_start(out=do_raw[h][:], in_=do_rows[:, :, h * D // 2 : (h + 1) * D // 2])
         offsets = sb.tile([P, SLOTS // 16], U16, name="offsets")
         nc.sync.dma_start(offsets[:], offs)
-        do_raw = sb.tile([P, LANES, D], F32, name="do_raw")
-        nc.sync.dma_start(out=do_raw[:], in_=do.rearrange("(p t) e -> p t e", t=LANES))
         cd_col = sb.tile([P, LANES], F32, name="cd_col")
         nc.scalar.dma_start(out=cd_col[:], in_=cd.rearrange("(p j) o -> p (j o)", j=LANES))
         ce_col = sb.tile([P, LANES], F32, name="ce_col")
@@ -56,10 +57,9 @@ def tile_attend_glin_v_pl_kernel(tc, kT, cd, ce, do, qT, ts, offs, out_0, out_1,
 
         ident = sb.tile([P, P], F32, name="ident")
         make_identity(nc, ident[:])
-        zeroed = [sb.tile([P, T], F32, name="window%d" % w) for w in range(WINDOWS)]
-        for w in range(WINDOWS):
-            nc.vector.memset(zeroed[w][:], 0.0)
-        window = [zeroed[g % WINDOWS] for g in range(LANES)]
+        zeroed = [sb.tile([P, T], F32, name="window%d" % w) for w in range(WINDOWS - 1)]
+        for tile in zeroed:
+            nc.vector.memset(tile[:].bitcast(I32), 0)
 
         q_pairs = sb.tile([P, LANES, 2, P, 2], BF16, name="q_pairs")
         q_il = sb.tile([P, D, LANES], BF16, name="q_il", align_bytes=64)
@@ -82,23 +82,38 @@ def tile_attend_glin_v_pl_kernel(tc, kT, cd, ce, do, qT, ts, offs, out_0, out_1,
                 out=il_words[:, 512 * h : 512 * (h + 1)].rearrange("p (j m u) -> p j m u", j=2, u=2),
                 in_=bank[:].rearrange("p j u m -> p j m u"),
             )
-        nc.vector.quantize_mx(out=q_codes[:].bitcast(E4M3), scales=q_scales[:], in_=q_il[:].rearrange("p c t -> p (c t)"))
+            half = slice(2 * P * h, 2 * P * (h + 1))
+            nc.vector.quantize_mx(
+                out=q_codes[:, half].bitcast(E4M3),
+                scales=q_scales[:, half],
+                in_=q_il[:, half, :].rearrange("p c t -> p (c t)"),
+            )
 
         ce_bank = ps.tile([P, LANES, P], F32, name="ce_bank", tag="bank2")
         for g in range(LANES):
             nc.tensor.transpose(ce_bank[:, g, :], ce_col[:, g : g + 1].to_broadcast([P, P]), ident[:])
-        ce_all = sb.tile([P, LANES, P], F32, name="ce_all")
-        nc.scalar.copy(out=ce_all[:], in_=ce_bank[:])
+        ce_all = sb.tile([P, D], F32, name="ce_all", tag="ce_then_keys")
+        nc.scalar.copy(out=ce_all[:].rearrange("p (m g) -> p m g", g=LANES), in_=ce_bank[:].rearrange("p g m -> p m g"))
 
-        do_il = sb.tile([P, D, LANES], BF16, name="do_il", align_bytes=64)
+        do_il = sb.tile([P, D, LANES], BF16, name="do_il", tag="do_then_window", align_bytes=64)
         do_codes = sb.tile([P, D], U32, name="do_codes", align_bytes=64)
         do_scales = sb.tile([P, D], U8, name="do_scales", align_bytes=64)
-        for weave, c in ((nc.scalar.copy, slice(0, DO_SCALAR_COLS)), (nc.vector.tensor_copy, slice(DO_SCALAR_COLS, D))):
-            weave(
-                out=do_il[:, c, :].rearrange("p (c i) t -> p c t i", i=4),
-                in_=do_raw[:, :, c].rearrange("p t (c i) -> p c t i", i=4),
+        for h in range(2):
+            half = slice(h * D // 2, (h + 1) * D // 2)
+            nc.vector.tensor_copy(
+                out=do_il[:, half, :].rearrange("p (c i) t -> p c t i", i=4),
+                in_=do_raw[h][:].rearrange("p t (c i) -> p c t i", i=4),
             )
-        nc.vector.quantize_mx(out=do_codes[:].bitcast(E5M2), scales=do_scales[:], in_=do_il[:].rearrange("p c t -> p (c t)"))
+            nc.vector.quantize_mx(
+                out=do_codes[:, half].bitcast(E5M2),
+                scales=do_scales[:, half],
+                in_=do_il[:, half, :].rearrange("p c t -> p (c t)"),
+            )
+
+        last_window = sb.tile([P, T], F32, name="window2", tag="do_then_window", align_bytes=64)
+        nc.gpsimd.memset(last_window[:].bitcast(I32), 0)
+        zeroed.append(last_window)
+        window = [zeroed[g % WINDOWS] for g in range(LANES)]
 
         s_rows = sb.tile([P, LANES, D], BF16, name="s_rows")
         for j in range(LANES):
@@ -113,8 +128,8 @@ def tile_attend_glin_v_pl_kernel(tc, kT, cd, ce, do, qT, ts, offs, out_0, out_1,
                 stop=True,
             )
             nc.vector.scalar_tensor_tensor(
-                out=s_rows[:, j, :].rearrange("p (g m) -> p g m", g=LANES),
-                in0=s_bank[:].rearrange("p (m g) -> p g m", g=LANES),
+                out=s_rows[:, j, :],
+                in0=s_bank[:],
                 scalar=cd_col[:, j : j + 1],
                 in1=ce_all[:],
                 op0=MULT,
@@ -124,27 +139,33 @@ def tile_attend_glin_v_pl_kernel(tc, kT, cd, ce, do, qT, ts, offs, out_0, out_1,
         s_codes = sb.tile([P, D], U32, name="s_codes", align_bytes=64)
         s_scales = sb.tile([P, D], U8, name="s_scales", align_bytes=64)
         nc.scalar.copy(
-            out=s_il[:].rearrange("p (c i) t -> p c t i", i=4),
-            in_=s_rows[:].rearrange("p t (c i) -> p c t i", i=4),
+            out=s_il[:].rearrange("p (g m) j -> p m g j", g=LANES),
+            in_=s_rows[:].rearrange("p j (m g) -> p m g j", g=LANES),
         )
         nc.vector.quantize_mx(out=s_codes[:].bitcast(E5M2), scales=s_scales[:], in_=s_il[:].rearrange("p c t -> p (c t)"))
 
-        k_il = sb.tile([P, SLOTS, LANES], BF16, name="k_il", align_bytes=64)
+        k_il = sb.tile([P, SLOTS, LANES], BF16, name="k_il", tag="keys_then_ts", align_bytes=64)
         k_codes = sb.tile([P, SLOTS], U32, name="k_codes", align_bytes=64)
         k_scales = sb.tile([P, SLOTS], U8, name="k_scales", align_bytes=64)
-        k_early = sb.tile([P, 2, SLOTS], BF16, name="k_early")
-        for t in range(2):
-            nc.vector.tensor_copy(out=k_early[:, t, :], in_=k_raw[t][:].indirect(offsets[:]))
-        nc.scalar.copy(out=k_il[:, :, 0:2], in_=k_early[:].rearrange("p t c -> p c t"))
-        for t in range(2, LANES):
-            nc.vector.tensor_copy(out=k_il[:, :, t], in_=k_raw[t][:].indirect(offsets[:]))
+        k_listed = sb.tile([P, LANES, SLOTS], BF16, name="k_listed", tag="ce_then_keys")
+        for t in range(LANES - 1):
+            nc.vector.tensor_copy(out=k_listed[:, t, :], in_=k_raw[t][:].indirect(offsets[:]))
+        halves = [slice(h * SLOTS // 2, (h + 1) * SLOTS // 2) for h in range(2)]
+        for h in range(2):
+            half_list = offsets[:, h * SLOTS // 32 : (h + 1) * SLOTS // 32]
+            nc.vector.tensor_copy(out=k_listed[:, LANES - 1, halves[h]], in_=k_raw[LANES - 1][:].indirect(half_list))
+        for weave, half in zip((nc.scalar.copy, nc.vector.tensor_copy), halves):
+            weave(
+                out=k_il[:, half, :].rearrange("p (c i) t -> p c t i", i=4),
+                in_=k_listed[:, :, half].rearrange("p t (c i) -> p c t i", i=4),
+            )
         nc.vector.quantize_mx(out=k_codes[:].bitcast(E4M3), scales=k_scales[:], in_=k_il[:].rearrange("p c t -> p (c t)"))
-        ts_listed = sb.tile([P, SLOTS], F32, name="ts_listed")
+        ts_listed = sb.tile([P, SLOTS], F32, name="ts_listed", tag="keys_then_ts", align_bytes=64)
         nc.vector.tensor_copy(out=ts_listed[:], in_=ts_raw[:].indirect(offsets[:]))
 
         out_rows = out_0.rearrange("(p g) c -> p g c", g=LANES)
         y_pairs = sb.tile([P, 2, T, 2], BF16, name="y_pairs")
-        n_chunks = T // CHUNK
+        dv0 = [sb.tile([P, SLOTS], F32, name="dv0_%d" % g) for g in range(LANES)]
         for g in range(LANES):
             dv_bank = ps.tile([P, SLOTS], F32, name="dv_bank%d" % g, tag="bank%d" % g)
             nc.tensor.matmul_mx(
@@ -156,17 +177,17 @@ def tile_attend_glin_v_pl_kernel(tc, kT, cd, ce, do, qT, ts, offs, out_0, out_1,
                 start=True,
                 stop=True,
             )
-            dv0 = sb.tile([P, SLOTS], F32, name="dv0_%d" % g)
-            nc.scalar.copy(out=dv0[:], in_=dv_bank[:])
-            nc.vector.tensor_tensor(window[g][:].indirect(offsets[:]), dv0[:], ts_listed[:], MULT)
+            nc.scalar.copy(out=dv0[g][:], in_=dv_bank[:])
+        for g in range(LANES):
+            nc.vector.tensor_tensor(window[g][:].indirect(offsets[:]), dv0[g][:], ts_listed[:], MULT)
             nc.sync.dma_start(out=out_rows[:, g, :], in_=window[g][:])
             if g < 2:
                 nc.scalar.copy(out=y_pairs[:, 0, :, g], in_=window[g][:])
             if g == 2:
-                split = VECTOR_CHUNKS * CHUNK
-                nc.scalar.copy(out=y_pairs[:, 1, TIE:split, 0], in_=window[g][:, TIE:split])
-                nc.scalar.copy(out=y_pairs[:, 1, 0:TIE, :], in_=window[g][:, 0:TIE].unsqueeze(2).to_broadcast([P, TIE, 2]))
-                nc.scalar.copy(out=y_pairs[:, 1, split:T, 0], in_=window[g][:, split:T])
+                tie = slice(PIECES[1] - TIE // 2, PIECES[1] + TIE // 2)
+                nc.scalar.copy(out=y_pairs[:, 1, 0:SPLIT, 0], in_=window[g][:, 0:SPLIT])
+                nc.scalar.copy(out=y_pairs[:, 1, tie, :], in_=window[g][:, tie].unsqueeze(2).to_broadcast([P, TIE, 2]))
+                nc.scalar.copy(out=y_pairs[:, 1, SPLIT:T, 0], in_=window[g][:, SPLIT:T])
 
         y_words = y_pairs[:].rearrange("p u c b -> p (u c b)").bitcast(F32).rearrange("p (u c) -> p c u", u=2)
         y_il = sb.tile([P, T * LANES], BF16, name="y_il", align_bytes=64)
@@ -175,27 +196,26 @@ def tile_attend_glin_v_pl_kernel(tc, kT, cd, ce, do, qT, ts, offs, out_0, out_1,
         il_words = y_il[:].bitcast(F32).rearrange("p (c u) -> p c u", u=2)
         words_out = out_1.rearrange("a p c l -> p (a c l)").bitcast(I32)
 
-        def cols(n):
-            return slice(n * CHUNK, (n + 1) * CHUNK)
+        def round_and_weave(copy, c):
+            copy(out=y_pairs[:, 1, c, 1], in_=window[3][:, c])
+            copy(out=il_words[:, c, :], in_=y_words[:, c, :])
 
-        def quantise(n):
+        scalar_cuts = (SPLIT,) + PIECES[3:]
+        for a, b in zip(scalar_cuts, scalar_cuts[1:]):
+            round_and_weave(nc.scalar.copy, slice(a, b))
+        vector_parts = (slice(0, PIECES[1]), slice(PIECES[1], SPLIT))
+        for c in vector_parts:
+            nc.vector.tensor_copy(out=y_pairs[:, 1, c, 1], in_=window[3][:, c])
+        for c in vector_parts:
+            nc.vector.tensor_copy(out=il_words[:, c, :], in_=y_words[:, c, :])
+        for a, b in zip(PIECES, PIECES[1:]):
             nc.vector.quantize_mx(
-                out=y_codes[:, cols(n)].bitcast(E4M3),
-                scales=y_scales[:, cols(n)],
-                in_=y_il[:, n * CHUNK * LANES : (n + 1) * CHUNK * LANES],
+                out=y_codes[:, a:b].bitcast(E4M3),
+                scales=y_scales[:, a:b],
+                in_=y_il[:, a * LANES : b * LANES],
             )
-
-        for n in range(VECTOR_CHUNKS, n_chunks):
-            nc.scalar.copy(out=y_pairs[:, 1, cols(n), 1], in_=window[3][:, cols(n)])
-            nc.scalar.copy(out=il_words[:, cols(n), :], in_=y_words[:, cols(n), :])
-        wide = slice(0, VECTOR_CHUNKS * CHUNK)
-        nc.vector.tensor_copy(out=y_pairs[:, 1, wide, 1], in_=window[3][:, wide])
-        for n in range(VECTOR_CHUNKS):
-            nc.vector.tensor_copy(out=il_words[:, cols(n), :], in_=y_words[:, cols(n), :])
-        for n in range(n_chunks):
-            quantise(n)
-            if n % STORE_CHUNKS == STORE_CHUNKS - 1:
-                c = slice((n + 1 - STORE_CHUNKS) * CHUNK, (n + 1) * CHUNK)
+            if b in STORES:
+                c = slice(STORES[STORES.index(b) - 1], b)
                 nc.sync.dma_start(out=words_out[:, c], in_=y_codes[:, c].bitcast(I32))
         scales_out = out_2.rearrange("a f c -> (a f) c").bitcast(I32)
         for quad in range(4):

@@ -34,39 +34,50 @@ def tile_attend_glin_v_pl_kernel(tc, kT, cd, ce, do, qT, ts, offs, out_0, out_1,
         sb = ctx.enter_context(tc.tile_pool(name="sb", bufs=1))
         ps = ctx.enter_context(tc.psum_pool(name="ps", bufs=1))
 
+        cd_col = sb.tile([P, LANES], F32, name="cd_col")
+        ce_col = sb.tile([P, LANES], F32, name="ce_col")
+        nc.scalar.dma_start(out=ce_col[:], in_=ce[0:1, :].rearrange("o (m g) -> m (o g)", g=LANES))
+        nc.scalar.dma_start(out=cd_col[:], in_=cd.rearrange("(p j) o -> p (j o)", j=LANES))
         q_rows = qT.rearrange("(m j) r -> m j r", j=LANES)
         q_raw = [sb.tile([P, 2, D], F32, name="q_raw%d" % h) for h in range(2)]
-        for h in range(2):
-            nc.sync.dma_start(out=q_raw[h][:], in_=q_rows[:, 2 * h : 2 * h + 2, :])
         do_rows = do.rearrange("(p t) e -> p t e", t=LANES)
         do_raw = [sb.tile([P, LANES, D // 2], F32, name="do_raw%d" % h) for h in range(2)]
         for h in range(2):
+            nc.sync.dma_start(out=q_raw[h][:], in_=q_rows[:, 2 * h : 2 * h + 2, :])
             nc.sync.dma_start(out=do_raw[h][:], in_=do_rows[:, :, h * D // 2 : (h + 1) * D // 2])
         offsets = sb.tile([P, SLOTS // 16], U16, name="offsets")
         nc.sync.dma_start(offsets[:], offs)
-        cd_col = sb.tile([P, LANES], F32, name="cd_col")
-        nc.scalar.dma_start(out=cd_col[:], in_=cd.rearrange("(p j) o -> p (j o)", j=LANES))
-        ce_col = sb.tile([P, LANES], F32, name="ce_col")
-        nc.scalar.dma_start(out=ce_col[:], in_=ce[0:1, :].rearrange("o (m g) -> m (o g)", g=LANES))
         k_rows = kT.rearrange("(p t) c -> p t c", t=LANES)
         k_raw = [sb.tile([P, T], F32, name="k_raw%d" % t) for t in range(LANES)]
         for t in range(LANES):
             nc.sync.dma_start(out=k_raw[t][:], in_=k_rows[:, t, :])
-        ts_raw = sb.tile([P, T], F32, name="ts_raw")
+        ts_raw = sb.tile([P, T], F32, name="ts_raw", tag="ts_then_window")
         nc.sync.dma_start(out=ts_raw[:], in_=ts)
 
         ident = sb.tile([P, P], F32, name="ident")
         make_identity(nc, ident[:])
-        zeroed = [sb.tile([P, T], F32, name="window%d" % w) for w in range(WINDOWS - 1)]
-        for tile in zeroed:
-            nc.vector.memset(tile[:].bitcast(I32), 0)
+        zeroed = [sb.tile([P, T], F32, name="window0")]
+        nc.vector.memset(zeroed[0][:].bitcast(I32), 0)
+
+        ce_bank = ps.tile([P, LANES, P], F32, name="ce_bank", tag="bank2")
+        for g in range(LANES):
+            nc.tensor.transpose(ce_bank[:, g, :], ce_col[:, g : g + 1].to_broadcast([P, P]), ident[:])
+        ce_all = sb.tile([P, D], F32, name="ce_all", tag="ce_then_keys")
+        nc.scalar.copy(out=ce_all[:], in_=ce_bank[:].rearrange("p g m -> p (g m)"))
 
         q_pairs = sb.tile([P, LANES, 2, P, 2], BF16, name="q_pairs")
-        q_il = sb.tile([P, D, LANES], BF16, name="q_il", align_bytes=64)
+        q_il = [
+            sb.tile([P, D * 2], BF16, name="q_il0", align_bytes=64),
+            sb.tile([P, D * 2], BF16, name="q_il1", tag="q_then_rows", align_bytes=64),
+        ]
         q_codes = sb.tile([P, D], U32, name="q_codes", align_bytes=64)
         q_scales = sb.tile([P, D], U8, name="q_scales", align_bytes=64)
-        for h in range(2):
-            round_q = nc.scalar.copy if h == 0 else nc.vector.tensor_copy
+        do_il = sb.tile([P, D, LANES], BF16, name="do_il", align_bytes=64)
+        do_codes = sb.tile([P, D], U32, name="do_codes", align_bytes=64)
+        do_scales = sb.tile([P, D], U8, name="do_scales", align_bytes=64)
+        halves = [slice(h * D // 2, (h + 1) * D // 2) for h in range(2)]
+
+        def turn_q(h, round_q):
             round_q(
                 out=q_pairs[:, 2 * h : 2 * h + 2, :, :, :],
                 in_=q_raw[h][:].rearrange("m j (p u b) -> m j u p b", u=2, b=2),
@@ -77,45 +88,48 @@ def tile_attend_glin_v_pl_kernel(tc, kT, cd, ce, do, qT, ts, offs, out_0, out_1,
                 for u in range(2):
                     w0 = ((2 * h + jj) * 2 + u) * P
                     nc.tensor.transpose(bank[:, jj, u, :], words[:, w0 : w0 + P], ident[:])
-            il_words = q_il[:].rearrange("p c t -> p (c t)").bitcast(F32)
             nc.scalar.copy(
-                out=il_words[:, 512 * h : 512 * (h + 1)].rearrange("p (j m u) -> p j m u", j=2, u=2),
+                out=q_il[h][:].bitcast(F32).rearrange("p (j m u) -> p j m u", j=2, u=2),
                 in_=bank[:].rearrange("p j u m -> p j m u"),
             )
-            half = slice(2 * P * h, 2 * P * (h + 1))
+
+        def quantise_q(h):
             nc.vector.quantize_mx(
-                out=q_codes[:, half].bitcast(E4M3),
-                scales=q_scales[:, half],
-                in_=q_il[:, half, :].rearrange("p c t -> p (c t)"),
+                out=q_codes[:, halves[h]].bitcast(E4M3),
+                scales=q_scales[:, halves[h]],
+                in_=q_il[h][:],
             )
 
-        ce_bank = ps.tile([P, LANES, P], F32, name="ce_bank", tag="bank2")
-        for g in range(LANES):
-            nc.tensor.transpose(ce_bank[:, g, :], ce_col[:, g : g + 1].to_broadcast([P, P]), ident[:])
-        ce_all = sb.tile([P, D], F32, name="ce_all", tag="ce_then_keys")
-        nc.scalar.copy(out=ce_all[:].rearrange("p (m g) -> p m g", g=LANES), in_=ce_bank[:].rearrange("p g m -> p m g"))
-
-        do_il = sb.tile([P, D, LANES], BF16, name="do_il", tag="do_then_window", align_bytes=64)
-        do_codes = sb.tile([P, D], U32, name="do_codes", align_bytes=64)
-        do_scales = sb.tile([P, D], U8, name="do_scales", align_bytes=64)
-        for h in range(2):
-            half = slice(h * D // 2, (h + 1) * D // 2)
+        def weave_do(h):
             nc.vector.tensor_copy(
-                out=do_il[:, half, :].rearrange("p (c i) t -> p c t i", i=4),
+                out=do_il[:, halves[h], :].rearrange("p (c i) t -> p c t i", i=4),
                 in_=do_raw[h][:].rearrange("p t (c i) -> p c t i", i=4),
             )
+
+        def quantise_do(h):
             nc.vector.quantize_mx(
-                out=do_codes[:, half].bitcast(E5M2),
-                scales=do_scales[:, half],
-                in_=do_il[:, half, :].rearrange("p c t -> p (c t)"),
+                out=do_codes[:, halves[h]].bitcast(E5M2),
+                scales=do_scales[:, halves[h]],
+                in_=do_il[:, halves[h], :].rearrange("p c t -> p (c t)"),
             )
 
-        last_window = sb.tile([P, T], F32, name="window2", tag="do_then_window", align_bytes=64)
-        nc.gpsimd.memset(last_window[:].bitcast(I32), 0)
-        zeroed.append(last_window)
-        window = [zeroed[g % WINDOWS] for g in range(LANES)]
+        turn_q(0, nc.vector.tensor_copy)
+        weave_do(0)
+        quantise_do(0)
+        turn_q(1, nc.scalar.copy)
+        quantise_q(0)
+        weave_do(1)
+        quantise_do(1)
+        quantise_q(1)
 
-        s_rows = sb.tile([P, LANES, D], BF16, name="s_rows")
+        rows = sb.tile([P, 3, D], BF16, name="rows", tag="q_then_rows", align_bytes=64)
+        s_late = sb.tile([P, 2, D], BF16, name="s_late")
+        s_rows = [rows[:, 1:3, :], s_late[:]]
+        k_early = rows[:, 0:2, :]
+        nc.vector.tensor_copy(out=k_early[:, 0, :], in_=k_raw[0][:].indirect(offsets[:]))
+        s_il = sb.tile([P, D, 2, 2], BF16, name="s_il", align_bytes=64)
+        s_codes = sb.tile([P, D], U32, name="s_codes", align_bytes=64)
+        s_scales = sb.tile([P, D], U8, name="s_scales", align_bytes=64)
         for j in range(LANES):
             s_bank = ps.tile([P, D], F32, name="s_bank%d" % j, tag="bank%d" % (4 + j))
             nc.tensor.matmul_mx(
@@ -128,38 +142,42 @@ def tile_attend_glin_v_pl_kernel(tc, kT, cd, ce, do, qT, ts, offs, out_0, out_1,
                 stop=True,
             )
             nc.vector.scalar_tensor_tensor(
-                out=s_rows[:, j, :],
-                in0=s_bank[:],
+                out=s_rows[j // 2][:, j % 2, :].rearrange("p (g m) -> p g m", g=LANES),
+                in0=s_bank[:].rearrange("p (m g) -> p g m", g=LANES),
                 scalar=cd_col[:, j : j + 1],
-                in1=ce_all[:],
+                in1=ce_all[:].rearrange("p (g m) -> p g m", g=LANES),
                 op0=MULT,
                 op1=MULT,
             )
-        s_il = sb.tile([P, D, LANES], BF16, name="s_il", align_bytes=64)
-        s_codes = sb.tile([P, D], U32, name="s_codes", align_bytes=64)
-        s_scales = sb.tile([P, D], U8, name="s_scales", align_bytes=64)
-        nc.scalar.copy(
-            out=s_il[:].rearrange("p (g m) j -> p m g j", g=LANES),
-            in_=s_rows[:].rearrange("p j (m g) -> p m g j", g=LANES),
-        )
-        nc.vector.quantize_mx(out=s_codes[:].bitcast(E5M2), scales=s_scales[:], in_=s_il[:].rearrange("p c t -> p (c t)"))
+            if j % 2 == 1:
+                nc.scalar.copy(out=s_il[:, :, j // 2, :], in_=s_rows[j // 2].rearrange("p b c -> p c b"))
 
-        k_il = sb.tile([P, SLOTS, LANES], BF16, name="k_il", tag="keys_then_ts", align_bytes=64)
-        k_codes = sb.tile([P, SLOTS], U32, name="k_codes", align_bytes=64)
+        def quantise_s(a, b):
+            nc.vector.quantize_mx(
+                out=s_codes[:, a:b].bitcast(E5M2),
+                scales=s_scales[:, a:b],
+                in_=s_il[:, a:b].rearrange("p c u b -> p (c u b)"),
+            )
+
+        quantise_s(0, P)
+
+        k_il = sb.tile([P, SLOTS, 2, 2], BF16, name="k_il", tag="keys_then_ts", align_bytes=64)
+        k_codes = sb.tile([P, SLOTS], U32, name="k_codes", tag="codes_then_window", align_bytes=64)
         k_scales = sb.tile([P, SLOTS], U8, name="k_scales", align_bytes=64)
-        k_listed = sb.tile([P, LANES, SLOTS], BF16, name="k_listed", tag="ce_then_keys")
-        for t in range(LANES - 1):
-            nc.vector.tensor_copy(out=k_listed[:, t, :], in_=k_raw[t][:].indirect(offsets[:]))
-        halves = [slice(h * SLOTS // 2, (h + 1) * SLOTS // 2) for h in range(2)]
+        k_late = sb.tile([P, 2, SLOTS], BF16, name="k_late", tag="ce_then_keys")
+        nc.vector.tensor_copy(out=k_early[:, 1, :], in_=k_raw[1][:].indirect(offsets[:]))
+        nc.scalar.copy(out=k_il[:, :, 0, :], in_=k_early.rearrange("p b c -> p c b"))
+        nc.vector.tensor_copy(out=k_late[:, 0, :], in_=k_raw[2][:].indirect(offsets[:]))
         for h in range(2):
             half_list = offsets[:, h * SLOTS // 32 : (h + 1) * SLOTS // 32]
-            nc.vector.tensor_copy(out=k_listed[:, LANES - 1, halves[h]], in_=k_raw[LANES - 1][:].indirect(half_list))
+            nc.vector.tensor_copy(out=k_late[:, 1, halves[h]], in_=k_raw[3][:].indirect(half_list))
         for weave, half in zip((nc.scalar.copy, nc.vector.tensor_copy), halves):
-            weave(
-                out=k_il[:, half, :].rearrange("p (c i) t -> p c t i", i=4),
-                in_=k_listed[:, :, half].rearrange("p t (c i) -> p c t i", i=4),
-            )
-        nc.vector.quantize_mx(out=k_codes[:].bitcast(E4M3), scales=k_scales[:], in_=k_il[:].rearrange("p c t -> p (c t)"))
+            weave(out=k_il[:, half, 1, :], in_=k_late[:, :, half].rearrange("p b c -> p c b"))
+        nc.vector.quantize_mx(
+            out=k_codes[:].bitcast(E4M3), scales=k_scales[:], in_=k_il[:].rearrange("p c u b -> p (c u b)")
+        )
+        quantise_s(P, 2 * P)
+        quantise_s(2 * P, D)
         ts_listed = sb.tile([P, SLOTS], F32, name="ts_listed", tag="keys_then_ts", align_bytes=64)
         nc.vector.tensor_copy(out=ts_listed[:], in_=ts_raw[:].indirect(offsets[:]))
 
@@ -178,6 +196,11 @@ def tile_attend_glin_v_pl_kernel(tc, kT, cd, ce, do, qT, ts, offs, out_0, out_1,
                 stop=True,
             )
             nc.scalar.copy(out=dv0[g][:], in_=dv_bank[:])
+        zeroed.append(sb.tile([P, T], F32, name="window1", tag="ts_then_window"))
+        zeroed.append(sb.tile([P, T], F32, name="window2", tag="codes_then_window", align_bytes=64))
+        for tile in zeroed[1:]:
+            nc.gpsimd.memset(tile[:].bitcast(I32), 0)
+        window = [zeroed[g % WINDOWS] for g in range(LANES)]
         for g in range(LANES):
             nc.vector.tensor_tensor(window[g][:].indirect(offsets[:]), dv0[g][:], ts_listed[:], MULT)
             nc.sync.dma_start(out=out_rows[:, g, :], in_=window[g][:])

@@ -18,9 +18,9 @@ LANES = 4
 D = 512
 T = 2048
 SLOTS = 512
-SPLIT = 896
+SPLIT = 1024
 PIECES = (0, 512, 1024, 1280, 1536, 1792, 2048)
-STORES = (0, 512, 1024, 1792, 2048)
+STORES = (0, 512, 1024, 1536, 1792, 2048)
 WINDOWS = 3
 TIE = 16
 
@@ -34,103 +34,84 @@ def tile_attend_glin_v_pl_kernel(tc, kT, cd, ce, do, qT, ts, offs, out_0, out_1,
         sb = ctx.enter_context(tc.tile_pool(name="sb", bufs=1))
         ps = ctx.enter_context(tc.psum_pool(name="ps", bufs=1))
 
-        cd_col = sb.tile([P, LANES], F32, name="cd_col")
+        shared = sb.tile([P, 3 * D], BF16, name="shared", align_bytes=64)
+        cd_late = sb.tile([P, 2], F32, name="cd_late")
+        cd_col = [shared[:, 0:4].bitcast(F32), cd_late[:]]
         ce_col = sb.tile([P, LANES], F32, name="ce_col")
         nc.scalar.dma_start(out=ce_col[:], in_=ce[0:1, :].rearrange("o (m g) -> m (o g)", g=LANES))
-        nc.scalar.dma_start(out=cd_col[:], in_=cd.rearrange("(p j) o -> p (j o)", j=LANES))
+        for h in range(2):
+            nc.scalar.dma_start(out=cd_col[h], in_=cd.rearrange("(p j) o -> p (j o)", j=LANES)[:, 2 * h : 2 * h + 2])
         q_rows = qT.rearrange("(m j) r -> m j r", j=LANES)
         q_raw = [sb.tile([P, 2, D], F32, name="q_raw%d" % h) for h in range(2)]
         do_rows = do.rearrange("(p t) e -> p t e", t=LANES)
-        do_raw = [sb.tile([P, LANES, D // 2], F32, name="do_raw%d" % h) for h in range(2)]
+        do_raw = [
+            sb.tile([P, LANES, D // 2], F32, name="do_raw%d" % h, tag="do_raw%d" % h, align_bytes=64) for h in range(2)
+        ]
+        nc.sync.dma_start(out=q_raw[0][:], in_=q_rows[:, 0:2, :])
         for h in range(2):
-            nc.sync.dma_start(out=q_raw[h][:], in_=q_rows[:, 2 * h : 2 * h + 2, :])
             nc.sync.dma_start(out=do_raw[h][:], in_=do_rows[:, :, h * D // 2 : (h + 1) * D // 2])
+        nc.sync.dma_start(out=q_raw[1][:], in_=q_rows[:, 2:4, :])
         offsets = sb.tile([P, SLOTS // 16], U16, name="offsets")
         nc.sync.dma_start(offsets[:], offs)
         k_rows = kT.rearrange("(p t) c -> p t c", t=LANES)
-        k_raw = [sb.tile([P, T], F32, name="k_raw%d" % t) for t in range(LANES)]
+        k_raw = [sb.tile([P, T], F32, name="k_raw%d" % t, tag="k_raw%d" % t, align_bytes=64) for t in range(LANES)]
         for t in range(LANES):
             nc.sync.dma_start(out=k_raw[t][:], in_=k_rows[:, t, :])
-        ts_raw = sb.tile([P, T], F32, name="ts_raw", tag="ts_then_window")
+        ts_raw = sb.tile([P, T], F32, name="ts_raw")
         nc.sync.dma_start(out=ts_raw[:], in_=ts)
 
         ident = sb.tile([P, P], F32, name="ident")
         make_identity(nc, ident[:])
-        zeroed = [sb.tile([P, T], F32, name="window0")]
+        zeroed = [sb.tile([P, T], F32, name="window%d" % w) for w in range(2)]
         nc.vector.memset(zeroed[0][:].bitcast(I32), 0)
+        nc.gpsimd.memset(zeroed[1][:].bitcast(I32), 0)
 
         ce_bank = ps.tile([P, LANES, P], F32, name="ce_bank", tag="bank2")
         for g in range(LANES):
             nc.tensor.transpose(ce_bank[:, g, :], ce_col[:, g : g + 1].to_broadcast([P, P]), ident[:])
-        ce_all = sb.tile([P, D], F32, name="ce_all", tag="ce_then_keys")
+        ce_all = sb.tile([P, D], F32, name="ce_all", tag="ce_then_keys", align_bytes=64)
         nc.scalar.copy(out=ce_all[:], in_=ce_bank[:].rearrange("p g m -> p (g m)"))
 
-        q_pairs = sb.tile([P, LANES, 2, P, 2], BF16, name="q_pairs")
-        q_il = [
-            sb.tile([P, D * 2], BF16, name="q_il0", align_bytes=64),
-            sb.tile([P, D * 2], BF16, name="q_il1", tag="q_then_rows", align_bytes=64),
-        ]
         q_codes = sb.tile([P, D], U32, name="q_codes", align_bytes=64)
         q_scales = sb.tile([P, D], U8, name="q_scales", align_bytes=64)
-        do_il = sb.tile([P, D, LANES], BF16, name="do_il", align_bytes=64)
         do_codes = sb.tile([P, D], U32, name="do_codes", align_bytes=64)
         do_scales = sb.tile([P, D], U8, name="do_scales", align_bytes=64)
         halves = [slice(h * D // 2, (h + 1) * D // 2) for h in range(2)]
 
-        def turn_q(h, round_q):
-            round_q(
-                out=q_pairs[:, 2 * h : 2 * h + 2, :, :, :],
-                in_=q_raw[h][:].rearrange("m j (p u b) -> m j u p b", u=2, b=2),
-            )
+        def turn_q(h, round_q, q_il, pairs_tag, bank_tag):
+            q_pairs = sb.tile([P, 2, 2, P, 2], BF16, name="q_pairs%d" % h, tag=pairs_tag, align_bytes=64)
+            round_q(out=q_pairs[:], in_=q_raw[h][:].rearrange("m j (p u b) -> m j u p b", u=2, b=2))
             words = q_pairs[:].rearrange("m j u p b -> m (j u p b)").bitcast(F32)
-            bank = ps.tile([P, 2, 2, P], F32, name="q_bank%d" % h, tag="bank%d" % h)
+            bank = ps.tile([P, 2, 2, P], F32, name="q_bank%d" % h, tag=bank_tag)
             for jj in range(2):
                 for u in range(2):
-                    w0 = ((2 * h + jj) * 2 + u) * P
+                    w0 = (jj * 2 + u) * P
                     nc.tensor.transpose(bank[:, jj, u, :], words[:, w0 : w0 + P], ident[:])
             nc.scalar.copy(
-                out=q_il[h][:].bitcast(F32).rearrange("p (j m u) -> p j m u", j=2, u=2),
+                out=q_il.bitcast(F32).rearrange("p (j m u) -> p j m u", j=2, u=2),
                 in_=bank[:].rearrange("p j u m -> p j m u"),
             )
 
-        def quantise_q(h):
-            nc.vector.quantize_mx(
-                out=q_codes[:, halves[h]].bitcast(E4M3),
-                scales=q_scales[:, halves[h]],
-                in_=q_il[h][:],
+        def quantise_q(h, q_il):
+            nc.vector.quantize_mx(out=q_codes[:, halves[h]].bitcast(E4M3), scales=q_scales[:, halves[h]], in_=q_il)
+
+        def weave_do(copy, do_il, h, c):
+            copy(
+                out=do_il[:, c, :].rearrange("p (c i) t -> p c t i", i=4),
+                in_=do_raw[h][:, :, c].rearrange("p t (c i) -> p c t i", i=4),
             )
 
-        def weave_do(h):
-            nc.vector.tensor_copy(
-                out=do_il[:, halves[h], :].rearrange("p (c i) t -> p c t i", i=4),
-                in_=do_raw[h][:].rearrange("p t (c i) -> p c t i", i=4),
-            )
-
-        def quantise_do(h):
+        def quantise_do(do_il, h):
             nc.vector.quantize_mx(
                 out=do_codes[:, halves[h]].bitcast(E5M2),
                 scales=do_scales[:, halves[h]],
-                in_=do_il[:, halves[h], :].rearrange("p c t -> p (c t)"),
+                in_=do_il[:].rearrange("p c t -> p (c t)"),
             )
 
-        turn_q(0, nc.vector.tensor_copy)
-        weave_do(0)
-        quantise_do(0)
-        turn_q(1, nc.scalar.copy)
-        quantise_q(0)
-        weave_do(1)
-        quantise_do(1)
-        quantise_q(1)
-
-        rows = sb.tile([P, 3, D], BF16, name="rows", tag="q_then_rows", align_bytes=64)
-        s_late = sb.tile([P, 2, D], BF16, name="s_late")
-        s_rows = [rows[:, 1:3, :], s_late[:]]
-        k_early = rows[:, 0:2, :]
-        nc.vector.tensor_copy(out=k_early[:, 0, :], in_=k_raw[0][:].indirect(offsets[:]))
-        s_il = sb.tile([P, D, 2, 2], BF16, name="s_il", align_bytes=64)
+        s_rows = [sb.tile([P, 2, D], BF16, name="s_rows%d" % u) for u in range(2)]
         s_codes = sb.tile([P, D], U32, name="s_codes", align_bytes=64)
-        s_scales = sb.tile([P, D], U8, name="s_scales", align_bytes=64)
-        for j in range(LANES):
+
+        def s_product(j):
             s_bank = ps.tile([P, D], F32, name="s_bank%d" % j, tag="bank%d" % (4 + j))
             nc.tensor.matmul_mx(
                 out=s_bank[:],
@@ -144,40 +125,67 @@ def tile_attend_glin_v_pl_kernel(tc, kT, cd, ce, do, qT, ts, offs, out_0, out_1,
             nc.vector.scalar_tensor_tensor(
                 out=s_rows[j // 2][:, j % 2, :].rearrange("p (g m) -> p g m", g=LANES),
                 in0=s_bank[:].rearrange("p (m g) -> p g m", g=LANES),
-                scalar=cd_col[:, j : j + 1],
+                scalar=cd_col[j // 2][:, j % 2 : j % 2 + 1],
                 in1=ce_all[:].rearrange("p (g m) -> p g m", g=LANES),
                 op0=MULT,
                 op1=MULT,
             )
-            if j % 2 == 1:
-                nc.scalar.copy(out=s_il[:, :, j // 2, :], in_=s_rows[j // 2].rearrange("p b c -> p c b"))
 
-        def quantise_s(a, b):
+        def weave_s(u, c):
+            nc.scalar.copy(out=s_il[:, c, u, :], in_=s_rows[u][:, :, c].rearrange("p b c -> p c b"))
+
+        def quantise_s(a, b, scales):
             nc.vector.quantize_mx(
-                out=s_codes[:, a:b].bitcast(E5M2),
-                scales=s_scales[:, a:b],
-                in_=s_il[:, a:b].rearrange("p c u b -> p (c u b)"),
+                out=s_codes[:, a:b].bitcast(E5M2), scales=scales, in_=s_il[:, a:b].rearrange("p c u b -> p (c u b)")
             )
 
-        quantise_s(0, P)
+        q_il0 = sb.tile([P, 2 * D], BF16, name="q_il0", align_bytes=64)
+        turn_q(0, nc.vector.tensor_copy, q_il0[:], "pairs_do_window", "bank0")
+        do_il0 = sb.tile([P, D // 2, LANES], BF16, name="do_il0", align_bytes=64)
+        weave_do(nc.vector.tensor_copy, do_il0, 0, slice(0, 2 * P))
+        quantise_do(do_il0, 0)
+        do_il1 = sb.tile([P, D // 2, LANES], BF16, name="do_il1", tag="pairs_do_window", align_bytes=64)
+        weave_do(nc.vector.tensor_copy, do_il1, 1, slice(0, P))
+        weave_do(nc.scalar.copy, do_il1, 1, slice(P, 2 * P))
+        quantise_q(0, q_il0[:])
+        quantise_do(do_il1, 1)
+        zeroed.append(sb.tile([P, T], F32, name="window2", tag="pairs_do_window", align_bytes=64))
+        nc.gpsimd.memset(zeroed[2][:].bitcast(I32), 0)
+        s_product(0)
+        s_product(1)
 
         k_il = sb.tile([P, SLOTS, 2, 2], BF16, name="k_il", tag="keys_then_ts", align_bytes=64)
-        k_codes = sb.tile([P, SLOTS], U32, name="k_codes", tag="codes_then_window", align_bytes=64)
+        k_codes = sb.tile([P, SLOTS], U32, name="k_codes", align_bytes=64)
         k_scales = sb.tile([P, SLOTS], U8, name="k_scales", align_bytes=64)
-        k_late = sb.tile([P, 2, SLOTS], BF16, name="k_late", tag="ce_then_keys")
+        k_early = shared[:, 0 : 2 * SLOTS].rearrange("p (b c) -> p b c", b=2)
+        q_il1 = shared[:, D : 3 * D]
+        turn_q(1, nc.scalar.copy, q_il1, "do_raw1", "bank4")
+        s_il = sb.tile([P, D, 2, 2], BF16, name="s_il", tag="do_raw1", align_bytes=64)
+        weave_s(0, slice(0, D))
+        nc.vector.tensor_copy(out=k_early[:, 0, :], in_=k_raw[0][:].indirect(offsets[:]))
+        quantise_q(1, q_il1)
         nc.vector.tensor_copy(out=k_early[:, 1, :], in_=k_raw[1][:].indirect(offsets[:]))
         nc.scalar.copy(out=k_il[:, :, 0, :], in_=k_early.rearrange("p b c -> p c b"))
+        s_product(2)
+        s_product(3)
+        for half in halves:
+            weave_s(1, half)
+        k_late = sb.tile([P, 2, SLOTS], BF16, name="k_late", tag="ce_then_keys", align_bytes=64)
         nc.vector.tensor_copy(out=k_late[:, 0, :], in_=k_raw[2][:].indirect(offsets[:]))
-        for h in range(2):
-            half_list = offsets[:, h * SLOTS // 32 : (h + 1) * SLOTS // 32]
-            nc.vector.tensor_copy(out=k_late[:, 1, halves[h]], in_=k_raw[3][:].indirect(half_list))
-        for weave, half in zip((nc.scalar.copy, nc.vector.tensor_copy), halves):
+        shares = (slice(0, 256), slice(256, SLOTS))
+        for c in shares:
+            part_list = offsets[:, c.start // 16 : c.stop // 16]
+            nc.vector.tensor_copy(out=k_late[:, 1, c], in_=k_raw[3][:].indirect(part_list))
+        s_first = sb.tile([P, D // 2], U8, name="s_first", tag="k_raw3", align_bytes=64)
+        quantise_s(0, D // 2, s_first[:])
+        for weave, half in zip((nc.scalar.copy, nc.vector.tensor_copy), shares):
             weave(out=k_il[:, half, 1, :], in_=k_late[:, :, half].rearrange("p b c -> p c b"))
         nc.vector.quantize_mx(
             out=k_codes[:].bitcast(E4M3), scales=k_scales[:], in_=k_il[:].rearrange("p c u b -> p (c u b)")
         )
-        quantise_s(P, 2 * P)
-        quantise_s(2 * P, D)
+        s_rest = sb.tile([P, D // 2], U8, name="s_rest", tag="ce_then_keys", align_bytes=64)
+        quantise_s(D // 2, D, s_rest[:])
+        s_scales = [tile[:, P * g : P * (g + 1)] for tile in (s_first, s_rest) for g in range(2)]
         ts_listed = sb.tile([P, SLOTS], F32, name="ts_listed", tag="keys_then_ts", align_bytes=64)
         nc.vector.tensor_copy(out=ts_listed[:], in_=ts_raw[:].indirect(offsets[:]))
 
@@ -189,17 +197,13 @@ def tile_attend_glin_v_pl_kernel(tc, kT, cd, ce, do, qT, ts, offs, out_0, out_1,
             nc.tensor.matmul_mx(
                 out=dv_bank[:],
                 lhsT=s_codes[:, P * g : P * (g + 1)].bitcast(E5M2),
-                lhsT_scale=s_scales[:, P * g : P * (g + 1)],
+                lhsT_scale=s_scales[g],
                 rhs=k_codes[:].bitcast(E4M3),
                 rhs_scale=k_scales[:],
                 start=True,
                 stop=True,
             )
             nc.scalar.copy(out=dv0[g][:], in_=dv_bank[:])
-        zeroed.append(sb.tile([P, T], F32, name="window1", tag="ts_then_window"))
-        zeroed.append(sb.tile([P, T], F32, name="window2", tag="codes_then_window", align_bytes=64))
-        for tile in zeroed[1:]:
-            nc.gpsimd.memset(tile[:].bitcast(I32), 0)
         window = [zeroed[g % WINDOWS] for g in range(LANES)]
         for g in range(LANES):
             nc.vector.tensor_tensor(window[g][:].indirect(offsets[:]), dv0[g][:], ts_listed[:], MULT)
@@ -219,13 +223,9 @@ def tile_attend_glin_v_pl_kernel(tc, kT, cd, ce, do, qT, ts, offs, out_0, out_1,
         il_words = y_il[:].bitcast(F32).rearrange("p (c u) -> p c u", u=2)
         words_out = out_1.rearrange("a p c l -> p (a c l)").bitcast(I32)
 
-        def round_and_weave(copy, c):
-            copy(out=y_pairs[:, 1, c, 1], in_=window[3][:, c])
-            copy(out=il_words[:, c, :], in_=y_words[:, c, :])
-
-        scalar_cuts = (SPLIT,) + PIECES[3:]
-        for a, b in zip(scalar_cuts, scalar_cuts[1:]):
-            round_and_weave(nc.scalar.copy, slice(a, b))
+        nc.scalar.copy(out=y_pairs[:, 1, SPLIT:T, 1], in_=window[3][:, SPLIT:T])
+        for a, b in zip(PIECES[2:], PIECES[3:]):
+            nc.scalar.copy(out=il_words[:, a:b, :], in_=y_words[:, a:b, :])
         vector_parts = (slice(0, PIECES[1]), slice(PIECES[1], SPLIT))
         for c in vector_parts:
             nc.vector.tensor_copy(out=y_pairs[:, 1, c, 1], in_=window[3][:, c])

@@ -18,8 +18,8 @@ LANES = 4
 D = 512
 T = 2048
 SLOTS = 512
-SPLIT = 1024
-PIECES = (0, 512, 1024, 1280, 1536, 1792, 2048)
+SPLIT = 1088
+PIECES = (0, 512, 1024, 1280, 1536, 1792, 1920, 2048)
 STORES = (0, 512, 1024, 1536, 1792, 2048)
 WINDOWS = 3
 TIE = 16
@@ -180,9 +180,10 @@ def tile_attend_glin_v_pl_kernel(tc, kT, cd, ce, do, qT, ts, offs, out_0, out_1,
         quantise_s(0, D // 2, s_first[:])
         for weave, half in zip((nc.scalar.copy, nc.vector.tensor_copy), shares):
             weave(out=k_il[:, half, 1, :], in_=k_late[:, :, half].rearrange("p b c -> p c b"))
-        nc.vector.quantize_mx(
-            out=k_codes[:].bitcast(E4M3), scales=k_scales[:], in_=k_il[:].rearrange("p c u b -> p (c u b)")
-        )
+        for c in shares:
+            nc.vector.quantize_mx(
+                out=k_codes[:, c].bitcast(E4M3), scales=k_scales[:, c], in_=k_il[:, c].rearrange("p c u b -> p (c u b)")
+            )
         s_rest = sb.tile([P, D // 2], U8, name="s_rest", tag="ce_then_keys", align_bytes=64)
         quantise_s(D // 2, D, s_rest[:])
         s_scales = [tile[:, P * g : P * (g + 1)] for tile in (s_first, s_rest) for g in range(2)]
@@ -224,7 +225,7 @@ def tile_attend_glin_v_pl_kernel(tc, kT, cd, ce, do, qT, ts, offs, out_0, out_1,
         words_out = out_1.rearrange("a p c l -> p (a c l)").bitcast(I32)
 
         nc.scalar.copy(out=y_pairs[:, 1, SPLIT:T, 1], in_=window[3][:, SPLIT:T])
-        for a, b in zip(PIECES[2:], PIECES[3:]):
+        for a, b in zip((SPLIT,) + PIECES[3:], PIECES[3:]):
             nc.scalar.copy(out=il_words[:, a:b, :], in_=y_words[:, a:b, :])
         vector_parts = (slice(0, PIECES[1]), slice(PIECES[1], SPLIT))
         for c in vector_parts:

@@ -1,7 +1,6 @@
 from contextlib import ExitStack
 
 import concourse.mybir as mybir
-from concourse.masks import make_identity
 
 F32 = mybir.dt.float32
 BF16 = mybir.dt.bfloat16
@@ -12,14 +11,16 @@ U8 = mybir.dt.uint8
 E4M3 = mybir.dt.float8_e4m3fn_x4
 E5M2 = mybir.dt.float8_e5m2_x4
 MULT = mybir.AluOpType.mult
+COPY = mybir.ActivationFunctionType.Copy
 
 P = 128
 LANES = 4
 D = 512
 T = 2048
 SLOTS = 512
-SPLIT = 1088
-PIECES = (0, 512, 1024, 1280, 1536, 1792, 1920, 2048)
+SPLIT = 896
+PIECE = 256
+PIECES = (0, 256, 512, 768, 1024, 1280, 1536, 1792, 1920, 2048)
 STORES = (0, 512, 1024, 1536, 1792, 2048)
 WINDOWS = 3
 TIE = 16
@@ -33,85 +34,104 @@ def tile_attend_glin_v_pl_kernel(tc, kT, cd, ce, do, qT, ts, offs, out_0, out_1,
     with ExitStack() as ctx:
         sb = ctx.enter_context(tc.tile_pool(name="sb", bufs=1))
         ps = ctx.enter_context(tc.psum_pool(name="ps", bufs=1))
+        halves = [slice(h * D // 2, (h + 1) * D // 2) for h in range(2)]
 
-        shared = sb.tile([P, 3 * D], BF16, name="shared", align_bytes=64)
-        cd_late = sb.tile([P, 2], F32, name="cd_late")
-        cd_col = [shared[:, 0:4].bitcast(F32), cd_late[:]]
+        cd_col = sb.tile([P, LANES], F32, name="cd_col")
         ce_col = sb.tile([P, LANES], F32, name="ce_col")
+        nc.scalar.dma_start(out=cd_col[:], in_=cd.rearrange("(p j) o -> p (j o)", j=LANES))
         nc.scalar.dma_start(out=ce_col[:], in_=ce[0:1, :].rearrange("o (m g) -> m (o g)", g=LANES))
-        for h in range(2):
-            nc.scalar.dma_start(out=cd_col[h], in_=cd.rearrange("(p j) o -> p (j o)", j=LANES)[:, 2 * h : 2 * h + 2])
         q_rows = qT.rearrange("(m j) r -> m j r", j=LANES)
-        q_raw = [sb.tile([P, 2, D], F32, name="q_raw%d" % h) for h in range(2)]
+        q_raw = [sb.tile([P, D], F32, name="q_raw%d" % j) for j in range(LANES)]
         do_rows = do.rearrange("(p t) e -> p t e", t=LANES)
-        do_raw = [
-            sb.tile([P, LANES, D // 2], F32, name="do_raw%d" % h, tag="do_raw%d" % h, align_bytes=64) for h in range(2)
-        ]
-        nc.sync.dma_start(out=q_raw[0][:], in_=q_rows[:, 0:2, :])
+        do_raw = [sb.tile([P, LANES, D // 2], F32, name="do_raw%d" % h) for h in range(2)]
+        ts_col = sb.tile([P, T // P], F32, name="ts_col", tag="ts_then_q")
+        nc.sync.dma_start(out=ts_col[:], in_=ts[0:1, :].rearrange("o (n g) -> n (o g)", n=P))
         for h in range(2):
-            nc.sync.dma_start(out=do_raw[h][:], in_=do_rows[:, :, h * D // 2 : (h + 1) * D // 2])
-        nc.sync.dma_start(out=q_raw[1][:], in_=q_rows[:, 2:4, :])
+            nc.sync.dma_start(out=do_raw[h][:], in_=do_rows[:, :, halves[h]])
+        for j in range(LANES):
+            nc.sync.dma_start(out=q_raw[j][:], in_=q_rows[:, j, :])
         offsets = sb.tile([P, SLOTS // 16], U16, name="offsets")
         nc.sync.dma_start(offsets[:], offs)
         k_rows = kT.rearrange("(p t) c -> p t c", t=LANES)
-        k_raw = [sb.tile([P, T], F32, name="k_raw%d" % t, tag="k_raw%d" % t, align_bytes=64) for t in range(LANES)]
+        k_raw = [sb.tile([P, T], F32, name="k_raw%d" % t) for t in range(LANES)]
         for t in range(LANES):
             nc.sync.dma_start(out=k_raw[t][:], in_=k_rows[:, t, :])
-        ts_raw = sb.tile([P, T], F32, name="ts_raw")
-        nc.sync.dma_start(out=ts_raw[:], in_=ts)
 
         ident = sb.tile([P, P], F32, name="ident")
-        make_identity(nc, ident[:])
-        zeroed = [sb.tile([P, T], F32, name="window%d" % w) for w in range(2)]
+        zero_block = sb.tile([P, P], F32, name="zero_block", tag="window1")
+        nc.gpsimd.memset(zero_block[:], 0.0)
+        nc.gpsimd.affine_select(
+            out=ident[:],
+            in_=zero_block[:],
+            compare_op=mybir.AluOpType.not_equal,
+            fill=1.0,
+            base=0,
+            pattern=[[-1, P]],
+            channel_multiplier=1,
+        )
+        zeroed = [sb.tile([P, T], F32, name="window%d" % w, tag="window%d" % w) for w in range(2)]
         nc.vector.memset(zeroed[0][:].bitcast(I32), 0)
         nc.gpsimd.memset(zeroed[1][:].bitcast(I32), 0)
 
-        ce_bank = ps.tile([P, LANES, P], F32, name="ce_bank", tag="bank2")
-        for g in range(LANES):
-            nc.tensor.transpose(ce_bank[:, g, :], ce_col[:, g : g + 1].to_broadcast([P, P]), ident[:])
-        ce_all = sb.tile([P, D], F32, name="ce_all", tag="ce_then_keys", align_bytes=64)
-        nc.scalar.copy(out=ce_all[:], in_=ce_bank[:].rearrange("p g m -> p (g m)"))
+        def turn_words(words, bank):
+            for block, columns in enumerate(words):
+                nc.tensor.transpose(bank[:, block, :], columns, ident[:])
 
-        q_codes = sb.tile([P, D], U32, name="q_codes", align_bytes=64)
-        q_scales = sb.tile([P, D], U8, name="q_scales", align_bytes=64)
+        def weave_words(woven, bank):
+            nc.scalar.copy(
+                out=woven.bitcast(F32).rearrange("p (j m u) -> p j m u", m=P, u=2),
+                in_=bank[:].rearrange("p (j u) m -> p j m u", u=2),
+            )
+
+        def quantise(codes, scales, fmt, woven):
+            nc.vector.quantize_mx(out=codes.bitcast(fmt), scales=scales, in_=woven)
+
+        ts_raw = sb.tile([P, T], F32, name="ts_raw")
+        for i in range(4):
+            bank = ps.tile([P, 4, P], F32, name="ts_bank%d" % i, tag="bank%d" % (4 + i))
+            turn_words([ts_col[:, 4 * i + g : 4 * i + g + 1].to_broadcast([P, P]) for g in range(4)], bank)
+            nc.scalar.copy(
+                out=ts_raw[:].rearrange("p (n i g) -> p i n g", i=4, g=4)[:, i], in_=bank[:].rearrange("p g n -> p n g")
+            )
+
         do_codes = sb.tile([P, D], U32, name="do_codes", align_bytes=64)
         do_scales = sb.tile([P, D], U8, name="do_scales", align_bytes=64)
-        halves = [slice(h * D // 2, (h + 1) * D // 2) for h in range(2)]
-
-        def turn_q(h, round_q, q_il, pairs_tag, bank_tag):
-            q_pairs = sb.tile([P, 2, 2, P, 2], BF16, name="q_pairs%d" % h, tag=pairs_tag, align_bytes=64)
-            round_q(out=q_pairs[:], in_=q_raw[h][:].rearrange("m j (p u b) -> m j u p b", u=2, b=2))
-            words = q_pairs[:].rearrange("m j u p b -> m (j u p b)").bitcast(F32)
-            bank = ps.tile([P, 2, 2, P], F32, name="q_bank%d" % h, tag=bank_tag)
-            for jj in range(2):
-                for u in range(2):
-                    w0 = (jj * 2 + u) * P
-                    nc.tensor.transpose(bank[:, jj, u, :], words[:, w0 : w0 + P], ident[:])
-            nc.scalar.copy(
-                out=q_il.bitcast(F32).rearrange("p (j m u) -> p j m u", j=2, u=2),
-                in_=bank[:].rearrange("p j u m -> p j m u"),
+        do_il = [sb.tile([P, D // 2, LANES], BF16, name="do_il%d" % h, tag="do_il%d" % h, align_bytes=64) for h in range(2)]
+        for h in range(2):
+            nc.vector.tensor_copy(
+                out=do_il[h][:].rearrange("p (c i) t -> p c t i", i=4),
+                in_=do_raw[h][:].rearrange("p t (c i) -> p c t i", i=4),
             )
+        for h in range(2):
+            quantise(do_codes[:, halves[h]], do_scales[:, halves[h]], E5M2, do_il[h][:].rearrange("p c t -> p (c t)"))
 
-        def quantise_q(h, q_il):
-            nc.vector.quantize_mx(out=q_codes[:, halves[h]].bitcast(E4M3), scales=q_scales[:, halves[h]], in_=q_il)
-
-        def weave_do(copy, do_il, h, c):
-            copy(
-                out=do_il[:, c, :].rearrange("p (c i) t -> p c t i", i=4),
-                in_=do_raw[h][:, :, c].rearrange("p t (c i) -> p c t i", i=4),
+        codes = sb.tile([P, D + SLOTS], U32, name="codes", align_bytes=64)
+        scales = sb.tile([P, D + SLOTS], U8, name="scales", align_bytes=64)
+        q_codes, k_codes = codes[:, 0:D], codes[:, D : D + SLOTS]
+        q_scales, k_scales = scales[:, 0:D], scales[:, D : D + SLOTS]
+        q_first = sb.tile([P, D], BF16, name="q_first", tag="ts_then_q")
+        q_later = sb.tile([P, 3 * D], BF16, name="q_later", tag="do_il0", align_bytes=64)
+        q_pairs = [q_first[:]] + [q_later[:, D * j : D * (j + 1)] for j in range(3)]
+        shared = sb.tile([P, 11 * D // 2], BF16, name="shared", align_bytes=64)
+        q_il = shared[:, 0 : LANES * D]
+        ts_listed = shared[:, 0 : 2 * D].bitcast(F32)
+        for j in range(LANES):
+            round_q = nc.scalar.copy if j == 0 else nc.vector.tensor_copy
+            round_q(
+                out=q_pairs[j].rearrange("m (u p b) -> m u p b", u=2, b=2),
+                in_=q_raw[j][:].rearrange("m (p u b) -> m u p b", u=2, b=2),
             )
+            bank = ps.tile([P, 2, P], F32, name="q_bank%d" % j, tag="bank%d" % j)
+            words = q_pairs[j].bitcast(F32)
+            turn_words([words[:, P * u : P * (u + 1)] for u in range(2)], bank)
+            weave_words(q_il[:, D * j : D * (j + 1)], bank)
+            columns = slice(P * j, P * (j + 1))
+            if j == LANES - 1:
+                nc.vector.tensor_copy(out=ts_listed, in_=ts_raw[:].indirect(offsets[:]))
+            quantise(q_codes[:, columns], q_scales[:, columns], E4M3, q_il[:, D * j : D * (j + 1)])
 
-        def quantise_do(do_il, h):
-            nc.vector.quantize_mx(
-                out=do_codes[:, halves[h]].bitcast(E5M2),
-                scales=do_scales[:, halves[h]],
-                in_=do_il[:].rearrange("p c t -> p (c t)"),
-            )
-
-        s_rows = [sb.tile([P, 2, D], BF16, name="s_rows%d" % u) for u in range(2)]
-        s_codes = sb.tile([P, D], U32, name="s_codes", align_bytes=64)
-
-        def s_product(j):
+        turned = [ps.tile([P, LANES, P], F32, name="turned%d" % g, tag="bank%d" % g) for g in range(LANES)]
+        for j in range(LANES):
             s_bank = ps.tile([P, D], F32, name="s_bank%d" % j, tag="bank%d" % (4 + j))
             nc.tensor.matmul_mx(
                 out=s_bank[:],
@@ -122,129 +142,142 @@ def tile_attend_glin_v_pl_kernel(tc, kT, cd, ce, do, qT, ts, offs, out_0, out_1,
                 start=True,
                 stop=True,
             )
-            nc.vector.scalar_tensor_tensor(
-                out=s_rows[j // 2][:, j % 2, :].rearrange("p (g m) -> p g m", g=LANES),
-                in0=s_bank[:].rearrange("p (m g) -> p g m", g=LANES),
-                scalar=cd_col[j // 2][:, j % 2 : j % 2 + 1],
-                in1=ce_all[:].rearrange("p (g m) -> p g m", g=LANES),
-                op0=MULT,
-                op1=MULT,
+            s_cd = sb.tile([P, LANES, P], F32, name="s_cd%d" % j, tag="s_cd%d" % j, align_bytes=64)
+            nc.scalar.activation(
+                out=s_cd[:], in_=s_bank[:].rearrange("p (m g) -> p g m", g=LANES), func=COPY, scale=cd_col[:, j : j + 1]
+            )
+            for g in range(LANES):
+                nc.tensor.transpose(turned[g][:, j, :], s_cd[:, g, :], ident[:])
+
+        k_pair = shared[:, 5 * D // 2 : 9 * D // 2].rearrange("p (b c) -> p b c", b=2)
+        s_late = sb.tile([P, 2 * D], BF16, name="s_late", tag="window2", align_bytes=64)
+        s_il = [shared[:, 7 * D // 2 : 11 * D // 2], s_late[:]]
+        for b in range(2):
+            nc.vector.tensor_copy(out=k_pair[:, b, :], in_=k_raw[b][:].indirect(offsets[:]))
+
+        k_il = sb.tile([P, SLOTS, 2, 2], BF16, name="k_il", tag="keys_then_scales", align_bytes=64)
+        nc.vector.tensor_copy(out=k_il[:, :, 0, :], in_=k_pair.rearrange("p b c -> p c b"))
+        nc.vector.tensor_copy(out=k_pair[:, 0, :], in_=k_raw[2][:].indirect(offsets[:]))
+
+        s_pairs = [sb.tile([P, 2 * P, 2], BF16, name="s_pairs%d" % g) for g in range(LANES)]
+
+        def round_s(g):
+            nc.scalar.activation(
+                out=s_pairs[g][:].rearrange("m (u p) b -> m u p b", u=2),
+                in_=turned[g][:].rearrange("m (u b) p -> m u p b", u=2),
+                func=COPY,
+                scale=ce_col[:, g : g + 1],
             )
 
-        def weave_s(u, c):
-            nc.scalar.copy(out=s_il[:, c, u, :], in_=s_rows[u][:, :, c].rearrange("p b c -> p c b"))
+        def turn_s_back(h):
+            bank = ps.tile([P, 4, P], F32, name="s_words%d" % h, tag="bank%d" % (4 + h))
+            words = [s_pairs[2 * h + i][:].rearrange("m w b -> m (w b)").bitcast(F32) for i in range(2)]
+            turn_words([words[block // 2][:, P * (block % 2) : P * (block % 2 + 1)] for block in range(4)], bank)
+            weave_words(s_il[h], bank)
 
-        def quantise_s(a, b, scales):
-            nc.vector.quantize_mx(
-                out=s_codes[:, a:b].bitcast(E5M2), scales=scales, in_=s_il[:, a:b].rearrange("p c u b -> p (c u b)")
-            )
+        for g in range(3):
+            round_s(g)
+        turn_s_back(0)
+        round_s(3)
+        turn_s_back(1)
+        s_codes = sb.tile([P, D], U32, name="s_codes", align_bytes=64)
+        s_first = sb.tile([P, D // 2], U8, name="s_first", align_bytes=64)
+        quantise(s_codes[:, halves[0]], s_first[:], E5M2, s_il[0])
 
-        q_il0 = sb.tile([P, 2 * D], BF16, name="q_il0", align_bytes=64)
-        turn_q(0, nc.vector.tensor_copy, q_il0[:], "pairs_do_window", "bank0")
-        do_il0 = sb.tile([P, D // 2, LANES], BF16, name="do_il0", align_bytes=64)
-        weave_do(nc.vector.tensor_copy, do_il0, 0, slice(0, 2 * P))
-        quantise_do(do_il0, 0)
-        do_il1 = sb.tile([P, D // 2, LANES], BF16, name="do_il1", tag="pairs_do_window", align_bytes=64)
-        weave_do(nc.vector.tensor_copy, do_il1, 1, slice(0, P))
-        weave_do(nc.scalar.copy, do_il1, 1, slice(P, 2 * P))
-        quantise_q(0, q_il0[:])
-        quantise_do(do_il1, 1)
-        zeroed.append(sb.tile([P, T], F32, name="window2", tag="pairs_do_window", align_bytes=64))
+        parts = [slice(P * i, P * (i + 1)) for i in range(4)]
+        for c in parts:
+            nc.vector.tensor_copy(out=k_pair[:, 1, c], in_=k_raw[3][:].indirect(offsets[:, c.start // 16 : c.stop // 16]))
+
+        def weave_keys(copy, c):
+            copy(out=k_il[:, c, 1, :], in_=k_pair[:, :, c].rearrange("p b c -> p c b"))
+
+        def quantise_keys(c):
+            quantise(k_codes[:, c], k_scales[:, c], E4M3, k_il[:, c].rearrange("p c u b -> p (c u b)"))
+
+        for i in (0, 1, 3):
+            weave_keys(nc.scalar.copy, parts[i])
+        quantise_keys(halves[0])
+        weave_keys(nc.vector.tensor_copy, parts[2])
+        quantise_keys(halves[1])
+        s_rest = sb.tile([P, D // 2], U8, name="s_rest", tag="keys_then_scales", align_bytes=64)
+        quantise(s_codes[:, halves[1]], s_rest[:], E5M2, s_il[1])
+        zeroed.append(sb.tile([P, T], F32, name="window2", tag="window2", align_bytes=64))
         nc.gpsimd.memset(zeroed[2][:].bitcast(I32), 0)
-        s_product(0)
-        s_product(1)
-
-        k_il = sb.tile([P, SLOTS, 2, 2], BF16, name="k_il", tag="keys_then_ts", align_bytes=64)
-        k_codes = sb.tile([P, SLOTS], U32, name="k_codes", align_bytes=64)
-        k_scales = sb.tile([P, SLOTS], U8, name="k_scales", align_bytes=64)
-        k_early = shared[:, 0 : 2 * SLOTS].rearrange("p (b c) -> p b c", b=2)
-        q_il1 = shared[:, D : 3 * D]
-        turn_q(1, nc.scalar.copy, q_il1, "do_raw1", "bank4")
-        s_il = sb.tile([P, D, 2, 2], BF16, name="s_il", tag="do_raw1", align_bytes=64)
-        weave_s(0, slice(0, D))
-        nc.vector.tensor_copy(out=k_early[:, 0, :], in_=k_raw[0][:].indirect(offsets[:]))
-        quantise_q(1, q_il1)
-        nc.vector.tensor_copy(out=k_early[:, 1, :], in_=k_raw[1][:].indirect(offsets[:]))
-        nc.scalar.copy(out=k_il[:, :, 0, :], in_=k_early.rearrange("p b c -> p c b"))
-        s_product(2)
-        s_product(3)
-        for half in halves:
-            weave_s(1, half)
-        k_late = sb.tile([P, 2, SLOTS], BF16, name="k_late", tag="ce_then_keys", align_bytes=64)
-        nc.vector.tensor_copy(out=k_late[:, 0, :], in_=k_raw[2][:].indirect(offsets[:]))
-        shares = (slice(0, 256), slice(256, SLOTS))
-        for c in shares:
-            part_list = offsets[:, c.start // 16 : c.stop // 16]
-            nc.vector.tensor_copy(out=k_late[:, 1, c], in_=k_raw[3][:].indirect(part_list))
-        s_first = sb.tile([P, D // 2], U8, name="s_first", tag="k_raw3", align_bytes=64)
-        quantise_s(0, D // 2, s_first[:])
-        for weave, half in zip((nc.scalar.copy, nc.vector.tensor_copy), shares):
-            weave(out=k_il[:, half, 1, :], in_=k_late[:, :, half].rearrange("p b c -> p c b"))
-        for c in shares:
-            nc.vector.quantize_mx(
-                out=k_codes[:, c].bitcast(E4M3), scales=k_scales[:, c], in_=k_il[:, c].rearrange("p c u b -> p (c u b)")
-            )
-        s_rest = sb.tile([P, D // 2], U8, name="s_rest", tag="ce_then_keys", align_bytes=64)
-        quantise_s(D // 2, D, s_rest[:])
         s_scales = [tile[:, P * g : P * (g + 1)] for tile in (s_first, s_rest) for g in range(2)]
-        ts_listed = sb.tile([P, SLOTS], F32, name="ts_listed", tag="keys_then_ts", align_bytes=64)
-        nc.vector.tensor_copy(out=ts_listed[:], in_=ts_raw[:].indirect(offsets[:]))
 
         out_rows = out_0.rearrange("(p g) c -> p g c", g=LANES)
         y_pairs = sb.tile([P, 2, T, 2], BF16, name="y_pairs")
         dv0 = [sb.tile([P, SLOTS], F32, name="dv0_%d" % g) for g in range(LANES)]
-        for g in range(LANES):
-            dv_bank = ps.tile([P, SLOTS], F32, name="dv_bank%d" % g, tag="bank%d" % g)
+
+        def dv_product(g, first, bank_tag, c):
+            dv_bank = ps.tile([P, SLOTS], F32, name="dv_bank", tag=bank_tag)
             nc.tensor.matmul_mx(
                 out=dv_bank[:],
                 lhsT=s_codes[:, P * g : P * (g + 1)].bitcast(E5M2),
                 lhsT_scale=s_scales[g],
-                rhs=k_codes[:].bitcast(E4M3),
-                rhs_scale=k_scales[:],
+                rhs=codes[:, first : first + SLOTS].bitcast(E4M3),
+                rhs_scale=scales[:, first : first + SLOTS],
                 start=True,
                 stop=True,
             )
-            nc.scalar.copy(out=dv0[g][:], in_=dv_bank[:])
+            shift = D - first
+            nc.scalar.copy(out=dv0[g][:, c], in_=dv_bank[:, c.start + shift : c.stop + shift])
+
+        dv_product(0, D // 2, "bank6", halves[0])
+        dv_product(0, D, "bank0", halves[1])
+        for g in range(1, LANES):
+            dv_product(g, D, "bank%d" % g, slice(0, SLOTS))
         window = [zeroed[g % WINDOWS] for g in range(LANES)]
         for g in range(LANES):
-            nc.vector.tensor_tensor(window[g][:].indirect(offsets[:]), dv0[g][:], ts_listed[:], MULT)
+            for c in halves if g == 0 else [slice(0, SLOTS)]:
+                listed = offsets[:, c.start // 16 : c.stop // 16]
+                nc.vector.tensor_tensor(window[g][:].indirect(listed), dv0[g][:, c], ts_listed[:, c], MULT)
             nc.sync.dma_start(out=out_rows[:, g, :], in_=window[g][:])
             if g < 2:
                 nc.scalar.copy(out=y_pairs[:, 0, :, g], in_=window[g][:])
             if g == 2:
-                tie = slice(PIECES[1] - TIE // 2, PIECES[1] + TIE // 2)
-                nc.scalar.copy(out=y_pairs[:, 1, 0:SPLIT, 0], in_=window[g][:, 0:SPLIT])
+                tie = slice(PIECE - TIE // 2, PIECE + TIE // 2)
+                nc.scalar.copy(out=y_pairs[:, 1, PIECE:SPLIT, 0], in_=window[g][:, PIECE:SPLIT])
                 nc.scalar.copy(out=y_pairs[:, 1, tie, :], in_=window[g][:, tie].unsqueeze(2).to_broadcast([P, TIE, 2]))
                 nc.scalar.copy(out=y_pairs[:, 1, SPLIT:T, 0], in_=window[g][:, SPLIT:T])
 
         y_words = y_pairs[:].rearrange("p u c b -> p (u c b)").bitcast(F32).rearrange("p (u c) -> p c u", u=2)
         y_il = sb.tile([P, T * LANES], BF16, name="y_il", align_bytes=64)
         y_codes = sb.tile([P, T], U32, name="y_codes", align_bytes=64)
-        y_scales = sb.tile([P, T], U8, name="y_scales", align_bytes=64)
+        y_scales = sb.tile([P, T // 4], U8, name="y_scales", align_bytes=64)
         il_words = y_il[:].bitcast(F32).rearrange("p (c u) -> p c u", u=2)
         words_out = out_1.rearrange("a p c l -> p (a c l)").bitcast(I32)
 
-        nc.scalar.copy(out=y_pairs[:, 1, SPLIT:T, 1], in_=window[3][:, SPLIT:T])
-        for a, b in zip((SPLIT,) + PIECES[3:], PIECES[3:]):
+        for c in (slice(SPLIT, T - 2 * PIECE), slice(T - 2 * PIECE, T)):
+            nc.scalar.copy(out=y_pairs[:, 1, c, 1], in_=window[3][:, c])
+        scalar_cuts = (SPLIT,) + tuple(b for b in PIECES if b > SPLIT)
+        for a, b in zip(scalar_cuts, scalar_cuts[1:]):
             nc.scalar.copy(out=il_words[:, a:b, :], in_=y_words[:, a:b, :])
-        vector_parts = (slice(0, PIECES[1]), slice(PIECES[1], SPLIT))
-        for c in vector_parts:
+        nc.vector.tensor_copy(out=y_pairs[:, 1, 0:PIECE, 0], in_=window[2][:, 0:PIECE])
+        for c in (slice(0, PIECE), slice(PIECE, SPLIT)):
             nc.vector.tensor_copy(out=y_pairs[:, 1, c, 1], in_=window[3][:, c])
-        for c in vector_parts:
-            nc.vector.tensor_copy(out=il_words[:, c, :], in_=y_words[:, c, :])
-        for a, b in zip(PIECES, PIECES[1:]):
-            nc.vector.quantize_mx(
-                out=y_codes[:, a:b].bitcast(E4M3),
-                scales=y_scales[:, a:b],
-                in_=y_il[:, a * LANES : b * LANES],
+
+        def weave_y(a, b):
+            nc.vector.tensor_copy(out=il_words[:, a:b, :], in_=y_words[:, a:b, :])
+
+        def quantise_y(a, b):
+            quarter, first = divmod(a, T // 4)
+            quantise(
+                y_codes[:, a:b], y_scales[4 * quarter : P, first : first + b - a], E4M3, y_il[:, a * LANES : b * LANES]
             )
             if b in STORES:
                 c = slice(STORES[STORES.index(b) - 1], b)
                 nc.sync.dma_start(out=words_out[:, c], in_=y_codes[:, c].bitcast(I32))
-        scales_out = out_2.rearrange("a f c -> (a f) c").bitcast(I32)
+
+        weave_y(0, PIECE)
+        for a, b in zip(PIECES, PIECES[1:]):
+            if b < SPLIT:
+                weave_y(b, min(b + PIECE, SPLIT))
+            quantise_y(a, b)
+        scales_out = out_2.bitcast(I32).rearrange("a (q f) (j c) -> (a q) j f c", f=4, j=4)
         for quad in range(4):
             queue = nc.sync if quad % 2 == 0 else nc.scalar
             queue.dma_start(
-                out=scales_out[4 * quad : 4 * quad + 4, :],
-                in_=y_scales[32 * quad : 32 * quad + 4, :].bitcast(I32),
+                out=scales_out[quad],
+                in_=y_scales[32 * quad : 32 * quad + 16, :].bitcast(I32),
             )

@@ -112,7 +112,7 @@ def tile_attend_glin_v_pl_kernel(tc, kT, cd, ce, do, qT, ts, offs, out_0, out_1,
         q_first = sb.tile([P, D], BF16, name="q_first", tag="ts_then_q")
         q_later = sb.tile([P, 3 * D], BF16, name="q_later", tag="do_il0", align_bytes=64)
         q_pairs = [q_first[:]] + [q_later[:, D * j : D * (j + 1)] for j in range(3)]
-        shared = sb.tile([P, 11 * D // 2], BF16, name="shared", align_bytes=64)
+        shared = sb.tile([P, 17 * D // 2], BF16, name="shared", align_bytes=64)
         q_il = shared[:, 0 : LANES * D]
         ts_listed = shared[:, 0 : 2 * D].bitcast(F32)
         for j in range(LANES):
@@ -130,6 +130,8 @@ def tile_attend_glin_v_pl_kernel(tc, kT, cd, ce, do, qT, ts, offs, out_0, out_1,
                 nc.vector.tensor_copy(out=ts_listed, in_=ts_raw[:].indirect(offsets[:]))
             quantise(q_codes[:, columns], q_scales[:, columns], E4M3, q_il[:, D * j : D * (j + 1)])
 
+        s_cd_rows = [sb.tile([P, D], F32, name="s_cd%d" % j)[:] for j in range(LANES - 1)]
+        s_cd_rows.append(shared[:, 9 * D // 2 : 13 * D // 2].bitcast(F32))
         turned = [ps.tile([P, LANES, P], F32, name="turned%d" % g, tag="bank%d" % g) for g in range(LANES)]
         for j in range(LANES):
             s_bank = ps.tile([P, D], F32, name="s_bank%d" % j, tag="bank%d" % (4 + j))
@@ -142,79 +144,77 @@ def tile_attend_glin_v_pl_kernel(tc, kT, cd, ce, do, qT, ts, offs, out_0, out_1,
                 start=True,
                 stop=True,
             )
-            s_cd = sb.tile([P, LANES, P], F32, name="s_cd%d" % j, tag="s_cd%d" % j, align_bytes=64)
+            s_cd = s_cd_rows[j].rearrange("p (g m) -> p g m", g=LANES)
             nc.scalar.activation(
-                out=s_cd[:], in_=s_bank[:].rearrange("p (m g) -> p g m", g=LANES), func=COPY, scale=cd_col[:, j : j + 1]
+                out=s_cd, in_=s_bank[:].rearrange("p (m g) -> p g m", g=LANES), func=COPY, scale=cd_col[:, j : j + 1]
             )
             for g in range(LANES):
                 nc.tensor.transpose(turned[g][:, j, :], s_cd[:, g, :], ident[:])
 
         k_pair = shared[:, 5 * D // 2 : 9 * D // 2].rearrange("p (b c) -> p b c", b=2)
-        s_late = sb.tile([P, 2 * D], BF16, name="s_late", tag="window2", align_bytes=64)
-        s_il = [shared[:, 7 * D // 2 : 11 * D // 2], s_late[:]]
+        s_il = [shared[:, 13 * D // 2 : 17 * D // 2], shared[:, 4 * D : 6 * D]]
+        k_late = shared[:, 11 * D // 2 : 15 * D // 2].rearrange("p (b c) -> p b c", b=2)
         for b in range(2):
             nc.vector.tensor_copy(out=k_pair[:, b, :], in_=k_raw[b][:].indirect(offsets[:]))
 
-        k_il = sb.tile([P, SLOTS, 2, 2], BF16, name="k_il", tag="keys_then_scales", align_bytes=64)
-        nc.vector.tensor_copy(out=k_il[:, :, 0, :], in_=k_pair.rearrange("p b c -> p c b"))
-        nc.vector.tensor_copy(out=k_pair[:, 0, :], in_=k_raw[2][:].indirect(offsets[:]))
+        s_pairs = []
 
-        s_pairs = [sb.tile([P, 2 * P, 2], BF16, name="s_pairs%d" % g) for g in range(LANES)]
-
-        def round_s(g):
-            nc.scalar.activation(
-                out=s_pairs[g][:].rearrange("m (u p) b -> m u p b", u=2),
-                in_=turned[g][:].rearrange("m (u b) p -> m u p b", u=2),
-                func=COPY,
-                scale=ce_col[:, g : g + 1],
-            )
+        def round_s(g, tag):
+            s_pairs.append(sb.tile([P, 2 * P, 2], BF16, name="s_pairs%d" % g, tag=tag))
+            rounded = s_pairs[g][:].rearrange("m (u p) b -> m u p b", u=2)
+            sums = turned[g][:].rearrange("m (u b) p -> m u p b", u=2)
+            nc.scalar.activation(out=rounded, in_=sums, func=COPY, scale=ce_col[:, g : g + 1])
 
         def turn_s_back(h):
             bank = ps.tile([P, 4, P], F32, name="s_words%d" % h, tag="bank%d" % (4 + h))
             words = [s_pairs[2 * h + i][:].rearrange("m w b -> m (w b)").bitcast(F32) for i in range(2)]
             turn_words([words[block // 2][:, P * (block % 2) : P * (block % 2 + 1)] for block in range(4)], bank)
-            weave_words(s_il[h], bank)
+            return bank
 
+        k_il = sb.tile([P, SLOTS, 2, 2], BF16, name="k_il", tag="window2", align_bytes=64)
+        nc.vector.tensor_copy(out=k_il[:, :, 0, :], in_=k_pair.rearrange("p b c -> p c b"))
         for g in range(3):
-            round_s(g)
-        turn_s_back(0)
-        round_s(3)
-        turn_s_back(1)
+            round_s(g, "s_pairs%d" % g)
+        nc.vector.tensor_copy(out=k_late[:, 0, :], in_=k_raw[2][:].indirect(offsets[:]))
+        weave_words(s_il[0], turn_s_back(0))
+        round_s(3, "s_pairs1")
+        late_bank = turn_s_back(1)
         s_codes = sb.tile([P, D], U32, name="s_codes", align_bytes=64)
         s_first = sb.tile([P, D // 2], U8, name="s_first", align_bytes=64)
         quantise(s_codes[:, halves[0]], s_first[:], E5M2, s_il[0])
 
         parts = [slice(P * i, P * (i + 1)) for i in range(4)]
         for c in parts:
-            nc.vector.tensor_copy(out=k_pair[:, 1, c], in_=k_raw[3][:].indirect(offsets[:, c.start // 16 : c.stop // 16]))
+            nc.vector.tensor_copy(out=k_late[:, 1, c], in_=k_raw[3][:].indirect(offsets[:, c.start // 16 : c.stop // 16]))
 
         def weave_keys(copy, c):
-            copy(out=k_il[:, c, 1, :], in_=k_pair[:, :, c].rearrange("p b c -> p c b"))
+            copy(out=k_il[:, c, 1, :], in_=k_late[:, :, c].rearrange("p b c -> p c b"))
 
         def quantise_keys(c):
             quantise(k_codes[:, c], k_scales[:, c], E4M3, k_il[:, c].rearrange("p c u b -> p (c u b)"))
 
-        for i in (0, 1, 3):
+        for i in (0, 1):
             weave_keys(nc.scalar.copy, parts[i])
+        weave_words(s_il[1], late_bank)
+        weave_keys(nc.scalar.copy, parts[3])
         quantise_keys(halves[0])
         weave_keys(nc.vector.tensor_copy, parts[2])
-        quantise_keys(halves[1])
-        s_rest = sb.tile([P, D // 2], U8, name="s_rest", tag="keys_then_scales", align_bytes=64)
+        s_rest = sb.tile([P, D // 2], U8, name="s_rest", align_bytes=64)
         quantise(s_codes[:, halves[1]], s_rest[:], E5M2, s_il[1])
+        quantise_keys(halves[1])
         zeroed.append(sb.tile([P, T], F32, name="window2", tag="window2", align_bytes=64))
         nc.gpsimd.memset(zeroed[2][:].bitcast(I32), 0)
-        s_scales = [tile[:, P * g : P * (g + 1)] for tile in (s_first, s_rest) for g in range(2)]
 
         out_rows = out_0.rearrange("(p g) c -> p g c", g=LANES)
         y_pairs = sb.tile([P, 2, T, 2], BF16, name="y_pairs")
         dv0 = [sb.tile([P, SLOTS], F32, name="dv0_%d" % g) for g in range(LANES)]
 
-        def dv_product(g, first, bank_tag, c):
+        def dv_product(g, s_scales, first, bank_tag, c):
             dv_bank = ps.tile([P, SLOTS], F32, name="dv_bank", tag=bank_tag)
             nc.tensor.matmul_mx(
                 out=dv_bank[:],
                 lhsT=s_codes[:, P * g : P * (g + 1)].bitcast(E5M2),
-                lhsT_scale=s_scales[g],
+                lhsT_scale=s_scales[:, P * (g % 2) : P * (g % 2 + 1)],
                 rhs=codes[:, first : first + SLOTS].bitcast(E4M3),
                 rhs_scale=scales[:, first : first + SLOTS],
                 start=True,
@@ -223,15 +223,20 @@ def tile_attend_glin_v_pl_kernel(tc, kT, cd, ce, do, qT, ts, offs, out_0, out_1,
             shift = D - first
             nc.scalar.copy(out=dv0[g][:, c], in_=dv_bank[:, c.start + shift : c.stop + shift])
 
-        dv_product(0, D // 2, "bank6", halves[0])
-        dv_product(0, D, "bank0", halves[1])
-        for g in range(1, LANES):
-            dv_product(g, D, "bank%d" % g, slice(0, SLOTS))
+        def scatter(window, g, c):
+            listed = offsets[:, c.start // 16 : c.stop // 16]
+            nc.vector.tensor_tensor(window[:].indirect(listed), dv0[g][:, c], ts_listed[:, c], MULT)
+
+        whole = slice(0, SLOTS)
+        dv_product(0, s_first, D // 2, "bank6", halves[0])
+        dv_product(0, s_first, D, "bank0", halves[1])
+        dv_product(1, s_first, D, "bank1", whole)
+        for g in range(2, LANES):
+            dv_product(g, s_rest, D, "bank%d" % g, whole)
+        scatter(zeroed[0], 0, halves[0])
         window = [zeroed[g % WINDOWS] for g in range(LANES)]
         for g in range(LANES):
-            for c in halves if g == 0 else [slice(0, SLOTS)]:
-                listed = offsets[:, c.start // 16 : c.stop // 16]
-                nc.vector.tensor_tensor(window[g][:].indirect(listed), dv0[g][:, c], ts_listed[:, c], MULT)
+            scatter(window[g], g, halves[1] if g == 0 else whole)
             nc.sync.dma_start(out=out_rows[:, g, :], in_=window[g][:])
             if g < 2:
                 nc.scalar.copy(out=y_pairs[:, 0, :, g], in_=window[g][:])

@@ -23,6 +23,7 @@ PIECE = 256
 PIECES = (0, 256, 512, 768, 1024, 1280, 1536, 1792, 1920, 2048)
 STORES = (0, 512, 1024, 1536, 1792, 2048)
 WINDOWS = 3
+CLEARED = 1280
 TIE = 16
 
 FLOPS = 2 * 2 * 512 * 512 * 512
@@ -69,9 +70,12 @@ def tile_attend_glin_v_pl_kernel(tc, kT, cd, ce, do, qT, ts, offs, out_0, out_1,
             pattern=[[-1, P]],
             channel_multiplier=1,
         )
-        zeroed = [sb.tile([P, T], F32, name="window%d" % w, tag="window%d" % w) for w in range(2)]
-        nc.vector.memset(zeroed[0][:].bitcast(I32), 0)
+        zeroed = [sb.tile([P, T], F32, name="window%d" % w, tag="window%d" % w) for w in range(WINDOWS)]
         nc.gpsimd.memset(zeroed[1][:].bitcast(I32), 0)
+        nc.gpsimd.memset(zeroed[2][:, CLEARED:T].bitcast(I32), 0)
+        for tile, width in ((zeroed[0], T), (zeroed[2], CLEARED)):
+            for c in (slice(0, width - 1), slice(width - 1, width)):
+                nc.vector.memset(tile[:, c].bitcast(I32), 0)
 
         def turn_words(words, bank):
             for block, columns in enumerate(words):
@@ -171,7 +175,7 @@ def tile_attend_glin_v_pl_kernel(tc, kT, cd, ce, do, qT, ts, offs, out_0, out_1,
             turn_words([words[block // 2][:, P * (block % 2) : P * (block % 2 + 1)] for block in range(4)], bank)
             return bank
 
-        k_il = sb.tile([P, SLOTS, 2, 2], BF16, name="k_il", tag="window2", align_bytes=64)
+        k_il = sb.tile([P, SLOTS, 2, 2], BF16, name="k_il", align_bytes=64)
         nc.vector.tensor_copy(out=k_il[:, :, 0, :], in_=k_pair.rearrange("p b c -> p c b"))
         for g in range(3):
             round_s(g, "s_pairs%d" % g)
@@ -202,8 +206,6 @@ def tile_attend_glin_v_pl_kernel(tc, kT, cd, ce, do, qT, ts, offs, out_0, out_1,
         s_rest = sb.tile([P, D // 2], U8, name="s_rest", align_bytes=64)
         quantise(s_codes[:, halves[1]], s_rest[:], E5M2, s_il[1])
         quantise_keys(halves[1])
-        zeroed.append(sb.tile([P, T], F32, name="window2", tag="window2", align_bytes=64))
-        nc.gpsimd.memset(zeroed[2][:].bitcast(I32), 0)
 
         out_rows = out_0.rearrange("(p g) c -> p g c", g=LANES)
         y_pairs = sb.tile([P, 2, T, 2], BF16, name="y_pairs")

@@ -1,6 +1,7 @@
 from contextlib import ExitStack
 
 import concourse.mybir as mybir
+from concourse.masks import make_identity
 
 F32 = mybir.dt.float32
 BF16 = mybir.dt.bfloat16
@@ -23,8 +24,8 @@ PIECE = 256
 PIECES = (0, 256, 512, 768, 1024, 1280, 1536, 1792, 1920, 2048)
 STORES = (0, 512, 1024, 1536, 1792, 2048)
 WINDOWS = 3
-CLEARED = 1280
-TIE = 16
+CLEARED = 896
+RELAY = 128
 
 FLOPS = 2 * 2 * 512 * 512 * 512
 BYTES = 4 * (512 * 2048 + 512 + 512 + 2 * 512 * 512 + 2048) + 2 * 128 * 32 + 4 * 512 * 2048 + 512 * 2048 + 16 * 2048
@@ -59,20 +60,11 @@ def tile_attend_glin_v_pl_kernel(tc, kT, cd, ce, do, qT, ts, offs, out_0, out_1,
             nc.sync.dma_start(out=k_raw[t][:], in_=k_rows[:, t, :])
 
         ident = sb.tile([P, P], F32, name="ident")
-        zero_block = sb.tile([P, P], F32, name="zero_block", tag="window1")
-        nc.gpsimd.memset(zero_block[:], 0.0)
-        nc.gpsimd.affine_select(
-            out=ident[:],
-            in_=zero_block[:],
-            compare_op=mybir.AluOpType.not_equal,
-            fill=1.0,
-            base=0,
-            pattern=[[-1, P]],
-            channel_multiplier=1,
-        )
-        zeroed = [sb.tile([P, T], F32, name="window%d" % w, tag="window%d" % w) for w in range(WINDOWS)]
-        nc.gpsimd.memset(zeroed[1][:].bitcast(I32), 0)
+        nc.vector.memset(ident[:], 0.0)
+        make_identity(nc, ident[:], nomemset=True)
+        zeroed = [sb.tile([P, T], F32, name="window%d" % w) for w in range(WINDOWS)]
         nc.gpsimd.memset(zeroed[2][:, CLEARED:T].bitcast(I32), 0)
+        nc.gpsimd.memset(zeroed[1][:].bitcast(I32), 0)
         for tile, width in ((zeroed[0], T), (zeroed[2], CLEARED)):
             for c in (slice(0, width - 1), slice(width - 1, width)):
                 nc.vector.memset(tile[:, c].bitcast(I32), 0)
@@ -243,9 +235,12 @@ def tile_attend_glin_v_pl_kernel(tc, kT, cd, ce, do, qT, ts, offs, out_0, out_1,
             if g < 2:
                 nc.scalar.copy(out=y_pairs[:, 0, :, g], in_=window[g][:])
             if g == 2:
-                tie = slice(PIECE - TIE // 2, PIECE + TIE // 2)
-                nc.scalar.copy(out=y_pairs[:, 1, PIECE:SPLIT, 0], in_=window[g][:, PIECE:SPLIT])
-                nc.scalar.copy(out=y_pairs[:, 1, tie, :], in_=window[g][:, tie].unsqueeze(2).to_broadcast([P, TIE, 2]))
+                first = SPLIT - 4 * RELAY
+                nc.scalar.copy(out=y_pairs[:, 1, 0:first, 0], in_=window[g][:, 0:first])
+                nc.scalar.copy(
+                    out=y_pairs[:, 1, first : first + 2 * RELAY, :],
+                    in_=window[g][:, first:SPLIT].rearrange("p (b c) -> p c b", b=2),
+                )
                 nc.scalar.copy(out=y_pairs[:, 1, SPLIT:T, 0], in_=window[g][:, SPLIT:T])
 
         y_words = y_pairs[:].rearrange("p u c b -> p (u c b)").bitcast(F32).rearrange("p (u c) -> p c u", u=2)
@@ -260,8 +255,11 @@ def tile_attend_glin_v_pl_kernel(tc, kT, cd, ce, do, qT, ts, offs, out_0, out_1,
         scalar_cuts = (SPLIT,) + tuple(b for b in PIECES if b > SPLIT)
         for a, b in zip(scalar_cuts, scalar_cuts[1:]):
             nc.scalar.copy(out=il_words[:, a:b, :], in_=y_words[:, a:b, :])
-        nc.vector.tensor_copy(out=y_pairs[:, 1, 0:PIECE, 0], in_=window[2][:, 0:PIECE])
-        for c in (slice(0, PIECE), slice(PIECE, SPLIT)):
+        for a in (SPLIT - 4 * RELAY, SPLIT - 3 * RELAY):
+            nc.vector.tensor_copy(
+                out=y_pairs[:, 1, a + 2 * RELAY : a + 3 * RELAY, 0], in_=y_pairs[:, 1, a : a + RELAY, 1]
+            )
+        for c in (slice(0, SPLIT - 3 * RELAY), slice(SPLIT - 3 * RELAY, SPLIT)):
             nc.vector.tensor_copy(out=y_pairs[:, 1, c, 1], in_=window[3][:, c])
 
         def weave_y(a, b):

@@ -24,7 +24,7 @@ PIECE = 256
 PIECES = (0, 256, 512, 768, 1024, 1280, 1536, 1792, 1920, 2048)
 STORES = (0, 512, 1024, 1536, 1792, 2048)
 WINDOWS = 3
-CLEARED = 896
+CLEARED = 1024
 RELAY = 128
 
 FLOPS = 2 * 2 * 512 * 512 * 512
@@ -45,11 +45,11 @@ def tile_attend_glin_v_pl_kernel(tc, kT, cd, ce, do, qT, ts, offs, out_0, out_1,
         q_rows = qT.rearrange("(m j) r -> m j r", j=LANES)
         q_raw = [sb.tile([P, D], F32, name="q_raw%d" % j) for j in range(LANES)]
         do_rows = do.rearrange("(p t) e -> p t e", t=LANES)
-        do_raw = [sb.tile([P, LANES, D // 2], F32, name="do_raw%d" % h) for h in range(2)]
+        do_raw = [sb.tile([P, 2, D], F32, name="do_raw%d" % u) for u in range(2)]
         ts_col = sb.tile([P, T // P], F32, name="ts_col", tag="ts_then_q")
         nc.sync.dma_start(out=ts_col[:], in_=ts[0:1, :].rearrange("o (n g) -> n (o g)", n=P))
-        for h in range(2):
-            nc.sync.dma_start(out=do_raw[h][:], in_=do_rows[:, :, halves[h]])
+        for u in range(2):
+            nc.sync.dma_start(out=do_raw[u][:], in_=do_rows[:, 2 * u : 2 * u + 2, :])
         for j in range(LANES):
             nc.sync.dma_start(out=q_raw[j][:], in_=q_rows[:, j, :])
         offsets = sb.tile([P, SLOTS // 16], U16, name="offsets")
@@ -92,27 +92,25 @@ def tile_attend_glin_v_pl_kernel(tc, kT, cd, ce, do, qT, ts, offs, out_0, out_1,
 
         do_codes = sb.tile([P, D], U32, name="do_codes", align_bytes=64)
         do_scales = sb.tile([P, D], U8, name="do_scales", align_bytes=64)
-        do_il = [sb.tile([P, D // 2, LANES], BF16, name="do_il%d" % h, tag="do_il%d" % h, align_bytes=64) for h in range(2)]
+        do_il = [sb.tile([P, D // 2, 2, 2], BF16, name="do_il%d" % h, tag="do_il%d" % h, align_bytes=64) for h in range(2)]
+        for u in range(2):
+            for h in range(2):
+                nc.vector.tensor_copy(out=do_il[h][:, :, u, :], in_=do_raw[u][:, :, halves[h]].rearrange("p b c -> p c b"))
         for h in range(2):
-            nc.vector.tensor_copy(
-                out=do_il[h][:].rearrange("p (c i) t -> p c t i", i=4),
-                in_=do_raw[h][:].rearrange("p t (c i) -> p c t i", i=4),
-            )
-        for h in range(2):
-            quantise(do_codes[:, halves[h]], do_scales[:, halves[h]], E5M2, do_il[h][:].rearrange("p c t -> p (c t)"))
+            quantise(do_codes[:, halves[h]], do_scales[:, halves[h]], E5M2, do_il[h][:].rearrange("p c u b -> p (c u b)"))
 
         codes = sb.tile([P, D + SLOTS], U32, name="codes", align_bytes=64)
         scales = sb.tile([P, D + SLOTS], U8, name="scales", align_bytes=64)
         q_codes, k_codes = codes[:, 0:D], codes[:, D : D + SLOTS]
         q_scales, k_scales = scales[:, 0:D], scales[:, D : D + SLOTS]
-        q_first = sb.tile([P, D], BF16, name="q_first", tag="ts_then_q")
-        q_later = sb.tile([P, 3 * D], BF16, name="q_later", tag="do_il0", align_bytes=64)
-        q_pairs = [q_first[:]] + [q_later[:, D * j : D * (j + 1)] for j in range(3)]
-        shared = sb.tile([P, 17 * D // 2], BF16, name="shared", align_bytes=64)
+        q_first = sb.tile([P, 2 * D], BF16, name="q_first", tag="ts_then_q")
+        q_later = sb.tile([P, 2 * D], BF16, name="q_later", tag="do_il0", align_bytes=64)
+        q_pairs = [tile[:, D * i : D * (i + 1)] for tile in (q_first, q_later) for i in range(2)]
+        shared = sb.tile([P, 15 * D // 2], BF16, name="shared", align_bytes=64)
         q_il = shared[:, 0 : LANES * D]
         ts_listed = shared[:, 0 : 2 * D].bitcast(F32)
         for j in range(LANES):
-            round_q = nc.scalar.copy if j == 0 else nc.vector.tensor_copy
+            round_q = nc.scalar.copy if j < 2 else nc.vector.tensor_copy
             round_q(
                 out=q_pairs[j].rearrange("m (u p b) -> m u p b", u=2, b=2),
                 in_=q_raw[j][:].rearrange("m (p u b) -> m u p b", u=2, b=2),
@@ -148,7 +146,7 @@ def tile_attend_glin_v_pl_kernel(tc, kT, cd, ce, do, qT, ts, offs, out_0, out_1,
                 nc.tensor.transpose(turned[g][:, j, :], s_cd[:, g, :], ident[:])
 
         k_pair = shared[:, 5 * D // 2 : 9 * D // 2].rearrange("p (b c) -> p b c", b=2)
-        s_il = [shared[:, 13 * D // 2 : 17 * D // 2], shared[:, 4 * D : 6 * D]]
+        s_il = [shared[:, 13 * D // 2 : 15 * D // 2]] + [shared[:, (3 + i) * D : (4 + i) * D] for i in range(3)]
         k_late = shared[:, 11 * D // 2 : 15 * D // 2].rearrange("p (b c) -> p b c", b=2)
         for b in range(2):
             nc.vector.tensor_copy(out=k_pair[:, b, :], in_=k_raw[b][:].indirect(offsets[:]))
@@ -161,23 +159,25 @@ def tile_attend_glin_v_pl_kernel(tc, kT, cd, ce, do, qT, ts, offs, out_0, out_1,
             sums = turned[g][:].rearrange("m (u b) p -> m u p b", u=2)
             nc.scalar.activation(out=rounded, in_=sums, func=COPY, scale=ce_col[:, g : g + 1])
 
-        def turn_s_back(h):
-            bank = ps.tile([P, 4, P], F32, name="s_words%d" % h, tag="bank%d" % (4 + h))
-            words = [s_pairs[2 * h + i][:].rearrange("m w b -> m (w b)").bitcast(F32) for i in range(2)]
-            turn_words([words[block // 2][:, P * (block % 2) : P * (block % 2 + 1)] for block in range(4)], bank)
+        def turn_s_back(g):
+            bank = ps.tile([P, 2, P], F32, name="s_words%d" % g, tag="bank%d" % (4 + g))
+            words = s_pairs[g][:].rearrange("m w b -> m (w b)").bitcast(F32)
+            turn_words([words[:, P * u : P * (u + 1)] for u in range(2)], bank)
             return bank
 
         k_il = sb.tile([P, SLOTS, 2, 2], BF16, name="k_il", align_bytes=64)
         nc.vector.tensor_copy(out=k_il[:, :, 0, :], in_=k_pair.rearrange("p b c -> p c b"))
-        for g in range(3):
+        for g in range(2):
             round_s(g, "s_pairs%d" % g)
         nc.vector.tensor_copy(out=k_late[:, 0, :], in_=k_raw[2][:].indirect(offsets[:]))
-        weave_words(s_il[0], turn_s_back(0))
-        round_s(3, "s_pairs1")
-        late_bank = turn_s_back(1)
+        banks = [turn_s_back(g) for g in range(2)]
+        weave_words(s_il[0], banks[0])
+        for g in (2, 3):
+            round_s(g, "s_pairs0" if g == 2 else "s_pairs3")
+        banks.extend(turn_s_back(g) for g in (2, 3))
         s_codes = sb.tile([P, D], U32, name="s_codes", align_bytes=64)
-        s_first = sb.tile([P, D // 2], U8, name="s_first", align_bytes=64)
-        quantise(s_codes[:, halves[0]], s_first[:], E5M2, s_il[0])
+        s_scales = sb.tile([P, D], U8, name="s_scales", align_bytes=64)
+        quantise(s_codes[:, 0:P], s_scales[:, 0:P], E5M2, s_il[0])
 
         parts = [slice(P * i, P * (i + 1)) for i in range(4)]
         for c in parts:
@@ -191,24 +191,25 @@ def tile_attend_glin_v_pl_kernel(tc, kT, cd, ce, do, qT, ts, offs, out_0, out_1,
 
         for i in (0, 1):
             weave_keys(nc.scalar.copy, parts[i])
-        weave_words(s_il[1], late_bank)
+        for g in (3, 2, 1):
+            weave_words(s_il[g], banks[g])
         weave_keys(nc.scalar.copy, parts[3])
         quantise_keys(halves[0])
         weave_keys(nc.vector.tensor_copy, parts[2])
-        s_rest = sb.tile([P, D // 2], U8, name="s_rest", align_bytes=64)
-        quantise(s_codes[:, halves[1]], s_rest[:], E5M2, s_il[1])
+        quantise(s_codes[:, 2 * P : D], s_scales[:, 2 * P : D], E5M2, shared[:, 4 * D : 6 * D])
+        quantise(s_codes[:, P : 2 * P], s_scales[:, P : 2 * P], E5M2, s_il[1])
         quantise_keys(halves[1])
 
         out_rows = out_0.rearrange("(p g) c -> p g c", g=LANES)
         y_pairs = sb.tile([P, 2, T, 2], BF16, name="y_pairs")
         dv0 = [sb.tile([P, SLOTS], F32, name="dv0_%d" % g) for g in range(LANES)]
 
-        def dv_product(g, s_scales, first, bank_tag, c):
+        def dv_product(g, first, bank_tag, c):
             dv_bank = ps.tile([P, SLOTS], F32, name="dv_bank", tag=bank_tag)
             nc.tensor.matmul_mx(
                 out=dv_bank[:],
                 lhsT=s_codes[:, P * g : P * (g + 1)].bitcast(E5M2),
-                lhsT_scale=s_scales[:, P * (g % 2) : P * (g % 2 + 1)],
+                lhsT_scale=s_scales[:, P * g : P * (g + 1)],
                 rhs=codes[:, first : first + SLOTS].bitcast(E4M3),
                 rhs_scale=scales[:, first : first + SLOTS],
                 start=True,
@@ -222,11 +223,10 @@ def tile_attend_glin_v_pl_kernel(tc, kT, cd, ce, do, qT, ts, offs, out_0, out_1,
             nc.vector.tensor_tensor(window[:].indirect(listed), dv0[g][:, c], ts_listed[:, c], MULT)
 
         whole = slice(0, SLOTS)
-        dv_product(0, s_first, D // 2, "bank6", halves[0])
-        dv_product(0, s_first, D, "bank0", halves[1])
-        dv_product(1, s_first, D, "bank1", whole)
-        for g in range(2, LANES):
-            dv_product(g, s_rest, D, "bank%d" % g, whole)
+        dv_product(0, D // 2, "bank4", halves[0])
+        dv_product(0, D, "bank0", halves[1])
+        for g in range(1, LANES):
+            dv_product(g, D, "bank%d" % g, whole)
         scatter(zeroed[0], 0, halves[0])
         window = [zeroed[g % WINDOWS] for g in range(LANES)]
         for g in range(LANES):

@@ -22,10 +22,7 @@ SLOTS = 512
 SPLIT = 896
 PIECE = 256
 PIECES = (0, 256, 512, 768, 1024, 1280, 1536, 1792, 1920, 2048)
-STORES = (0, 512, 1024, 1536, 1792, 2048)
-WINDOWS = 3
-CLEARED = 1024
-RELAY = 128
+STORES = (0, 1024, 1792, 2048)
 
 FLOPS = 2 * 2 * 512 * 512 * 512
 BYTES = 4 * (512 * 2048 + 512 + 512 + 2 * 512 * 512 + 2048) + 2 * 128 * 32 + 4 * 512 * 2048 + 512 * 2048 + 16 * 2048
@@ -37,211 +34,213 @@ def tile_attend_glin_v_pl_kernel(tc, kT, cd, ce, do, qT, ts, offs, out_0, out_1,
         sb = ctx.enter_context(tc.tile_pool(name="sb", bufs=1))
         ps = ctx.enter_context(tc.psum_pool(name="ps", bufs=1))
         halves = [slice(h * D // 2, (h + 1) * D // 2) for h in range(2)]
+        quarters = [slice(P * i, P * (i + 1)) for i in range(4)]
 
-        cd_col = sb.tile([P, LANES], F32, name="cd_col")
+        cd_col = sb.tile([P, LANES], F32, name="cd_col", tag="cd_do_window", align_bytes=64)
         ce_col = sb.tile([P, LANES], F32, name="ce_col")
-        nc.scalar.dma_start(out=cd_col[:], in_=cd.rearrange("(p j) o -> p (j o)", j=LANES))
-        nc.scalar.dma_start(out=ce_col[:], in_=ce[0:1, :].rearrange("o (m g) -> m (o g)", g=LANES))
+        nc.sync.dma_start(out=ce_col[:], in_=ce[0:1, :].rearrange("o (m g) -> m (o g)", g=LANES))
+        nc.sync.dma_start(out=cd_col[:], in_=cd.rearrange("(p j) o -> p (j o)", j=LANES))
+        ts_col = sb.tile([P, T // P], F32, name="ts_col")
+        nc.scalar.dma_start(out=ts_col[:], in_=ts[0:1, :].rearrange("o (n g) -> n (o g)", n=P))
         q_rows = qT.rearrange("(m j) r -> m j r", j=LANES)
-        q_raw = [sb.tile([P, D], F32, name="q_raw%d" % j) for j in range(LANES)]
-        do_rows = do.rearrange("(p t) e -> p t e", t=LANES)
-        do_raw = [sb.tile([P, 2, D], F32, name="do_raw%d" % u) for u in range(2)]
-        ts_col = sb.tile([P, T // P], F32, name="ts_col", tag="ts_then_q")
-        nc.sync.dma_start(out=ts_col[:], in_=ts[0:1, :].rearrange("o (n g) -> n (o g)", n=P))
-        for u in range(2):
-            nc.sync.dma_start(out=do_raw[u][:], in_=do_rows[:, 2 * u : 2 * u + 2, :])
-        for j in range(LANES):
-            nc.sync.dma_start(out=q_raw[j][:], in_=q_rows[:, j, :])
+        q_raw = [sb.tile([P, 2, D], F32, name="q_raw%d" % h, tag="q_raw%d" % h) for h in range(2)]
+        for h in range(2):
+            nc.sync.dma_start(out=q_raw[h][:], in_=q_rows[:, 2 * h : 2 * h + 2, :])
         offsets = sb.tile([P, SLOTS // 16], U16, name="offsets")
         nc.sync.dma_start(offsets[:], offs)
+        do_raw = sb.tile([P, LANES, D], F32, name="do_raw")
+        nc.sync.dma_start(out=do_raw[:], in_=do.rearrange("(p t) e -> p t e", t=LANES))
         k_rows = kT.rearrange("(p t) c -> p t c", t=LANES)
-        k_raw = [sb.tile([P, T], F32, name="k_raw%d" % t) for t in range(LANES)]
+        k_raw = [sb.tile([P, T], F32, name="k_raw%d" % t, tag="k_raw%d" % t) for t in range(LANES)]
         for t in range(LANES):
             nc.sync.dma_start(out=k_raw[t][:], in_=k_rows[:, t, :])
 
+        def listed(c):
+            return offsets[:, c.start // 16 : c.stop // 16]
+
         ident = sb.tile([P, P], F32, name="ident")
-        nc.vector.memset(ident[:], 0.0)
+        window = [sb.tile([P, T], F32, name="window%d" % g) for g in range(LANES - 1)]
+        nc.gpsimd.memset(ident[:], 0.0)
+        nc.gpsimd.memset(window[1][:, 0:PIECE].bitcast(I32), 0)
         make_identity(nc, ident[:], nomemset=True)
-        zeroed = [sb.tile([P, T], F32, name="window%d" % w) for w in range(WINDOWS)]
-        nc.gpsimd.memset(zeroed[2][:, CLEARED:T].bitcast(I32), 0)
-        nc.gpsimd.memset(zeroed[1][:].bitcast(I32), 0)
-        for tile, width in ((zeroed[0], T), (zeroed[2], CLEARED)):
-            for c in (slice(0, width - 1), slice(width - 1, width)):
-                nc.vector.memset(tile[:, c].bitcast(I32), 0)
+        nc.gpsimd.memset(window[1][:, PIECE:T].bitcast(I32), 0)
+        nc.gpsimd.memset(window[2][:].bitcast(I32), 0)
+        for c in (slice(0, T - 1), slice(T - 1, T)):
+            nc.vector.memset(window[0][:, c].bitcast(I32), 0)
 
-        def turn_words(words, bank):
-            for block, columns in enumerate(words):
-                nc.tensor.transpose(bank[:, block, :], columns, ident[:])
+        def turn(columns, bank):
+            for block, source in enumerate(columns):
+                nc.tensor.transpose(bank[:, block, :], source, ident[:])
 
-        def weave_words(woven, bank):
-            nc.scalar.copy(
-                out=woven.bitcast(F32).rearrange("p (j m u) -> p j m u", m=P, u=2),
-                in_=bank[:].rearrange("p (j u) m -> p j m u", u=2),
-            )
+        def spread(column):
+            return column.to_broadcast([P, P])
 
         def quantise(codes, scales, fmt, woven):
             nc.vector.quantize_mx(out=codes.bitcast(fmt), scales=scales, in_=woven)
 
-        ts_raw = sb.tile([P, T], F32, name="ts_raw")
+        def product(bank, stationary, moving, formats):
+            nc.tensor.matmul_mx(
+                out=bank,
+                lhsT=stationary[0].bitcast(formats[0]),
+                lhsT_scale=stationary[1],
+                rhs=moving[0].bitcast(formats[1]),
+                rhs_scale=moving[1],
+                start=True,
+                stop=True,
+            )
+
+        ce_bank = ps.tile([P, LANES, P], F32, name="ce_bank", tag="bank2")
+        turn([spread(ce_col[:, g : g + 1]) for g in range(LANES)], ce_bank)
+        table = sb.tile([P, LANES, P, LANES], F32, name="table")
+        nc.vector.tensor_tensor(
+            table[:].rearrange("p g m j -> p (g m) j"),
+            ce_bank[:].rearrange("p g m -> p (g m)").unsqueeze(2).to_broadcast([P, D, LANES]),
+            cd_col[:].unsqueeze(1).to_broadcast([P, D, LANES]),
+            MULT,
+        )
+
+        q_codes = sb.tile([P, D], U32, name="q_codes", align_bytes=64)
+        q_scales = sb.tile([P, D], U8, name="q_scales", align_bytes=64)
+        q_il = [sb.tile([P, 2 * D], BF16, name="q_il%d" % h, tag="q_il%d" % h, align_bytes=64) for h in range(2)]
+        for h in range(2):
+            q_pairs = sb.tile([P, 2 * D], BF16, name="q_pairs%d" % h, tag="q_pairs%d" % h)
+            nc.scalar.copy(
+                out=q_pairs[:].rearrange("m (j u p b) -> m j u p b", j=2, u=2, b=2),
+                in_=q_raw[h][:].rearrange("m j (p u b) -> m j u p b", u=2, b=2),
+            )
+            bank = ps.tile([P, 4, P], F32, name="q_bank%d" % h, tag="bank%d" % h)
+            words = q_pairs[:].bitcast(F32)
+            turn([words[:, c] for c in quarters], bank)
+            nc.scalar.copy(
+                out=q_il[h][:].bitcast(F32).rearrange("p (j m u) -> p j m u", m=P, u=2),
+                in_=bank[:].rearrange("p (j u) m -> p j m u", u=2),
+            )
+        for h in range(2):
+            quantise(q_codes[:, halves[h]], q_scales[:, halves[h]], E4M3, q_il[h][:])
+
+        ts_raw = sb.tile([P, T], F32, name="ts_raw", tag="q_pairs1")
         for i in range(4):
             bank = ps.tile([P, 4, P], F32, name="ts_bank%d" % i, tag="bank%d" % (4 + i))
-            turn_words([ts_col[:, 4 * i + g : 4 * i + g + 1].to_broadcast([P, P]) for g in range(4)], bank)
+            turn([spread(ts_col[:, 4 * i + g : 4 * i + g + 1]) for g in range(4)], bank)
             nc.scalar.copy(
                 out=ts_raw[:].rearrange("p (n i g) -> p i n g", i=4, g=4)[:, i], in_=bank[:].rearrange("p g n -> p n g")
             )
 
         do_codes = sb.tile([P, D], U32, name="do_codes", align_bytes=64)
         do_scales = sb.tile([P, D], U8, name="do_scales", align_bytes=64)
-        do_il = [sb.tile([P, D // 2, 2, 2], BF16, name="do_il%d" % h, tag="do_il%d" % h, align_bytes=64) for h in range(2)]
-        for u in range(2):
-            for h in range(2):
-                nc.vector.tensor_copy(out=do_il[h][:, :, u, :], in_=do_raw[u][:, :, halves[h]].rearrange("p b c -> p c b"))
+        do_il = sb.tile([P, D * LANES], BF16, name="do_il", tag="cd_do_window", align_bytes=64)
+        do_halves = [do_il[:, 2 * D * h : 2 * D * (h + 1)] for h in range(2)]
         for h in range(2):
-            quantise(do_codes[:, halves[h]], do_scales[:, halves[h]], E5M2, do_il[h][:].rearrange("p c u b -> p (c u b)"))
-
-        codes = sb.tile([P, D + SLOTS], U32, name="codes", align_bytes=64)
-        scales = sb.tile([P, D + SLOTS], U8, name="scales", align_bytes=64)
-        q_codes, k_codes = codes[:, 0:D], codes[:, D : D + SLOTS]
-        q_scales, k_scales = scales[:, 0:D], scales[:, D : D + SLOTS]
-        q_first = sb.tile([P, 2 * D], BF16, name="q_first", tag="ts_then_q")
-        q_later = sb.tile([P, 2 * D], BF16, name="q_later", tag="do_il0", align_bytes=64)
-        q_pairs = [tile[:, D * i : D * (i + 1)] for tile in (q_first, q_later) for i in range(2)]
-        shared = sb.tile([P, 15 * D // 2], BF16, name="shared", align_bytes=64)
-        q_il = shared[:, 0 : LANES * D]
-        ts_listed = shared[:, 0 : 2 * D].bitcast(F32)
-        for j in range(LANES):
-            round_q = nc.scalar.copy if j < 2 else nc.vector.tensor_copy
-            round_q(
-                out=q_pairs[j].rearrange("m (u p b) -> m u p b", u=2, b=2),
-                in_=q_raw[j][:].rearrange("m (p u b) -> m u p b", u=2, b=2),
+            nc.vector.tensor_copy(
+                out=do_halves[h].rearrange("p (c i t) -> p c t i", i=4, t=LANES),
+                in_=do_raw[:, :, halves[h]].rearrange("p t (c i) -> p c t i", i=4),
             )
-            bank = ps.tile([P, 2, P], F32, name="q_bank%d" % j, tag="bank%d" % j)
-            words = q_pairs[j].bitcast(F32)
-            turn_words([words[:, P * u : P * (u + 1)] for u in range(2)], bank)
-            weave_words(q_il[:, D * j : D * (j + 1)], bank)
-            columns = slice(P * j, P * (j + 1))
-            if j == LANES - 1:
-                nc.vector.tensor_copy(out=ts_listed, in_=ts_raw[:].indirect(offsets[:]))
-            quantise(q_codes[:, columns], q_scales[:, columns], E4M3, q_il[:, D * j : D * (j + 1)])
+        for h in range(2):
+            quantise(do_codes[:, halves[h]], do_scales[:, halves[h]], E5M2, do_halves[h])
+        window.append(sb.tile([P, T], F32, name="window3", tag="cd_do_window", align_bytes=64))
+        nc.gpsimd.memset(window[3][:].bitcast(I32), 0)
 
-        s_cd_rows = [sb.tile([P, D], F32, name="s_cd%d" % j)[:] for j in range(LANES - 1)]
-        s_cd_rows.append(shared[:, 9 * D // 2 : 13 * D // 2].bitcast(F32))
-        turned = [ps.tile([P, LANES, P], F32, name="turned%d" % g, tag="bank%d" % g) for g in range(LANES)]
-        for j in range(LANES):
-            s_bank = ps.tile([P, D], F32, name="s_bank%d" % j, tag="bank%d" % (4 + j))
-            nc.tensor.matmul_mx(
-                out=s_bank[:],
-                lhsT=q_codes[:, P * j : P * (j + 1)].bitcast(E4M3),
-                lhsT_scale=q_scales[:, P * j : P * (j + 1)],
-                rhs=do_codes[:].bitcast(E5M2),
-                rhs_scale=do_scales[:],
-                start=True,
-                stop=True,
+        s_il = sb.tile([P, LANES, P, LANES], BF16, name="s_il", tag="s_then_k", align_bytes=64)
+        for b in range(4):
+            bank = ps.tile([P, LANES, P], F32, name="s_bank%d" % b, tag="bank%d" % b)
+            for j in range(LANES):
+                product(
+                    bank[:, j, :],
+                    (q_codes[:, quarters[j]], q_scales[:, quarters[j]]),
+                    (do_codes[:, quarters[b]], do_scales[:, quarters[b]]),
+                    (E4M3, E5M2),
+                )
+            nc.vector.tensor_tensor(
+                s_il[:, :, 32 * b : 32 * (b + 1), :],
+                bank[:].rearrange("p j (m g) -> p g m j", g=LANES),
+                table[:, :, 32 * b : 32 * (b + 1), :],
+                MULT,
             )
-            s_cd = s_cd_rows[j].rearrange("p (g m) -> p g m", g=LANES)
-            nc.scalar.activation(
-                out=s_cd, in_=s_bank[:].rearrange("p (m g) -> p g m", g=LANES), func=COPY, scale=cd_col[:, j : j + 1]
-            )
-            for g in range(LANES):
-                nc.tensor.transpose(turned[g][:, j, :], s_cd[:, g, :], ident[:])
-
-        k_pair = shared[:, 5 * D // 2 : 9 * D // 2].rearrange("p (b c) -> p b c", b=2)
-        s_il = [shared[:, 13 * D // 2 : 15 * D // 2]] + [shared[:, (3 + i) * D : (4 + i) * D] for i in range(3)]
-        k_late = shared[:, 11 * D // 2 : 15 * D // 2].rearrange("p (b c) -> p b c", b=2)
-        for b in range(2):
-            nc.vector.tensor_copy(out=k_pair[:, b, :], in_=k_raw[b][:].indirect(offsets[:]))
-
-        s_pairs = []
-
-        def round_s(g, tag):
-            s_pairs.append(sb.tile([P, 2 * P, 2], BF16, name="s_pairs%d" % g, tag=tag))
-            rounded = s_pairs[g][:].rearrange("m (u p) b -> m u p b", u=2)
-            sums = turned[g][:].rearrange("m (u b) p -> m u p b", u=2)
-            nc.scalar.activation(out=rounded, in_=sums, func=COPY, scale=ce_col[:, g : g + 1])
-
-        def turn_s_back(g):
-            bank = ps.tile([P, 2, P], F32, name="s_words%d" % g, tag="bank%d" % (4 + g))
-            words = s_pairs[g][:].rearrange("m w b -> m (w b)").bitcast(F32)
-            turn_words([words[:, P * u : P * (u + 1)] for u in range(2)], bank)
-            return bank
-
-        k_il = sb.tile([P, SLOTS, 2, 2], BF16, name="k_il", align_bytes=64)
-        nc.vector.tensor_copy(out=k_il[:, :, 0, :], in_=k_pair.rearrange("p b c -> p c b"))
-        for g in range(2):
-            round_s(g, "s_pairs%d" % g)
-        nc.vector.tensor_copy(out=k_late[:, 0, :], in_=k_raw[2][:].indirect(offsets[:]))
-        banks = [turn_s_back(g) for g in range(2)]
-        weave_words(s_il[0], banks[0])
-        for g in (2, 3):
-            round_s(g, "s_pairs0" if g == 2 else "s_pairs3")
-        banks.extend(turn_s_back(g) for g in (2, 3))
-        s_codes = sb.tile([P, D], U32, name="s_codes", align_bytes=64)
-        s_scales = sb.tile([P, D], U8, name="s_scales", align_bytes=64)
-        quantise(s_codes[:, 0:P], s_scales[:, 0:P], E5M2, s_il[0])
-
-        parts = [slice(P * i, P * (i + 1)) for i in range(4)]
-        for c in parts:
-            nc.vector.tensor_copy(out=k_late[:, 1, c], in_=k_raw[3][:].indirect(offsets[:, c.start // 16 : c.stop // 16]))
-
-        def weave_keys(copy, c):
-            copy(out=k_il[:, c, 1, :], in_=k_late[:, :, c].rearrange("p b c -> p c b"))
-
-        def quantise_keys(c):
-            quantise(k_codes[:, c], k_scales[:, c], E4M3, k_il[:, c].rearrange("p c u b -> p (c u b)"))
-
-        for i in (0, 1):
-            weave_keys(nc.scalar.copy, parts[i])
-        for g in (3, 2, 1):
-            weave_words(s_il[g], banks[g])
-        weave_keys(nc.scalar.copy, parts[3])
-        quantise_keys(halves[0])
-        weave_keys(nc.vector.tensor_copy, parts[2])
-        quantise(s_codes[:, 2 * P : D], s_scales[:, 2 * P : D], E5M2, shared[:, 4 * D : 6 * D])
-        quantise(s_codes[:, P : 2 * P], s_scales[:, P : 2 * P], E5M2, s_il[1])
-        quantise_keys(halves[1])
-
-        out_rows = out_0.rearrange("(p g) c -> p g c", g=LANES)
-        y_pairs = sb.tile([P, 2, T, 2], BF16, name="y_pairs")
-        dv0 = [sb.tile([P, SLOTS], F32, name="dv0_%d" % g) for g in range(LANES)]
-
-        def dv_product(g, first, bank_tag, c):
-            dv_bank = ps.tile([P, SLOTS], F32, name="dv_bank", tag=bank_tag)
-            nc.tensor.matmul_mx(
-                out=dv_bank[:],
-                lhsT=s_codes[:, P * g : P * (g + 1)].bitcast(E5M2),
-                lhsT_scale=s_scales[:, P * g : P * (g + 1)],
-                rhs=codes[:, first : first + SLOTS].bitcast(E4M3),
-                rhs_scale=scales[:, first : first + SLOTS],
-                start=True,
-                stop=True,
-            )
-            shift = D - first
-            nc.scalar.copy(out=dv0[g][:, c], in_=dv_bank[:, c.start + shift : c.stop + shift])
-
-        def scatter(window, g, c):
-            listed = offsets[:, c.start // 16 : c.stop // 16]
-            nc.vector.tensor_tensor(window[:].indirect(listed), dv0[g][:, c], ts_listed[:, c], MULT)
 
         whole = slice(0, SLOTS)
-        dv_product(0, D // 2, "bank4", halves[0])
-        dv_product(0, D, "bank0", halves[1])
-        for g in range(1, LANES):
-            dv_product(g, D, "bank%d" % g, whole)
-        scatter(zeroed[0], 0, halves[0])
-        window = [zeroed[g % WINDOWS] for g in range(LANES)]
-        for g in range(LANES):
-            scatter(window[g], g, halves[1] if g == 0 else whole)
+        ts_listed = sb.tile([P, SLOTS], F32, name="ts_listed", tag="q_il0", align_bytes=64)
+        nc.scalar.activation(out=ts_listed[:], in_=ts_raw[:].indirect(offsets[:]), func=COPY)
+        k_early = sb.tile([P, 2 * SLOTS], BF16, name="k_early", tag="q_il1", align_bytes=64)
+        for t in range(2):
+            nc.scalar.activation(
+                out=k_early[:, SLOTS * t : SLOTS * (t + 1)], in_=k_raw[t][:].indirect(offsets[:]), func=COPY
+            )
+        s_codes = sb.tile([P, D], U32, name="s_codes", align_bytes=64)
+        s_scales = sb.tile([P, D], U8, name="s_scales", align_bytes=64)
+        quantise(s_codes[:], s_scales[:], E5M2, s_il[:].rearrange("p g m j -> p (g m j)"))
+        k_il = sb.tile([P, SLOTS, 2, 2], BF16, name="k_il", align_bytes=64)
+        k_late = sb.tile([P, 2, SLOTS], BF16, name="k_late", tag="s_then_k", align_bytes=64)
+        nc.vector.tensor_copy(out=k_late[:, 0, :], in_=k_raw[2][:].indirect(offsets[:]))
+        nc.vector.tensor_copy(out=k_il[:, :, 0, :], in_=k_early[:].rearrange("p (b c) -> p c b", b=2))
+
+        for i, c in enumerate(quarters):
+            if i % 2 == 0:
+                nc.vector.tensor_copy(out=k_late[:, 1, c], in_=k_raw[3][:].indirect(listed(c)))
+            else:
+                nc.scalar.activation(out=k_late[:, 1, c], in_=k_raw[3][:].indirect(listed(c)), func=COPY)
+        k_codes = sb.tile([P, SLOTS], U32, name="k_codes", align_bytes=64)
+        k_scales = sb.tile([P, SLOTS], U8, name="k_scales", align_bytes=64)
+        for c, copy in zip(halves, (nc.vector.tensor_copy, nc.scalar.copy)):
+            copy(out=k_il[:, c, 1, :], in_=k_late[:, :, c].rearrange("p b c -> p c b"))
+        for c in halves:
+            quantise(k_codes[:, c], k_scales[:, c], E4M3, k_il[:, c].rearrange("p c u b -> p (c u b)"))
+
+        out_rows = out_0.rearrange("(p g) c -> p g c", g=LANES)
+        dv = [sb.tile([P, SLOTS], F32, name="dv%d" % g) for g in range(LANES)]
+        free_banks = ["bank%d" % i for i in range(8)]
+
+        def dv_product(g, c, weigh):
+            bank = ps.tile([P, SLOTS], F32, name="dv_bank", tag=free_banks.pop(0))
+            sums = bank[:, 0 : c.stop - c.start]
+            product(
+                sums,
+                (s_codes[:, quarters[g]], s_scales[:, quarters[g]]),
+                (k_codes[:, c], k_scales[:, c]),
+                (E5M2, E4M3),
+            )
+            if weigh:
+                return lambda: nc.vector.tensor_tensor(dv[g][:, c], sums, ts_listed[:, c], MULT)
+            return lambda: nc.scalar.copy(out=dv[g][:, c], in_=sums)
+
+        y_pairs = sb.tile([P, 2, T, 2], BF16, name="y_pairs")
+
+        def scatter_on_scalar(g, c):
+            nc.scalar.activation(out=window[g][:].indirect(listed(c)), in_=dv[g][:, c], func=COPY)
+
+        def scatter_on_vector(g, c):
+            nc.vector.tensor_tensor(window[g][:].indirect(listed(c)), dv[g][:, c], ts_listed[:, c], MULT)
+
+        def store(g):
             nc.sync.dma_start(out=out_rows[:, g, :], in_=window[g][:])
-            if g < 2:
-                nc.scalar.copy(out=y_pairs[:, 0, :, g], in_=window[g][:])
-            if g == 2:
-                first = SPLIT - 4 * RELAY
-                nc.scalar.copy(out=y_pairs[:, 1, 0:first, 0], in_=window[g][:, 0:first])
-                nc.scalar.copy(
-                    out=y_pairs[:, 1, first : first + 2 * RELAY, :],
-                    in_=window[g][:, first:SPLIT].rearrange("p (b c) -> p c b", b=2),
-                )
-                nc.scalar.copy(out=y_pairs[:, 1, SPLIT:T, 0], in_=window[g][:, SPLIT:T])
+
+        def round_y(copy, g, a, b):
+            copy(out=y_pairs[:, g // 2, a:b, g % 2], in_=window[g][:, a:b])
+
+        first, second = halves
+        dv_product(1, first, True)()
+        dv_product(0, first, False)()
+        scatter_on_scalar(1, first)
+        dv_product(1, second, True)()
+        empty_0 = dv_product(0, second, False)
+        empty_2 = dv_product(2, whole, True)
+        empty_3 = [dv_product(3, first, False), dv_product(3, second, True)]
+        scatter_on_vector(0, first)
+        empty_0()
+        empty_2()
+        scatter_on_scalar(1, second)
+        store(1)
+        scatter_on_vector(0, second)
+        store(0)
+        empty_3[0]()
+        for c in halves:
+            scatter_on_scalar(2, c)
+        store(2)
+        scatter_on_vector(3, first)
+        empty_3[1]()
+        scatter_on_scalar(3, second)
+        store(3)
+        for g in (1, 0):
+            round_y(nc.vector.tensor_copy, g, 0, T)
 
         y_words = y_pairs[:].rearrange("p u c b -> p (u c b)").bitcast(F32).rearrange("p (u c) -> p c u", u=2)
         y_il = sb.tile([P, T * LANES], BF16, name="y_il", align_bytes=64)
@@ -250,25 +249,20 @@ def tile_attend_glin_v_pl_kernel(tc, kT, cd, ce, do, qT, ts, offs, out_0, out_1,
         il_words = y_il[:].bitcast(F32).rearrange("p (c u) -> p c u", u=2)
         words_out = out_1.rearrange("a p c l -> p (a c l)").bitcast(I32)
 
-        for c in (slice(SPLIT, T - 2 * PIECE), slice(T - 2 * PIECE, T)):
-            nc.scalar.copy(out=y_pairs[:, 1, c, 1], in_=window[3][:, c])
+        for g in (2, 3):
+            round_y(nc.scalar.copy, g, SPLIT, T)
+            round_y(nc.vector.tensor_copy, g, 0, SPLIT)
         scalar_cuts = (SPLIT,) + tuple(b for b in PIECES if b > SPLIT)
         for a, b in zip(scalar_cuts, scalar_cuts[1:]):
             nc.scalar.copy(out=il_words[:, a:b, :], in_=y_words[:, a:b, :])
-        for a in (SPLIT - 4 * RELAY, SPLIT - 3 * RELAY):
-            nc.vector.tensor_copy(
-                out=y_pairs[:, 1, a + 2 * RELAY : a + 3 * RELAY, 0], in_=y_pairs[:, 1, a : a + RELAY, 1]
-            )
-        for c in (slice(0, SPLIT - 3 * RELAY), slice(SPLIT - 3 * RELAY, SPLIT)):
-            nc.vector.tensor_copy(out=y_pairs[:, 1, c, 1], in_=window[3][:, c])
 
         def weave_y(a, b):
             nc.vector.tensor_copy(out=il_words[:, a:b, :], in_=y_words[:, a:b, :])
 
         def quantise_y(a, b):
-            quarter, first = divmod(a, T // 4)
+            quarter, start = divmod(a, T // 4)
             quantise(
-                y_codes[:, a:b], y_scales[4 * quarter : P, first : first + b - a], E4M3, y_il[:, a * LANES : b * LANES]
+                y_codes[:, a:b], y_scales[4 * quarter : P, start : start + b - a], E4M3, y_il[:, a * LANES : b * LANES]
             )
             if b in STORES:
                 c = slice(STORES[STORES.index(b) - 1], b)

@@ -19,7 +19,7 @@ LANES = 4
 D = 512
 T = 2048
 SLOTS = 512
-SPLIT = 896
+SPLIT = 1088
 PIECE = 256
 PIECES = (0, 256, 512, 768, 1024, 1280, 1536, 1792, 1920, 2048)
 STORES = (0, 1024, 1792, 2048)
@@ -38,8 +38,8 @@ def tile_attend_glin_v_pl_kernel(tc, kT, cd, ce, do, qT, ts, offs, out_0, out_1,
 
         cd_col = sb.tile([P, LANES], F32, name="cd_col", tag="cd_do_window", align_bytes=64)
         ce_col = sb.tile([P, LANES], F32, name="ce_col")
-        nc.sync.dma_start(out=ce_col[:], in_=ce[0:1, :].rearrange("o (m g) -> m (o g)", g=LANES))
-        nc.sync.dma_start(out=cd_col[:], in_=cd.rearrange("(p j) o -> p (j o)", j=LANES))
+        nc.scalar.dma_start(out=ce_col[:], in_=ce[0:1, :].rearrange("o (m g) -> m (o g)", g=LANES))
+        nc.scalar.dma_start(out=cd_col[:], in_=cd.rearrange("(p j) o -> p (j o)", j=LANES))
         ts_col = sb.tile([P, T // P], F32, name="ts_col")
         nc.scalar.dma_start(out=ts_col[:], in_=ts[0:1, :].rearrange("o (n g) -> n (o g)", n=P))
         q_rows = qT.rearrange("(m j) r -> m j r", j=LANES)
@@ -251,7 +251,9 @@ def tile_attend_glin_v_pl_kernel(tc, kT, cd, ce, do, qT, ts, offs, out_0, out_1,
 
         for g in (2, 3):
             round_y(nc.scalar.copy, g, SPLIT, T)
-            round_y(nc.vector.tensor_copy, g, 0, SPLIT)
+        round_y(nc.vector.tensor_copy, 2, 0, SPLIT)
+        round_y(nc.vector.tensor_copy, 3, 0, PIECE)
+        round_y(nc.vector.tensor_copy, 3, PIECE, SPLIT)
         scalar_cuts = (SPLIT,) + tuple(b for b in PIECES if b > SPLIT)
         for a, b in zip(scalar_cuts, scalar_cuts[1:]):
             nc.scalar.copy(out=il_words[:, a:b, :], in_=y_words[:, a:b, :])

@@ -19,7 +19,7 @@ LANES = 4
 D = 512
 T = 2048
 SLOTS = 512
-SPLIT = 1088
+SPLIT = 1024
 PIECE = 256
 PIECES = (0, 256, 512, 768, 1024, 1280, 1536, 1792, 1920, 2048)
 STORES = (0, 1024, 1792, 2048)
@@ -158,13 +158,13 @@ def tile_attend_glin_v_pl_kernel(tc, kT, cd, ce, do, qT, ts, offs, out_0, out_1,
             )
 
         whole = slice(0, SLOTS)
-        ts_listed = sb.tile([P, SLOTS], F32, name="ts_listed", tag="q_il0", align_bytes=64)
-        nc.scalar.activation(out=ts_listed[:], in_=ts_raw[:].indirect(offsets[:]), func=COPY)
         k_early = sb.tile([P, 2 * SLOTS], BF16, name="k_early", tag="q_il1", align_bytes=64)
         for t in range(2):
             nc.scalar.activation(
                 out=k_early[:, SLOTS * t : SLOTS * (t + 1)], in_=k_raw[t][:].indirect(offsets[:]), func=COPY
             )
+        ts_listed = sb.tile([P, SLOTS], F32, name="ts_listed", tag="q_il0", align_bytes=64)
+        nc.scalar.activation(out=ts_listed[:], in_=ts_raw[:].indirect(offsets[:]), func=COPY)
         s_codes = sb.tile([P, D], U32, name="s_codes", align_bytes=64)
         s_scales = sb.tile([P, D], U8, name="s_scales", align_bytes=64)
         quantise(s_codes[:], s_scales[:], E5M2, s_il[:].rearrange("p g m j -> p (g m j)"))
@@ -180,7 +180,8 @@ def tile_attend_glin_v_pl_kernel(tc, kT, cd, ce, do, qT, ts, offs, out_0, out_1,
                 nc.scalar.activation(out=k_late[:, 1, c], in_=k_raw[3][:].indirect(listed(c)), func=COPY)
         k_codes = sb.tile([P, SLOTS], U32, name="k_codes", align_bytes=64)
         k_scales = sb.tile([P, SLOTS], U8, name="k_scales", align_bytes=64)
-        for c, copy in zip(halves, (nc.vector.tensor_copy, nc.scalar.copy)):
+        for c in quarters:
+            copy = nc.scalar.copy if c == quarters[3] else nc.vector.tensor_copy
             copy(out=k_il[:, c, 1, :], in_=k_late[:, :, c].rearrange("p b c -> p c b"))
         for c in halves:
             quantise(k_codes[:, c], k_scales[:, c], E4M3, k_il[:, c].rearrange("p c u b -> p (c u b)"))
@@ -249,11 +250,12 @@ def tile_attend_glin_v_pl_kernel(tc, kT, cd, ce, do, qT, ts, offs, out_0, out_1,
         il_words = y_il[:].bitcast(F32).rearrange("p (c u) -> p c u", u=2)
         words_out = out_1.rearrange("a p c l -> p (a c l)").bitcast(I32)
 
-        for g in (2, 3):
-            round_y(nc.scalar.copy, g, SPLIT, T)
+        round_y(nc.scalar.copy, 2, SPLIT, T)
+        round_y(nc.scalar.copy, 3, SPLIT, T - 2 * PIECE)
+        round_y(nc.scalar.copy, 3, T - 2 * PIECE, T)
         round_y(nc.vector.tensor_copy, 2, 0, SPLIT)
-        round_y(nc.vector.tensor_copy, 3, 0, PIECE)
-        round_y(nc.vector.tensor_copy, 3, PIECE, SPLIT)
+        round_y(nc.vector.tensor_copy, 3, 0, 2 * PIECE)
+        round_y(nc.vector.tensor_copy, 3, 2 * PIECE, SPLIT)
         scalar_cuts = (SPLIT,) + tuple(b for b in PIECES if b > SPLIT)
         for a, b in zip(scalar_cuts, scalar_cuts[1:]):
             nc.scalar.copy(out=il_words[:, a:b, :], in_=y_words[:, a:b, :])
@@ -270,10 +272,9 @@ def tile_attend_glin_v_pl_kernel(tc, kT, cd, ce, do, qT, ts, offs, out_0, out_1,
                 c = slice(STORES[STORES.index(b) - 1], b)
                 nc.sync.dma_start(out=words_out[:, c], in_=y_codes[:, c].bitcast(I32))
 
-        weave_y(0, PIECE)
+        weave_y(0, 2 * PIECE)
+        weave_y(2 * PIECE, SPLIT)
         for a, b in zip(PIECES, PIECES[1:]):
-            if b < SPLIT:
-                weave_y(b, min(b + PIECE, SPLIT))
             quantise_y(a, b)
         scales_out = out_2.bitcast(I32).rearrange("a (q f) (j c) -> (a q) j f c", f=4, j=4)
         for quad in range(4):

@@ -190,7 +190,7 @@ def tile_attend_glin_v_pl_kernel(tc, kT, cd, ce, do, qT, ts, offs, out_0, out_1,
         dv = [sb.tile([P, SLOTS], F32, name="dv%d" % g) for g in range(LANES)]
         free_banks = ["bank%d" % i for i in range(8)]
 
-        def dv_product(g, c, weigh):
+        def dv_product(g, c):
             bank = ps.tile([P, SLOTS], F32, name="dv_bank", tag=free_banks.pop(0))
             sums = bank[:, 0 : c.stop - c.start]
             product(
@@ -199,9 +199,7 @@ def tile_attend_glin_v_pl_kernel(tc, kT, cd, ce, do, qT, ts, offs, out_0, out_1,
                 (k_codes[:, c], k_scales[:, c]),
                 (E5M2, E4M3),
             )
-            if weigh:
-                return lambda: nc.vector.tensor_tensor(dv[g][:, c], sums, ts_listed[:, c], MULT)
-            return lambda: nc.scalar.copy(out=dv[g][:, c], in_=sums)
+            return lambda: nc.vector.tensor_tensor(dv[g][:, c], sums, ts_listed[:, c], MULT)
 
         y_pairs = sb.tile([P, 2, T, 2], BF16, name="y_pairs")
 
@@ -209,7 +207,7 @@ def tile_attend_glin_v_pl_kernel(tc, kT, cd, ce, do, qT, ts, offs, out_0, out_1,
             nc.scalar.activation(out=window[g][:].indirect(listed(c)), in_=dv[g][:, c], func=COPY)
 
         def scatter_on_vector(g, c):
-            nc.vector.tensor_tensor(window[g][:].indirect(listed(c)), dv[g][:, c], ts_listed[:, c], MULT)
+            nc.vector.tensor_copy(out=window[g][:].indirect(listed(c)), in_=dv[g][:, c])
 
         def store(g):
             nc.sync.dma_start(out=out_rows[:, g, :], in_=window[g][:])
@@ -218,26 +216,21 @@ def tile_attend_glin_v_pl_kernel(tc, kT, cd, ce, do, qT, ts, offs, out_0, out_1,
             copy(out=y_pairs[:, g // 2, a:b, g % 2], in_=window[g][:, a:b])
 
         first, second = halves
-        dv_product(1, first, True)()
-        dv_product(0, first, False)()
-        scatter_on_scalar(1, first)
-        dv_product(1, second, True)()
-        empty_0 = dv_product(0, second, False)
-        empty_2 = dv_product(2, whole, True)
-        empty_3 = [dv_product(3, first, False), dv_product(3, second, True)]
-        scatter_on_vector(0, first)
-        empty_0()
-        empty_2()
-        scatter_on_scalar(1, second)
+        for c in halves:
+            for g in (1, 0):
+                dv_product(g, c)()
+            scatter_on_scalar(1, c)
         store(1)
+        weigh_2, weigh_3 = dv_product(2, whole), dv_product(3, whole)
+        scatter_on_vector(0, first)
+        weigh_2()
         scatter_on_vector(0, second)
         store(0)
-        empty_3[0]()
+        weigh_3()
         for c in halves:
             scatter_on_scalar(2, c)
         store(2)
         scatter_on_vector(3, first)
-        empty_3[1]()
         scatter_on_scalar(3, second)
         store(3)
         for g in (1, 0):

@@ -187,7 +187,7 @@ def tile_attend_glin_v_pl_kernel(tc, kT, cd, ce, do, qT, ts, offs, out_0, out_1,
             quantise(k_codes[:, c], k_scales[:, c], E4M3, k_il[:, c].rearrange("p c u b -> p (c u b)"))
 
         out_rows = out_0.rearrange("(p g) c -> p g c", g=LANES)
-        dv = [sb.tile([P, SLOTS], F32, name="dv%d" % g) for g in range(LANES)]
+        dv = [sb.tile([P, SLOTS], F32, name="dv%d" % g, tag="dv%d" % g) for g in range(LANES)]
         free_banks = ["bank%d" % i for i in range(8)]
 
         def dv_product(g, c):
@@ -199,9 +199,10 @@ def tile_attend_glin_v_pl_kernel(tc, kT, cd, ce, do, qT, ts, offs, out_0, out_1,
                 (k_codes[:, c], k_scales[:, c]),
                 (E5M2, E4M3),
             )
-            return lambda: nc.vector.tensor_tensor(dv[g][:, c], sums, ts_listed[:, c], MULT)
+            return lambda part: nc.vector.tensor_tensor(
+                dv[g][:, part], bank[:, part.start - c.start : part.stop - c.start], ts_listed[:, part], MULT
+            )
 
-        y_pairs = sb.tile([P, 2, T, 2], BF16, name="y_pairs")
 
         def scatter_on_scalar(g, c):
             nc.scalar.activation(out=window[g][:].indirect(listed(c)), in_=dv[g][:, c], func=COPY)
@@ -218,21 +219,23 @@ def tile_attend_glin_v_pl_kernel(tc, kT, cd, ce, do, qT, ts, offs, out_0, out_1,
         first, second = halves
         for c in halves:
             for g in (1, 0):
-                dv_product(g, c)()
+                dv_product(g, c)(c)
             scatter_on_scalar(1, c)
         store(1)
         weigh_2, weigh_3 = dv_product(2, whole), dv_product(3, whole)
         scatter_on_vector(0, first)
-        weigh_2()
+        weigh_2(whole)
+        weigh_3(first)
         scatter_on_vector(0, second)
         store(0)
-        weigh_3()
         for c in halves:
             scatter_on_scalar(2, c)
         store(2)
         scatter_on_vector(3, first)
+        weigh_3(second)
         scatter_on_scalar(3, second)
         store(3)
+        y_pairs = sb.tile([P, 2, T, 2], BF16, name="y_pairs", tag="dv0")
         for g in (1, 0):
             round_y(nc.vector.tensor_copy, g, 0, T)
 

@@ -19,7 +19,7 @@ LANES = 4
 D = 512
 T = 2048
 SLOTS = 512
-SPLIT = 1024
+SPLIT = 1280
 PIECE = 256
 PIECES = (0, 256, 512, 768, 1024, 1280, 1536, 1792, 1920, 2048)
 STORES = (0, 1024, 1792, 2048)
@@ -216,6 +216,12 @@ def tile_attend_glin_v_pl_kernel(tc, kT, cd, ce, do, qT, ts, offs, out_0, out_1,
         def round_y(copy, g, a, b):
             copy(out=y_pairs[:, g // 2, a:b, g % 2], in_=window[g][:, a:b])
 
+        turned_pieces = [slice(a, a + PIECE) for a in range(SPLIT, T, PIECE)]
+
+        def turn_plane(g):
+            for bank, c in zip(sum_banks[g // 2], turned_pieces):
+                turn([window[g][:, a : a + P] for a in range(c.start, c.stop, P)], bank[:, :, g % 2, :])
+
         first, second = halves
         for c in halves:
             for g in (1, 0):
@@ -235,9 +241,15 @@ def tile_attend_glin_v_pl_kernel(tc, kT, cd, ce, do, qT, ts, offs, out_0, out_1,
         weigh_3(second)
         scatter_on_scalar(3, second)
         store(3)
-        y_pairs = sb.tile([P, 2, T, 2], BF16, name="y_pairs", tag="dv0")
-        for g in (1, 0):
-            round_y(nc.vector.tensor_copy, g, 0, T)
+        sum_banks = [
+            [ps.tile([P, 2, 2, P], F32, name="turned%d_%d" % (u, i), tag="bank%d" % tag) for i, tag in enumerate(tags)]
+            for u, tags in enumerate(((0, 1, 2), (3, 4, 6)))
+        ]
+        for g in (1, 0, 2, 3):
+            turn_plane(g)
+        y_pairs = sb.tile([P, 2, SPLIT, 2], BF16, name="y_pairs", tag="dv0")
+        for g in (1, 0, 2):
+            round_y(nc.vector.tensor_copy, g, 0, SPLIT)
 
         y_words = y_pairs[:].rearrange("p u c b -> p (u c b)").bitcast(F32).rearrange("p (u c) -> p c u", u=2)
         y_il = sb.tile([P, T * LANES], BF16, name="y_il", align_bytes=64)
@@ -246,15 +258,38 @@ def tile_attend_glin_v_pl_kernel(tc, kT, cd, ce, do, qT, ts, offs, out_0, out_1,
         il_words = y_il[:].bitcast(F32).rearrange("p (c u) -> p c u", u=2)
         words_out = out_1.rearrange("a p c l -> p (a c l)").bitcast(I32)
 
-        round_y(nc.scalar.copy, 2, SPLIT, T)
-        round_y(nc.scalar.copy, 3, SPLIT, T - 2 * PIECE)
-        round_y(nc.scalar.copy, 3, T - 2 * PIECE, T)
-        round_y(nc.vector.tensor_copy, 2, 0, SPLIT)
         round_y(nc.vector.tensor_copy, 3, 0, 2 * PIECE)
         round_y(nc.vector.tensor_copy, 3, 2 * PIECE, SPLIT)
-        scalar_cuts = (SPLIT,) + tuple(b for b in PIECES if b > SPLIT)
-        for a, b in zip(scalar_cuts, scalar_cuts[1:]):
-            nc.scalar.copy(out=il_words[:, a:b, :], in_=y_words[:, a:b, :])
+
+        first_pairs = sb.tile([P, 2 * PIECE], BF16, name="first_pairs", tag="dv2")
+        later_pairs = sb.tile([P, 5, 2 * PIECE], BF16, name="later_pairs", tag="dv3")
+        word_banks = []
+
+        def round_turned(u, i):
+            pairs = first_pairs[:] if u == i == 0 else later_pairs[:, 3 * u + i - 1, :]
+            nc.scalar.copy(
+                out=pairs.rearrange("c (k p b) -> c k p b", k=2, b=2),
+                in_=sum_banks[u][i][:].rearrange("c k b p -> c k p b"),
+            )
+            if u == 0:
+                word_banks.append(ps.tile([P, 2, 2, P], F32, name="words%d" % i, tag="bank%d" % (7, 5, 0)[i]))
+            words = pairs.bitcast(F32)
+            turn([words[:, 0:P], words[:, P : 2 * P]], word_banks[i][:, u])
+
+        def weave_turned(i, blocks):
+            c = turned_pieces[i]
+            nc.scalar.copy(
+                out=il_words[:, c, :].rearrange("p (k c) u -> p k c u", k=2)[:, blocks],
+                in_=word_banks[i][:].rearrange("p u k c -> p k c u")[:, blocks],
+            )
+
+        for u, i in ((0, 0), (0, 1), (1, 0), (0, 2), (1, 1)):
+            round_turned(u, i)
+        weave_turned(0, slice(0, 2))
+        round_turned(1, 2)
+        weave_turned(1, slice(0, 2))
+        weave_turned(2, slice(0, 1))
+        weave_turned(2, slice(1, 2))
 
         def weave_y(a, b):
             nc.vector.tensor_copy(out=il_words[:, a:b, :], in_=y_words[:, a:b, :])
@@ -269,7 +304,8 @@ def tile_attend_glin_v_pl_kernel(tc, kT, cd, ce, do, qT, ts, offs, out_0, out_1,
                 nc.sync.dma_start(out=words_out[:, c], in_=y_codes[:, c].bitcast(I32))
 
         weave_y(0, 2 * PIECE)
-        weave_y(2 * PIECE, SPLIT)
+        weave_y(2 * PIECE, 4 * PIECE)
+        weave_y(4 * PIECE, SPLIT)
         for a, b in zip(PIECES, PIECES[1:]):
             quantise_y(a, b)
         scales_out = out_2.bitcast(I32).rearrange("a (q f) (j c) -> (a q) j f c", f=4, j=4)

@@ -22,7 +22,7 @@ SLOTS = 512
 SPLIT = 1280
 PIECE = 256
 PIECES = (0, 256, 512, 768, 1024, 1280, 1536, 1792, 1920, 2048)
-STORES = (0, 1024, 1792, 2048)
+STORES = (0, 1024, 1536, 2048)
 
 FLOPS = 2 * 2 * 512 * 512 * 512
 BYTES = 4 * (512 * 2048 + 512 + 512 + 2 * 512 * 512 + 2048) + 2 * 128 * 32 + 4 * 512 * 2048 + 512 * 2048 + 16 * 2048
@@ -310,8 +310,7 @@ def tile_attend_glin_v_pl_kernel(tc, kT, cd, ce, do, qT, ts, offs, out_0, out_1,
             quantise_y(a, b)
         scales_out = out_2.bitcast(I32).rearrange("a (q f) (j c) -> (a q) j f c", f=4, j=4)
         for quad in range(4):
-            queue = nc.sync if quad % 2 == 0 else nc.scalar
-            queue.dma_start(
+            nc.scalar.dma_start(
                 out=scales_out[quad],
                 in_=y_scales[32 * quad : 32 * quad + 16, :].bitcast(I32),
             )

@@ -301,7 +301,8 @@ def tile_attend_glin_v_pl_kernel(tc, kT, cd, ce, do, qT, ts, offs, out_0, out_1,
             )
             if b in STORES:
                 c = slice(STORES[STORES.index(b) - 1], b)
-                nc.sync.dma_start(out=words_out[:, c], in_=y_codes[:, c].bitcast(I32))
+                queue = nc.scalar if b == STORES[2] else nc.sync
+                queue.dma_start(out=words_out[:, c], in_=y_codes[:, c].bitcast(I32))
 
         weave_y(0, 2 * PIECE)
         weave_y(2 * PIECE, 4 * PIECE)

@@ -21,8 +21,6 @@ T = 2048
 SLOTS = 512
 SPLIT = 1280
 PIECE = 256
-PIECES = (0, 256, 512, 768, 1024, 1280, 1536, 1792, 1920, 2048)
-STORES = (0, 1024, 1536, 2048)
 
 FLOPS = 2 * 2 * 512 * 512 * 512
 BYTES = 4 * (512 * 2048 + 512 + 512 + 2 * 512 * 512 + 2048) + 2 * 128 * 32 + 4 * 512 * 2048 + 512 * 2048 + 16 * 2048
@@ -183,7 +181,7 @@ def tile_attend_glin_v_pl_kernel(tc, kT, cd, ce, do, qT, ts, offs, out_0, out_1,
         for c in quarters:
             copy = nc.scalar.copy if c == quarters[3] else nc.vector.tensor_copy
             copy(out=k_il[:, c, 1, :], in_=k_late[:, :, c].rearrange("p b c -> p c b"))
-        for c in halves:
+        for c in (quarters[0], quarters[1], halves[1]):
             quantise(k_codes[:, c], k_scales[:, c], E4M3, k_il[:, c].rearrange("p c u b -> p (c u b)"))
 
         out_rows = out_0.rearrange("(p g) c -> p g c", g=LANES)
@@ -192,13 +190,13 @@ def tile_attend_glin_v_pl_kernel(tc, kT, cd, ce, do, qT, ts, offs, out_0, out_1,
 
         def dv_product(g, c):
             bank = ps.tile([P, SLOTS], F32, name="dv_bank", tag=free_banks.pop(0))
-            sums = bank[:, 0 : c.stop - c.start]
-            product(
-                sums,
-                (s_codes[:, quarters[g]], s_scales[:, quarters[g]]),
-                (k_codes[:, c], k_scales[:, c]),
-                (E5M2, E4M3),
-            )
+            for cut in quarters[0:2] if (g, c) == (1, halves[0]) else [c]:
+                product(
+                    bank[:, cut.start - c.start : cut.stop - c.start],
+                    (s_codes[:, quarters[g]], s_scales[:, quarters[g]]),
+                    (k_codes[:, cut], k_scales[:, cut]),
+                    (E5M2, E4M3),
+                )
             return lambda part: nc.vector.tensor_tensor(
                 dv[g][:, part], bank[:, part.start - c.start : part.stop - c.start], ts_listed[:, part], MULT
             )
@@ -258,8 +256,8 @@ def tile_attend_glin_v_pl_kernel(tc, kT, cd, ce, do, qT, ts, offs, out_0, out_1,
         il_words = y_il[:].bitcast(F32).rearrange("p (c u) -> p c u", u=2)
         words_out = out_1.rearrange("a p c l -> p (a c l)").bitcast(I32)
 
-        round_y(nc.vector.tensor_copy, 3, 0, 2 * PIECE)
-        round_y(nc.vector.tensor_copy, 3, 2 * PIECE, SPLIT)
+        round_y(nc.vector.tensor_copy, 3, PIECE, 3 * PIECE)
+        round_y(nc.vector.tensor_copy, 3, 3 * PIECE, SPLIT)
 
         first_pairs = sb.tile([P, 2 * PIECE], BF16, name="first_pairs", tag="dv2")
         later_pairs = sb.tile([P, 5, 2 * PIECE], BF16, name="later_pairs", tag="dv3")
@@ -299,16 +297,27 @@ def tile_attend_glin_v_pl_kernel(tc, kT, cd, ce, do, qT, ts, offs, out_0, out_1,
             quantise(
                 y_codes[:, a:b], y_scales[4 * quarter : P, start : start + b - a], E4M3, y_il[:, a * LANES : b * LANES]
             )
-            if b in STORES:
-                c = slice(STORES[STORES.index(b) - 1], b)
-                queue = nc.scalar if b == STORES[2] else nc.sync
-                queue.dma_start(out=words_out[:, c], in_=y_codes[:, c].bitcast(I32))
 
-        weave_y(0, 2 * PIECE)
-        weave_y(2 * PIECE, 4 * PIECE)
-        weave_y(4 * PIECE, SPLIT)
-        for a, b in zip(PIECES, PIECES[1:]):
-            quantise_y(a, b)
+        def store_codes(queue, pieces):
+            queue.dma_start(
+                out=words_out.rearrange("p (a c) -> p a c", c=PIECE)[:, pieces],
+                in_=y_codes[:].bitcast(I32).rearrange("p (a c) -> p a c", c=PIECE)[:, pieces],
+            )
+
+        weave_y(PIECE, 3 * PIECE)
+        weave_y(3 * PIECE, SPLIT)
+        for a in range(PIECE, SPLIT, PIECE):
+            quantise_y(a, a + PIECE)
+        store_codes(nc.sync, slice(1, 5))
+        round_y(nc.vector.tensor_copy, 3, 0, PIECE)
+        quantise_y(SPLIT, SPLIT + PIECE)
+        weave_y(0, PIECE)
+        quantise_y(SPLIT + PIECE, T - PIECE)
+        store_codes(nc.scalar, slice(5, 7))
+        quantise_y(T - PIECE, T - P)
+        quantise_y(0, PIECE)
+        quantise_y(T - P, T)
+        store_codes(nc.sync, slice(0, 8, 7))
         scales_out = out_2.bitcast(I32).rearrange("a (q f) (j c) -> (a q) j f c", f=4, j=4)
         for quad in range(4):
             nc.scalar.dma_start(

@@ -19,7 +19,7 @@ LANES = 4
 D = 512
 T = 2048
 SLOTS = 512
-SPLIT = 1280
+OWN = slice(512, 1792)
 PIECE = 256
 
 FLOPS = 2 * 2 * 512 * 512 * 512
@@ -190,13 +190,12 @@ def tile_attend_glin_v_pl_kernel(tc, kT, cd, ce, do, qT, ts, offs, out_0, out_1,
 
         def dv_product(g, c):
             bank = ps.tile([P, SLOTS], F32, name="dv_bank", tag=free_banks.pop(0))
-            for cut in quarters[0:2] if (g, c) == (1, halves[0]) else [c]:
-                product(
-                    bank[:, cut.start - c.start : cut.stop - c.start],
-                    (s_codes[:, quarters[g]], s_scales[:, quarters[g]]),
-                    (k_codes[:, cut], k_scales[:, cut]),
-                    (E5M2, E4M3),
-                )
+            product(
+                bank[:, 0 : c.stop - c.start],
+                (s_codes[:, quarters[g]], s_scales[:, quarters[g]]),
+                (k_codes[:, c], k_scales[:, c]),
+                (E5M2, E4M3),
+            )
             return lambda part: nc.vector.tensor_tensor(
                 dv[g][:, part], bank[:, part.start - c.start : part.stop - c.start], ts_listed[:, part], MULT
             )
@@ -212,19 +211,21 @@ def tile_attend_glin_v_pl_kernel(tc, kT, cd, ce, do, qT, ts, offs, out_0, out_1,
             nc.sync.dma_start(out=out_rows[:, g, :], in_=window[g][:])
 
         def round_y(copy, g, a, b):
-            copy(out=y_pairs[:, g // 2, a:b, g % 2], in_=window[g][:, a:b])
+            copy(out=y_pairs[:, g // 2, a - OWN.start : b - OWN.start, g % 2], in_=window[g][:, a:b])
 
-        turned_pieces = [slice(a, a + PIECE) for a in range(SPLIT, T, PIECE)]
+        turned_pieces = [slice(a, a + PIECE) for a in range(0, T, PIECE) if not OWN.start <= a < OWN.stop]
 
         def turn_plane(g):
             for bank, c in zip(sum_banks[g // 2], turned_pieces):
                 turn([window[g][:, a : a + P] for a in range(c.start, c.stop, P)], bank[:, :, g % 2, :])
 
         first, second = halves
-        for c in halves:
-            for g in (1, 0):
-                dv_product(g, c)(c)
-            scatter_on_scalar(1, c)
+        for g, c in ((1, quarters[0]), (1, quarters[1]), (0, first)):
+            dv_product(g, c)(c)
+        scatter_on_scalar(1, first)
+        for g in (1, 0):
+            dv_product(g, second)(second)
+        scatter_on_scalar(1, second)
         store(1)
         weigh_2, weigh_3 = dv_product(2, whole), dv_product(3, whole)
         scatter_on_vector(0, first)
@@ -241,13 +242,13 @@ def tile_attend_glin_v_pl_kernel(tc, kT, cd, ce, do, qT, ts, offs, out_0, out_1,
         store(3)
         sum_banks = [
             [ps.tile([P, 2, 2, P], F32, name="turned%d_%d" % (u, i), tag="bank%d" % tag) for i, tag in enumerate(tags)]
-            for u, tags in enumerate(((0, 1, 2), (3, 4, 6)))
+            for u, tags in enumerate(((0, 1, 2), (3, 4, 5)))
         ]
         for g in (1, 0, 2, 3):
             turn_plane(g)
-        y_pairs = sb.tile([P, 2, SPLIT, 2], BF16, name="y_pairs", tag="dv0")
+        y_pairs = sb.tile([P, 2, OWN.stop - OWN.start, 2], BF16, name="y_pairs", tag="dv0")
         for g in (1, 0, 2):
-            round_y(nc.vector.tensor_copy, g, 0, SPLIT)
+            round_y(nc.vector.tensor_copy, g, OWN.start, OWN.stop)
 
         y_words = y_pairs[:].rearrange("p u c b -> p (u c b)").bitcast(F32).rearrange("p (u c) -> p c u", u=2)
         y_il = sb.tile([P, T * LANES], BF16, name="y_il", align_bytes=64)
@@ -256,8 +257,8 @@ def tile_attend_glin_v_pl_kernel(tc, kT, cd, ce, do, qT, ts, offs, out_0, out_1,
         il_words = y_il[:].bitcast(F32).rearrange("p (c u) -> p c u", u=2)
         words_out = out_1.rearrange("a p c l -> p (a c l)").bitcast(I32)
 
-        round_y(nc.vector.tensor_copy, 3, PIECE, 3 * PIECE)
-        round_y(nc.vector.tensor_copy, 3, 3 * PIECE, SPLIT)
+        round_y(nc.vector.tensor_copy, 3, 2 * PIECE, 4 * PIECE)
+        round_y(nc.vector.tensor_copy, 3, 4 * PIECE, 6 * PIECE)
 
         first_pairs = sb.tile([P, 2 * PIECE], BF16, name="first_pairs", tag="dv2")
         later_pairs = sb.tile([P, 5, 2 * PIECE], BF16, name="later_pairs", tag="dv3")
@@ -270,7 +271,7 @@ def tile_attend_glin_v_pl_kernel(tc, kT, cd, ce, do, qT, ts, offs, out_0, out_1,
                 in_=sum_banks[u][i][:].rearrange("c k b p -> c k p b"),
             )
             if u == 0:
-                word_banks.append(ps.tile([P, 2, 2, P], F32, name="words%d" % i, tag="bank%d" % (7, 5, 0)[i]))
+                word_banks.append(ps.tile([P, 2, 2, P], F32, name="words%d" % i, tag="bank%d" % (7, 6, 0)[i]))
             words = pairs.bitcast(F32)
             turn([words[:, 0:P], words[:, P : 2 * P]], word_banks[i][:, u])
 
@@ -290,7 +291,7 @@ def tile_attend_glin_v_pl_kernel(tc, kT, cd, ce, do, qT, ts, offs, out_0, out_1,
         weave_turned(2, slice(1, 2))
 
         def weave_y(a, b):
-            nc.vector.tensor_copy(out=il_words[:, a:b, :], in_=y_words[:, a:b, :])
+            nc.vector.tensor_copy(out=il_words[:, a:b, :], in_=y_words[:, a - OWN.start : b - OWN.start, :])
 
         def quantise_y(a, b):
             quarter, start = divmod(a, T // 4)
@@ -298,26 +299,23 @@ def tile_attend_glin_v_pl_kernel(tc, kT, cd, ce, do, qT, ts, offs, out_0, out_1,
                 y_codes[:, a:b], y_scales[4 * quarter : P, start : start + b - a], E4M3, y_il[:, a * LANES : b * LANES]
             )
 
-        def store_codes(queue, pieces):
-            queue.dma_start(
-                out=words_out.rearrange("p (a c) -> p a c", c=PIECE)[:, pieces],
-                in_=y_codes[:].bitcast(I32).rearrange("p (a c) -> p a c", c=PIECE)[:, pieces],
-            )
+        def store_codes(queue, a, b):
+            queue.dma_start(out=words_out[:, a:b], in_=y_codes[:, a:b].bitcast(I32))
 
-        weave_y(PIECE, 3 * PIECE)
-        weave_y(3 * PIECE, SPLIT)
-        for a in range(PIECE, SPLIT, PIECE):
+        weave_y(2 * PIECE, 4 * PIECE)
+        weave_y(4 * PIECE, 6 * PIECE)
+        for a in range(2 * PIECE, 6 * PIECE, PIECE):
             quantise_y(a, a + PIECE)
-        store_codes(nc.sync, slice(1, 5))
-        round_y(nc.vector.tensor_copy, 3, 0, PIECE)
-        quantise_y(SPLIT, SPLIT + PIECE)
-        weave_y(0, PIECE)
-        quantise_y(SPLIT + PIECE, T - PIECE)
-        store_codes(nc.scalar, slice(5, 7))
-        quantise_y(T - PIECE, T - P)
+        store_codes(nc.sync, 2 * PIECE, 6 * PIECE)
+        round_y(nc.vector.tensor_copy, 3, 6 * PIECE, 7 * PIECE)
         quantise_y(0, PIECE)
+        weave_y(6 * PIECE, 7 * PIECE)
+        quantise_y(PIECE, 2 * PIECE)
+        store_codes(nc.scalar, 0, 2 * PIECE)
+        quantise_y(6 * PIECE, 7 * PIECE)
+        quantise_y(T - PIECE, T - P)
         quantise_y(T - P, T)
-        store_codes(nc.sync, slice(0, 8, 7))
+        store_codes(nc.sync, 6 * PIECE, T)
         scales_out = out_2.bitcast(I32).rearrange("a (q f) (j c) -> (a q) j f c", f=4, j=4)
         for quad in range(4):
             nc.scalar.dma_start(

from contextlib import ExitStack

import concourse.mybir as mybir
from concourse.masks import make_identity

F32 = mybir.dt.float32
BF16 = mybir.dt.bfloat16
I32 = mybir.dt.int32
U32 = mybir.dt.uint32
U16 = mybir.dt.uint16
U8 = mybir.dt.uint8
E4M3 = mybir.dt.float8_e4m3fn_x4
E5M2 = mybir.dt.float8_e5m2_x4
MULT = mybir.AluOpType.mult
COPY = mybir.ActivationFunctionType.Copy

P = 128
LANES = 4
D = 512
T = 2048
SLOTS = 512
OWN = slice(512, 1792)
PIECE = 256

FLOPS = 2 * 2 * 512 * 512 * 512
BYTES = 4 * (512 * 2048 + 512 + 512 + 2 * 512 * 512 + 2048) + 2 * 128 * 32 + 4 * 512 * 2048 + 512 * 2048 + 16 * 2048


def tile_attend_glin_v_pl_kernel(tc, kT, cd, ce, do, qT, ts, offs, out_0, out_1, out_2):
    nc = tc.nc
    with ExitStack() as ctx:
        sb = ctx.enter_context(tc.tile_pool(name="sb", bufs=1))
        ps = ctx.enter_context(tc.psum_pool(name="ps", bufs=1))
        halves = [slice(h * D // 2, (h + 1) * D // 2) for h in range(2)]
        quarters = [slice(P * i, P * (i + 1)) for i in range(4)]

        cd_col = sb.tile([P, LANES], F32, name="cd_col", tag="cd_do_window", align_bytes=64)
        ce_col = sb.tile([P, LANES], F32, name="ce_col")
        nc.scalar.dma_start(out=ce_col[:], in_=ce[0:1, :].rearrange("o (m g) -> m (o g)", g=LANES))
        nc.scalar.dma_start(out=cd_col[:], in_=cd.rearrange("(p j) o -> p (j o)", j=LANES))
        ts_col = sb.tile([P, T // P], F32, name="ts_col")
        nc.scalar.dma_start(out=ts_col[:], in_=ts[0:1, :].rearrange("o (n g) -> n (o g)", n=P))
        q_rows = qT.rearrange("(m j) r -> m j r", j=LANES)
        q_raw = [sb.tile([P, 2, D], F32, name="q_raw%d" % h, tag="q_raw%d" % h) for h in range(2)]
        for h in range(2):
            nc.sync.dma_start(out=q_raw[h][:], in_=q_rows[:, 2 * h : 2 * h + 2, :])
        offsets = sb.tile([P, SLOTS // 16], U16, name="offsets")
        nc.sync.dma_start(offsets[:], offs)
        do_raw = sb.tile([P, LANES, D], F32, name="do_raw")
        nc.sync.dma_start(out=do_raw[:], in_=do.rearrange("(p t) e -> p t e", t=LANES))
        k_rows = kT.rearrange("(p t) c -> p t c", t=LANES)
        k_raw = [sb.tile([P, T], F32, name="k_raw%d" % t, tag="k_raw%d" % t) for t in range(LANES)]
        for t in range(LANES):
            nc.sync.dma_start(out=k_raw[t][:], in_=k_rows[:, t, :])

        def listed(c):
            return offsets[:, c.start // 16 : c.stop // 16]

        ident = sb.tile([P, P], F32, name="ident")
        window = [sb.tile([P, T], F32, name="window%d" % g) for g in range(LANES - 1)]
        nc.gpsimd.memset(ident[:], 0.0)
        nc.gpsimd.memset(window[1][:, 0:PIECE].bitcast(I32), 0)
        make_identity(nc, ident[:], nomemset=True)
        nc.gpsimd.memset(window[1][:, PIECE:T].bitcast(I32), 0)
        nc.gpsimd.memset(window[2][:].bitcast(I32), 0)
        for c in (slice(0, T - 1), slice(T - 1, T)):
            nc.vector.memset(window[0][:, c].bitcast(I32), 0)

        def turn(columns, bank):
            for block, source in enumerate(columns):
                nc.tensor.transpose(bank[:, block, :], source, ident[:])

        def spread(column):
            return column.to_broadcast([P, P])

        def quantise(codes, scales, fmt, woven):
            nc.vector.quantize_mx(out=codes.bitcast(fmt), scales=scales, in_=woven)

        def product(bank, stationary, moving, formats):
            nc.tensor.matmul_mx(
                out=bank,
                lhsT=stationary[0].bitcast(formats[0]),
                lhsT_scale=stationary[1],
                rhs=moving[0].bitcast(formats[1]),
                rhs_scale=moving[1],
                start=True,
                stop=True,
            )

        ce_bank = ps.tile([P, LANES, P], F32, name="ce_bank", tag="bank2")
        turn([spread(ce_col[:, g : g + 1]) for g in range(LANES)], ce_bank)
        table = sb.tile([P, LANES, P, LANES], F32, name="table")
        nc.vector.tensor_tensor(
            table[:].rearrange("p g m j -> p (g m) j"),
            ce_bank[:].rearrange("p g m -> p (g m)").unsqueeze(2).to_broadcast([P, D, LANES]),
            cd_col[:].unsqueeze(1).to_broadcast([P, D, LANES]),
            MULT,
        )

        q_codes = sb.tile([P, D], U32, name="q_codes", align_bytes=64)
        q_scales = sb.tile([P, D], U8, name="q_scales", align_bytes=64)
        q_il = [sb.tile([P, 2 * D], BF16, name="q_il%d" % h, tag="q_il%d" % h, align_bytes=64) for h in range(2)]
        for h in range(2):
            q_pairs = sb.tile([P, 2 * D], BF16, name="q_pairs%d" % h, tag="q_pairs%d" % h)
            nc.scalar.copy(
                out=q_pairs[:].rearrange("m (j u p b) -> m j u p b", j=2, u=2, b=2),
                in_=q_raw[h][:].rearrange("m j (p u b) -> m j u p b", u=2, b=2),
            )
            bank = ps.tile([P, 4, P], F32, name="q_bank%d" % h, tag="bank%d" % h)
            words = q_pairs[:].bitcast(F32)
            turn([words[:, c] for c in quarters], bank)
            nc.scalar.copy(
                out=q_il[h][:].bitcast(F32).rearrange("p (j m u) -> p j m u", m=P, u=2),
                in_=bank[:].rearrange("p (j u) m -> p j m u", u=2),
            )
        for h in range(2):
            quantise(q_codes[:, halves[h]], q_scales[:, halves[h]], E4M3, q_il[h][:])

        ts_raw = sb.tile([P, T], F32, name="ts_raw", tag="q_pairs1")
        for i in range(4):
            bank = ps.tile([P, 4, P], F32, name="ts_bank%d" % i, tag="bank%d" % (4 + i))
            turn([spread(ts_col[:, 4 * i + g : 4 * i + g + 1]) for g in range(4)], bank)
            nc.scalar.copy(
                out=ts_raw[:].rearrange("p (n i g) -> p i n g", i=4, g=4)[:, i], in_=bank[:].rearrange("p g n -> p n g")
            )

        do_codes = sb.tile([P, D], U32, name="do_codes", align_bytes=64)
        do_scales = sb.tile([P, D], U8, name="do_scales", align_bytes=64)
        do_il = sb.tile([P, D * LANES], BF16, name="do_il", tag="cd_do_window", align_bytes=64)
        do_halves = [do_il[:, 2 * D * h : 2 * D * (h + 1)] for h in range(2)]
        for h in range(2):
            nc.vector.tensor_copy(
                out=do_halves[h].rearrange("p (c i t) -> p c t i", i=4, t=LANES),
                in_=do_raw[:, :, halves[h]].rearrange("p t (c i) -> p c t i", i=4),
            )
        for h in range(2):
            quantise(do_codes[:, halves[h]], do_scales[:, halves[h]], E5M2, do_halves[h])
        window.append(sb.tile([P, T], F32, name="window3", tag="cd_do_window", align_bytes=64))
        nc.gpsimd.memset(window[3][:].bitcast(I32), 0)

        s_il = sb.tile([P, LANES, P, LANES], BF16, name="s_il", tag="s_then_k", align_bytes=64)
        for b in range(4):
            bank = ps.tile([P, LANES, P], F32, name="s_bank%d" % b, tag="bank%d" % b)
            for j in range(LANES):
                product(
                    bank[:, j, :],
                    (q_codes[:, quarters[j]], q_scales[:, quarters[j]]),
                    (do_codes[:, quarters[b]], do_scales[:, quarters[b]]),
                    (E4M3, E5M2),
                )
            nc.vector.tensor_tensor(
                s_il[:, :, 32 * b : 32 * (b + 1), :],
                bank[:].rearrange("p j (m g) -> p g m j", g=LANES),
                table[:, :, 32 * b : 32 * (b + 1), :],
                MULT,
            )

        whole = slice(0, SLOTS)
        k_early = sb.tile([P, 2 * SLOTS], BF16, name="k_early", tag="q_il1", align_bytes=64)
        for t in range(2):
            nc.scalar.activation(
                out=k_early[:, SLOTS * t : SLOTS * (t + 1)], in_=k_raw[t][:].indirect(offsets[:]), func=COPY
            )
        ts_listed = sb.tile([P, SLOTS], F32, name="ts_listed", tag="q_il0", align_bytes=64)
        nc.scalar.activation(out=ts_listed[:], in_=ts_raw[:].indirect(offsets[:]), func=COPY)
        s_codes = sb.tile([P, D], U32, name="s_codes", align_bytes=64)
        s_scales = sb.tile([P, D], U8, name="s_scales", align_bytes=64)
        quantise(s_codes[:], s_scales[:], E5M2, s_il[:].rearrange("p g m j -> p (g m j)"))
        k_il = sb.tile([P, SLOTS, 2, 2], BF16, name="k_il", align_bytes=64)
        k_late = sb.tile([P, 2, SLOTS], BF16, name="k_late", tag="s_then_k", align_bytes=64)
        nc.vector.tensor_copy(out=k_late[:, 0, :], in_=k_raw[2][:].indirect(offsets[:]))
        nc.vector.tensor_copy(out=k_il[:, :, 0, :], in_=k_early[:].rearrange("p (b c) -> p c b", b=2))

        for i, c in enumerate(quarters):
            if i % 2 == 0:
                nc.vector.tensor_copy(out=k_late[:, 1, c], in_=k_raw[3][:].indirect(listed(c)))
            else:
                nc.scalar.activation(out=k_late[:, 1, c], in_=k_raw[3][:].indirect(listed(c)), func=COPY)
        k_codes = sb.tile([P, SLOTS], U32, name="k_codes", align_bytes=64)
        k_scales = sb.tile([P, SLOTS], U8, name="k_scales", align_bytes=64)
        for c in quarters:
            copy = nc.scalar.copy if c == quarters[3] else nc.vector.tensor_copy
            copy(out=k_il[:, c, 1, :], in_=k_late[:, :, c].rearrange("p b c -> p c b"))
        for c in (quarters[0], quarters[1], halves[1]):
            quantise(k_codes[:, c], k_scales[:, c], E4M3, k_il[:, c].rearrange("p c u b -> p (c u b)"))

        out_rows = out_0.rearrange("(p g) c -> p g c", g=LANES)
        dv = [sb.tile([P, SLOTS], F32, name="dv%d" % g, tag="dv%d" % g) for g in range(LANES)]
        free_banks = ["bank%d" % i for i in range(8)]

        def dv_product(g, c):
            bank = ps.tile([P, SLOTS], F32, name="dv_bank", tag=free_banks.pop(0))
            product(
                bank[:, 0 : c.stop - c.start],
                (s_codes[:, quarters[g]], s_scales[:, quarters[g]]),
                (k_codes[:, c], k_scales[:, c]),
                (E5M2, E4M3),
            )
            return lambda part: nc.vector.tensor_tensor(
                dv[g][:, part], bank[:, part.start - c.start : part.stop - c.start], ts_listed[:, part], MULT
            )


        def scatter_on_scalar(g, c):
            nc.scalar.activation(out=window[g][:].indirect(listed(c)), in_=dv[g][:, c], func=COPY)

        def scatter_on_vector(g, c):
            nc.vector.tensor_copy(out=window[g][:].indirect(listed(c)), in_=dv[g][:, c])

        def store(g):
            nc.sync.dma_start(out=out_rows[:, g, :], in_=window[g][:])

        def round_y(copy, g, a, b):
            copy(out=y_pairs[:, g // 2, a - OWN.start : b - OWN.start, g % 2], in_=window[g][:, a:b])

        turned_pieces = [slice(a, a + PIECE) for a in range(0, T, PIECE) if not OWN.start <= a < OWN.stop]

        def turn_plane(g):
            for bank, c in zip(sum_banks[g // 2], turned_pieces):
                turn([window[g][:, a : a + P] for a in range(c.start, c.stop, P)], bank[:, :, g % 2, :])

        first, second = halves
        for g, c in ((1, quarters[0]), (1, quarters[1]), (0, first)):
            dv_product(g, c)(c)
        scatter_on_scalar(1, first)
        for g in (1, 0):
            dv_product(g, second)(second)
        scatter_on_scalar(1, second)
        store(1)
        weigh_2, weigh_3 = dv_product(2, whole), dv_product(3, whole)
        scatter_on_vector(0, first)
        weigh_2(whole)
        weigh_3(first)
        scatter_on_vector(0, second)
        store(0)
        for c in halves:
            scatter_on_scalar(2, c)
        store(2)
        scatter_on_vector(3, first)
        weigh_3(second)
        scatter_on_scalar(3, second)
        store(3)
        sum_banks = [
            [ps.tile([P, 2, 2, P], F32, name="turned%d_%d" % (u, i), tag="bank%d" % tag) for i, tag in enumerate(tags)]
            for u, tags in enumerate(((0, 1, 2), (3, 4, 5)))
        ]
        for g in (1, 0, 2, 3):
            turn_plane(g)
        y_pairs = sb.tile([P, 2, OWN.stop - OWN.start, 2], BF16, name="y_pairs", tag="dv0")
        for g in (1, 0, 2):
            round_y(nc.vector.tensor_copy, g, OWN.start, OWN.stop)

        y_words = y_pairs[:].rearrange("p u c b -> p (u c b)").bitcast(F32).rearrange("p (u c) -> p c u", u=2)
        y_il = sb.tile([P, T * LANES], BF16, name="y_il", align_bytes=64)
        y_codes = sb.tile([P, T], U32, name="y_codes", align_bytes=64)
        y_scales = sb.tile([P, T // 4], U8, name="y_scales", align_bytes=64)
        il_words = y_il[:].bitcast(F32).rearrange("p (c u) -> p c u", u=2)
        words_out = out_1.rearrange("a p c l -> p (a c l)").bitcast(I32)

        round_y(nc.vector.tensor_copy, 3, 2 * PIECE, 4 * PIECE)
        round_y(nc.vector.tensor_copy, 3, 4 * PIECE, 6 * PIECE)

        first_pairs = sb.tile([P, 2 * PIECE], BF16, name="first_pairs", tag="dv2")
        later_pairs = sb.tile([P, 5, 2 * PIECE], BF16, name="later_pairs", tag="dv3")
        word_banks = []

        def round_turned(u, i):
            pairs = first_pairs[:] if u == i == 0 else later_pairs[:, 3 * u + i - 1, :]
            nc.scalar.copy(
                out=pairs.rearrange("c (k p b) -> c k p b", k=2, b=2),
                in_=sum_banks[u][i][:].rearrange("c k b p -> c k p b"),
            )
            if u == 0:
                word_banks.append(ps.tile([P, 2, 2, P], F32, name="words%d" % i, tag="bank%d" % (7, 6, 0)[i]))
            words = pairs.bitcast(F32)
            turn([words[:, 0:P], words[:, P : 2 * P]], word_banks[i][:, u])

        def weave_turned(i, blocks):
            c = turned_pieces[i]
            nc.scalar.copy(
                out=il_words[:, c, :].rearrange("p (k c) u -> p k c u", k=2)[:, blocks],
                in_=word_banks[i][:].rearrange("p u k c -> p k c u")[:, blocks],
            )

        for u, i in ((0, 0), (0, 1), (1, 0), (0, 2), (1, 1)):
            round_turned(u, i)
        weave_turned(0, slice(0, 2))
        round_turned(1, 2)
        weave_turned(1, slice(0, 2))
        weave_turned(2, slice(0, 1))
        weave_turned(2, slice(1, 2))

        def weave_y(a, b):
            nc.vector.tensor_copy(out=il_words[:, a:b, :], in_=y_words[:, a - OWN.start : b - OWN.start, :])

        def quantise_y(a, b):
            quarter, start = divmod(a, T // 4)
            quantise(
                y_codes[:, a:b], y_scales[4 * quarter : P, start : start + b - a], E4M3, y_il[:, a * LANES : b * LANES]
            )

        def store_codes(queue, a, b):
            queue.dma_start(out=words_out[:, a:b], in_=y_codes[:, a:b].bitcast(I32))

        weave_y(2 * PIECE, 4 * PIECE)
        weave_y(4 * PIECE, 6 * PIECE)
        for a in range(2 * PIECE, 6 * PIECE, PIECE):
            quantise_y(a, a + PIECE)
        store_codes(nc.sync, 2 * PIECE, 6 * PIECE)
        round_y(nc.vector.tensor_copy, 3, 6 * PIECE, 7 * PIECE)
        quantise_y(0, PIECE)
        weave_y(6 * PIECE, 7 * PIECE)
        quantise_y(PIECE, 2 * PIECE)
        store_codes(nc.scalar, 0, 2 * PIECE)
        quantise_y(6 * PIECE, 7 * PIECE)
        quantise_y(T - PIECE, T - P)
        quantise_y(T - P, T)
        store_codes(nc.sync, 6 * PIECE, T)
        scales_out = out_2.bitcast(I32).rearrange("a (q f) (j c) -> (a q) j f c", f=4, j=4)
        for quad in range(4):
            nc.scalar.dma_start(
                out=scales_out[quad],
                in_=y_scales[32 * quad : 32 * quad + 16, :].bitcast(I32),
            )
